import numpy as np
import ml_dtypes


def mxq(x, axis, fmt="e4m3"):
    dtype, down = {"e4m3": (ml_dtypes.float8_e4m3fn, 7), "e5m2": (ml_dtypes.float8_e5m2, 14)}[fmt]
    v = np.moveaxis(np.asarray(x, np.float32).astype(ml_dtypes.bfloat16).astype(np.float64), axis, -1)
    blocks = v.reshape(v.shape[:-1] + (-1, 32))
    amax = np.abs(blocks).max(-1, keepdims=True)
    byte = np.maximum(np.where(amax > 0, np.frexp(amax)[1] - 1 + 127, 0) - down, 1)
    scale = np.exp2(byte - 127.0)
    codes = (blocks / scale).astype(np.float32).astype(dtype).astype(np.float64)
    return np.moveaxis((codes * scale).reshape(v.shape), -1, axis)


WIDE = False


def mx_kscale(k):
    if not WIDE:
        return np.ones(k)
    levels = np.array([10, -10, 5, -5, 0])
    if k % 512:
        return np.exp2(np.random.permutation(np.resize(levels, k // 32))).repeat(32)
    a = np.empty((k // 512, 16))
    for p in range(k // 512):
        a[p, :8] = np.random.permutation(np.resize(levels, 8))
        for g in range(8):
            far = levels[np.abs(levels - a[p, g]) >= 10]
            a[p, g + 8] = far[np.random.randint(len(far))]
    return np.exp2(a.ravel()).repeat(32)


def f64(x):
    return np.asarray(x).astype(np.float64)


def striped(idx):
    return np.tile(idx.reshape(-1, 16).T, (8, 1)).astype(np.uint16)


def unstriped(offs):
    return offs[:16].T.reshape(-1).astype(np.int64)


E2M1 = np.array([0.0, 0.5, 1.0, 1.5, 2.0, 3.0, 4.0, 6.0, -0.0, -0.5, -1.0, -1.5, -2.0, -3.0, -4.0, -6.0])


def pack_weight(w, fmt):
    k, n = w.shape
    w = f64(np.asarray(w, np.float32).astype(ml_dtypes.bfloat16)).reshape(k // 32, 32, n)
    amax = np.abs(w).max(1)
    if fmt == "e4m3":
        byte = np.frexp(amax)[1] - 1 + 127 - 7
    else:
        mant, ex = np.frexp(amax / 6.0)
        byte = np.where(mant > 0.5, ex, ex - 1) + 127
    byte = np.clip(np.where(amax > 0, byte, 1), 1, 254)
    scaled = (w * np.exp2(127.0 - byte)[:, None, :]).reshape(k, n).astype(np.float32)
    by_word = np.ascontiguousarray(scaled.reshape(k // 512, 128, 4, n).transpose(0, 1, 3, 2))
    if fmt == "e4m3":
        words = by_word.astype(ml_dtypes.float8_e4m3fn).view(np.uint8)
    else:
        c = by_word.astype(ml_dtypes.float4_e2m1fn).view(np.uint8) & 0xF
        words = (c[..., 0::2] | (c[..., 1::2] << 4)).reshape(k // 512, 128, 2 * n)
    return np.ascontiguousarray(words), np.ascontiguousarray(byte.astype(np.uint8).reshape(k // 512, 16, n))


def unpack_weight(words, scales, fmt):
    g, _, n = scales.shape
    words = np.ascontiguousarray(words).reshape(g, 128, n, -1)
    if fmt == "e4m3":
        vals = words.view(ml_dtypes.float8_e4m3fn).astype(np.float64)
    else:
        nib = np.empty((g, 128, n, 4), np.uint8)
        nib[..., 0::2] = words & 0xF
        nib[..., 1::2] = words >> 4
        vals = E2M1[nib]
    vals = vals * np.repeat(np.exp2(scales.astype(np.float64) - 127.0), 8, axis=1)[..., None]
    return vals.transpose(0, 1, 3, 2).reshape(g * 512, n)


def gelu(v):
    return 0.5 * v * (1.0 + np.tanh(np.sqrt(2.0 / np.pi) * (v + 0.044715 * v**3)))


K, H, T, S, T2, T3, S2, P = 1024, 512, 2048, 1024, 2048, 2048, 512, 1024

def setup_inputs():
    n = np.random.standard_normal
    s, u = mx_kscale(K)[:, None], mx_kscale(H)[:, None]
    tab_words, tab_scales = pack_weight(n((K, T)) * s, "e4m3")
    tab2_words, tab2_scales = pack_weight(n((H, T3)) / np.sqrt(H) / u, "e4m3")
    w2_words, w2_scales = pack_weight(n((K, H)) / np.sqrt(K) / s, "e2m1")
    w3_words, w3_scales = pack_weight(n((K, H)) / np.sqrt(K) / s, "e4m3")
    return {
        "tab_words": tab_words, "tab_scales": tab_scales,
        "tab2_words": tab2_words, "tab2_scales": tab2_scales,
        "w1": (n((K, H)) / np.sqrt(K) / s * u.T).astype(np.float32),
        "w2_words": w2_words, "w2_scales": w2_scales,
        "w3_words": w3_words, "w3_scales": w3_scales,
        "w4": (n((K, H)) / np.sqrt(K) / s * u.T).astype(np.float32),
        "briefs": (n((K, S)) * s).astype(np.float32),
        "page0": (n((H, T2)) * u).astype(np.float32),
        "wgs": np.exp(0.3 * n((128, S))).astype(np.float32),
        "room": np.exp(0.3 * n(S2)).astype(np.float32),
        "offs": striped(np.random.permutation(T)[:S]),
        "offs2": striped(np.random.permutation(T3)[:S2]),
        "offs3": striped(np.random.permutation(T2)[:S]),
        "offs4": striped(np.random.permutation(T2)[:P]),
    }

def reference(tab_words, tab_scales, tab2_words, tab2_scales, w1, w2_words, w2_scales, w3_words, w3_scales,
              w4, briefs, page0, wgs, room, offs, offs2, offs3, offs4):
    v = unpack_weight(tab_words, tab_scales, "e4m3")[:, unstriped(offs)]
    f1 = mxq(f64(w1), 0, "e4m3").T @ v
    f2 = unpack_weight(w2_words, w2_scales, "e2m1").T @ v
    f3 = unpack_weight(w3_words, w3_scales, "e4m3").T @ v
    d = mxq(f64(w4), 0, "e4m3").T @ mxq(f64(briefs), 0, "e4m3")
    h = f1 * f2 * f3 + d
    page = f64(page0).copy()
    page[:, unstriped(offs3)] = np.tile(f64(wgs), (H // 128, 1)) * h
    v2 = unpack_weight(tab2_words, tab2_scales, "e4m3")[:, unstriped(offs2)]
    e = v2.T @ mxq(page, 0, "e4m3")
    x = e[:, unstriped(offs4)]
    return x / (f64(room)[:, None] + np.abs(x))

@@ -1,0 +1,326 @@
+from contextlib import ExitStack
+
+import concourse.mybir as mybir
+from concourse.masks import make_identity
+
+K, H, T, S, T2, T3, S2, PICK = 1024, 512, 2048, 1024, 2048, 2048, 512, 1024
+FLOPS = 4 * 2 * K * H * S + 2 * H * S2 * T2
+
+F32 = mybir.dt.float32
+BF16 = mybir.dt.bfloat16
+I32 = mybir.dt.int32
+U32 = mybir.dt.uint32
+U16 = mybir.dt.uint16
+U8 = mybir.dt.uint8
+FP8X4 = mybir.dt.float8_e4m3fn_x4
+FP4X4 = mybir.dt.float4_e2m1fn_x4
+MULT = mybir.AluOpType.mult
+ACT = mybir.ActivationFunctionType
+
+P = 128
+PACK = 4
+K_PASS = P * PACK
+PASSES = K // K_PASS
+QUADS = 4
+BANK = 512
+PER_COL = 16
+HALVES = S // BANK
+CHUNKS = T2 // BANK
+GROUPS = S2 // P
+VECTOR_EVAC = ((0, 3), (3, 0), (3, 1), (3, 2), (3, 3))
+
+
+def tile_list_translator_brief_scores_kernel(
+    tc, tab_words, tab_scales, tab2_words, tab2_scales, w1, w2_words, w2_scales, w3_words, w3_scales,
+    w4, briefs, page0, wgs, room, offs, offs2, offs3, offs4, out,
+):
+    nc = tc.nc
+    with ExitStack() as ctx:
+        keep = ctx.enter_context(tc.tile_pool(name="keep", bufs=1))
+        ring = ctx.enter_context(tc.tile_pool(name="ring", bufs=1))
+        psum = ctx.enter_context(tc.psum_pool(name="psum", bufs=1))
+
+        def big(shape, name):
+            return ring.tile(shape, F32, name=name, tag="big", bufs=6, align_bytes=64)
+
+        def mid(shape, dtype, name):
+            return ring.tile(shape, dtype, name=name, tag="mid", bufs=4, align_bytes=64)
+
+        def wide_codes(name):
+            codes = ring.tile([P, BANK], U32, name=name + "_codes", tag="wide_codes", bufs=4, align_bytes=64)
+            scales = ring.tile([P, BANK], U8, name=name + "_scales", tag="wide_scales", bufs=4, align_bytes=64)
+            return codes, scales
+
+        def load_list(src, name):
+            lst = keep.tile(list(src.shape), U16, name=name)
+            nc.sync.dma_start(lst[:], src)
+            return lst
+
+        def load_scale_rows(queue, plane, src):
+            for q in range(QUADS):
+                queue.dma_start(
+                    plane[32 * q : 32 * q + 4].bitcast(I32),
+                    src[:, 4 * q : 4 * q + 4, :].rearrange("a r c -> r a c").bitcast(I32),
+                )
+
+        def load_rows(raw, src):
+            nc.sync.dma_start(raw[:], src.rearrange("(p i) c -> p i c", i=PACK))
+
+        def round_and_interleave(copy, raw, width):
+            grouped = ring.tile([P, width, PACK], BF16, name="grouped", tag="grouped", bufs=3, align_bytes=64)
+            copy(
+                grouped[:].rearrange("p (c n) i -> p c i n", n=4),
+                raw[:].rearrange("p i (c n) -> p c i n", n=4),
+            )
+            return grouped
+
+        def quantize(grouped, codes, scales):
+            nc.vector.quantize_mx(
+                out=codes.bitcast(FP8X4), scales=scales, in_=grouped[:].rearrange("p c i -> p (c i)")
+            )
+
+        tab_plane = keep.tile([P, PASSES, T], U8, align_bytes=64)
+        nc.vector.memset(tab_plane[:].bitcast(I32), 0)
+        w2_plane = keep.tile([P, PASSES, H], U8, align_bytes=64)
+        w3_plane = keep.tile([P, PASSES, H], U8, align_bytes=64)
+        tab2_plane = keep.tile([P, 1, T3], U8, align_bytes=64)
+        nc.gpsimd.memset(w3_plane[:].bitcast(I32), 0)
+        nc.vector.memset(w2_plane[:].bitcast(I32), 0)
+        nc.vector.memset(tab2_plane[:].bitcast(I32), 0)
+        ones = keep.tile([P, 1], F32)
+        nc.vector.memset(ones[:], 1.0)
+        warm = keep.tile([P, 1], F32)
+
+        idx = load_list(offs, "idx")
+        load_scale_rows(nc.gpsimd, tab_plane, tab_scales)
+        nc.scalar.activation(warm[:], ones[:], ACT.Abs_reciprocal_sqrt)
+        load_scale_rows(nc.gpsimd, w3_plane, w3_scales)
+        load_scale_rows(nc.gpsimd, w2_plane, w2_scales)
+        ident = keep.tile([P, P], F32)
+        make_identity(nc, ident[:])
+
+        def load_words(words, src):
+            nc.sync.dma_start(words[:].bitcast(I32), src.rearrange("p t i -> p (t i)").bitcast(I32))
+
+        w1_raw, w4_raw, tab = [], [], []
+        for a in range(PASSES):
+            tab.append(keep.tile([P, T], U32, name=f"tab{a}", tag=f"tab{a}", align_bytes=64))
+            load_words(tab[a], tab_words[a])
+        w3_codes = keep.tile([P, PASSES, H], U32, align_bytes=64)
+        nc.sync.dma_start(w3_codes[:].bitcast(I32), w3_words.rearrange("a p c i -> p a (c i)").bitcast(I32))
+        w2_codes = keep.tile([P, PASSES, 2 * H], U8, align_bytes=64)
+        nc.sync.dma_start(w2_codes[:].bitcast(I32), w2_words.rearrange("a p c -> p a c").bitcast(I32))
+        for w_raw, w, name in ((w1_raw, w1, "w1"), (w4_raw, w4, "w4")):
+            for a in range(PASSES):
+                w_raw.append(big([P, PACK, H], f"{name}_raw{a}"))
+                load_rows(w_raw[a], w[a * K_PASS : (a + 1) * K_PASS, :])
+
+        weight, page = [], []
+
+        def load_board(i):
+            weight.append(keep.tile([P, S], F32, name=f"weight{i}"))
+            for q in (0, 2, 1, 3):
+                nc.sync.dma_start(weight[i][32 * q : 32 * q + 32], wgs.rearrange("(q i) j -> q i j", i=PACK)[:, i, :])
+            page.append(keep.tile([P, T2], F32, name=f"page{i}"))
+            nc.sync.dma_start(page[i][:], page0.rearrange("(p i) t -> p i t", i=PACK)[:, i, :])
+
+        briefs_raw = {}
+
+        def load_briefs(s):
+            for a in range(PASSES):
+                briefs_raw[s, a] = big([P, PACK, BANK], f"briefs_raw{s}{a}")
+                load_rows(briefs_raw[s, a], briefs[a * K_PASS : (a + 1) * K_PASS, s * BANK : (s + 1) * BANK])
+
+        load_briefs(0)
+        idx3 = load_list(offs3, "idx3")
+        load_board(0)
+        load_briefs(1)
+        load_board(1)
+        load_board(2)
+        idx2 = load_list(offs2, "idx2")
+        tab2 = keep.tile([P, T3], U32, align_bytes=64)
+        load_words(tab2, tab2_words[0])
+        load_board(PACK - 1)
+        load_scale_rows(nc.sync, tab2_plane, tab2_scales)
+        idx4 = load_list(offs4, "idx4")
+        room_col = keep.tile([P, GROUPS], F32)
+        with nc.allow_non_contiguous_dma(reason="one value of room for each partition and group"):
+            nc.sync.dma_start(room_col[:], room.rearrange("(g p) -> p g", p=P))
+
+        v_scales = [keep.tile([P, S], U8, name=f"v_scales{a}", align_bytes=64) for a in range(PASSES)]
+        v_codes = [keep.tile([P, S], U32, name=f"v_codes{a}", align_bytes=64) for a in range(PASSES)]
+        for a in range(PASSES):
+            nc.vector.tensor_copy(v_codes[a][:], tab[a][:].indirect(idx[:]))
+        for s in range(HALVES):
+            for a in range(PASSES):
+                nc.vector.tensor_copy(
+                    v_scales[a][:, s * BANK : (s + 1) * BANK],
+                    tab_plane[:, a, :].indirect(idx[:, s * BANK // PER_COL : (s + 1) * BANK // PER_COL]),
+                )
+
+        def mx_sum(bank, lhs, rhs):
+            for a in range(PASSES):
+                nc.tensor.matmul_mx(
+                    out=bank[:], lhsT=lhs[a][0], lhsT_scale=lhs[a][1], rhs=rhs[a][0], rhs_scale=rhs[a][1],
+                    start=(a == 0), stop=(a == PASSES - 1),
+                )
+
+        def by_slot(bank):
+            return bank[:].rearrange("j (m i) -> j i m", i=PACK)
+
+        w2_ops = [(w2_codes[:, a, :].bitcast(FP4X4), w2_plane[:, a, :]) for a in range(PASSES)]
+        w3_ops = [(w3_codes[:, a, :].bitcast(FP8X4), w3_plane[:, a, :]) for a in range(PASSES)]
+        prod = {}
+
+        def table_sum(b, w_ops):
+            cols = slice(b * P, (b + 1) * P)
+            v_ops = [(v_codes[a][:, cols].bitcast(FP8X4), v_scales[a][:, cols]) for a in range(PASSES)]
+            bank = psum.tile([P, H], F32, name="f_bank", tag="f", bufs=5)
+            mx_sum(bank, v_ops, w_ops)
+            return by_slot(bank)
+
+        def f2_times_f3(b):
+            f3 = ring.tile([P, PACK, P], F32, name="f3", bufs=2)
+            nc.scalar.copy(f3[:], table_sum(b, w3_ops))
+            if b % 2 == 0:
+                prod[b // 2] = ring.tile([P, 2, PACK, P], F32, name="prod", tag="prod", bufs=4)
+            nc.vector.tensor_tensor(prod[b // 2][:, b % 2], table_sum(b, w2_ops), f3[:], MULT)
+
+        def times_f1(b):
+            part = prod[b // 2][:, b % 2]
+            nc.vector.tensor_tensor(part, table_sum(b, w1_ops), part, MULT)
+
+        def quantize_weight(raw, name, copy):
+            codes, scales = wide_codes(name)
+            quantize(round_and_interleave(copy, raw, H), codes[:], scales[:])
+            return codes[:].bitcast(FP8X4), scales[:]
+
+        briefs_q = {}
+
+        def quantize_briefs(s, a, copy):
+            grouped = round_and_interleave(copy, briefs_raw[s, a], BANK)
+            codes = keep.tile([P, BANK], U32, name=f"briefs_codes{s}{a}", align_bytes=64)
+            scales = keep.tile([P, BANK], U8, name=f"briefs_scales{s}{a}", align_bytes=64)
+            quantize(grouped, codes[:], scales[:])
+            briefs_q[s, a] = codes, scales
+
+        h = {}
+
+        def features(s):
+            h[s] = big([P, PACK, BANK], f"h{s}")
+            for n in range(BANK // P):
+                b = s * BANK // P + n
+                cols = slice(n * P, (n + 1) * P)
+                b_ops = [(briefs_q[s, a][0][:, cols].bitcast(FP8X4), briefs_q[s, a][1][:, cols]) for a in range(PASSES)]
+                d_bank = psum.tile([P, H], F32, name="d_bank", tag="g", bufs=3)
+                mx_sum(d_bank, b_ops, w4_ops)
+                d = ring.tile([P, PACK, P], F32, name="d", bufs=2)
+                nc.scalar.copy(d[:], by_slot(d_bank))
+                h_bank = psum.tile([P, PACK, P], F32, name="h_bank", tag="g", bufs=3)
+                for i in range(PACK):
+                    nc.tensor.matmul(h_bank[:, i, :], prod[b // 2][:, b % 2, i, :], ident[:],
+                                     start=True, stop=False, is_transpose=True)
+                    nc.tensor.matmul(h_bank[:, i, :], d[:, i, :], ident[:],
+                                     start=False, stop=True, is_transpose=True)
+                nc.scalar.copy(h[s][:, :, cols], h_bank[:])
+
+        def amend(i, lo, hi):
+            s, off = divmod(lo, BANK)
+            nc.vector.tensor_tensor(
+                page[i][:].indirect(idx3[:, lo // PER_COL : hi // PER_COL]),
+                h[s][:, i, off : off + hi - lo], weight[i][:, lo:hi], MULT,
+            )
+
+        w1_ops, w4_ops = [], []
+        for a in range(PASSES):
+            for b in range(2 * a, 2 * a + 2):
+                f2_times_f3(b)
+            w1_ops.append(quantize_weight(w1_raw[a], f"w1_{a}", nc.scalar.copy))
+        for a, copy in enumerate((nc.scalar.copy, nc.vector.tensor_copy)):
+            for b in range(4 + 2 * a, 6 + 2 * a):
+                f2_times_f3(b)
+            w4_ops.append(quantize_weight(w4_raw[a], f"w4_{a}", copy))
+        for b in range(4):
+            times_f1(b)
+        quantize_briefs(0, 0, nc.scalar.copy)
+        quantize_briefs(0, 1, nc.vector.tensor_copy)
+        for b in range(4, 8):
+            times_f1(b)
+        features(0)
+        quantize_briefs(1, 0, nc.scalar.copy)
+        quantize_briefs(1, 1, nc.scalar.copy)
+        features(1)
+        amend(0, 0, BANK // 2)
+        amend(0, BANK // 2, BANK)
+        amend(1, 0, BANK)
+
+        v2_codes = keep.tile([P, S2], U32, align_bytes=64)
+        v2_scales = keep.tile([P, S2], U8, align_bytes=64)
+        pairs = [mid([P, 2, BANK, 2], BF16, f"pairs{c}") for c in range(CHUNKS)]
+        for i in range(PACK):
+            if i == PACK - 1:
+                nc.vector.tensor_copy(v2_codes[:], tab2[:].indirect(idx2[:]))
+            if i >= 2:
+                amend(i, 0, BANK)
+            amend(i, BANK, S)
+            for c in range(CHUNKS):
+                nc.scalar.copy(pairs[c][:, i // 2, :, i % 2], page[i][:, c * BANK : (c + 1) * BANK])
+        nc.vector.tensor_copy(v2_scales[:], tab2_plane[:, 0, :].indirect(idx2[:]))
+
+        page_q = []
+        for c in range(CHUNKS):
+            grouped = ring.tile([P, BANK, PACK], BF16, name="grouped", tag="grouped", bufs=3, align_bytes=64)
+            nc.vector.tensor_copy(
+                grouped[:].rearrange("p c i -> p (c i)").bitcast(F32).rearrange("p (c n u) -> p c u n", n=4, u=2),
+                pairs[c][:].rearrange("p u c e -> p u (c e)").bitcast(F32).rearrange("p u (c n) -> p c u n", n=4),
+            )
+            page_q.append(wide_codes(f"page_{c}"))
+            quantize(grouped, page_q[c][0][:], page_q[c][1][:])
+
+        e = {}
+
+        def scores(g):
+            rows = slice(g * P, (g + 1) * P)
+            if g % 2 == 0:
+                e[g] = big([P, T2], f"e{g}")
+            else:
+                e[g] = keep.tile([P, T2], F32, name=f"e{g}", tag="tab0", align_bytes=64)
+            for c in range(CHUNKS):
+                if c % 2 == 0:
+                    e_bank = psum.tile([P, BANK], F32, name="e_bank", tag="f", bufs=5)
+                else:
+                    e_bank = psum.tile([P, BANK], F32, name="e_bank", tag="g", bufs=3)
+                nc.tensor.matmul_mx(
+                    out=e_bank[:], lhsT=v2_codes[:, rows].bitcast(FP8X4), lhsT_scale=v2_scales[:, rows],
+                    rhs=page_q[c][0][:].bitcast(FP8X4), rhs_scale=page_q[c][1][:], start=True, stop=True,
+                )
+                copy = nc.vector.tensor_copy if (g, c) in VECTOR_EVAC else nc.scalar.copy
+                copy(e[g][:, c * BANK : (c + 1) * BANK], e_bank[:])
+
+        def pick(g, lo, width):
+            x = ring.tile([P, width], F32, name="x", bufs=3)
+            nc.vector.tensor_copy(x[:], e[g][:].indirect(idx4[:, lo // PER_COL : (lo + width) // PER_COL]))
+            return x
+
+        def softsign(x, g, lo, width):
+            inv = ring.tile([P, width], F32, name="inv", tag="prod", bufs=4)
+            nc.scalar.activation(inv[:], x[:], ACT.Abs)
+            nc.scalar.activation(inv[:], inv[:], ACT.Abs_reciprocal_sqrt, bias=room_col[:, g : g + 1])
+            nc.scalar.activation(inv[:], inv[:], ACT.Square)
+            result = mid([P, width], F32, "result")
+            nc.vector.tensor_tensor(result[:], x[:], inv[:], MULT)
+            nc.sync.dma_start(out[g * P : (g + 1) * P, lo : lo + width], result[:])
+
+        scores(0)
+        x0 = pick(0, 0, PICK)
+        scores(1)
+        scores(2)
+        x1 = pick(1, 0, PICK)
+        softsign(x0, 0, 0, PICK)
+        scores(3)
+        x2 = pick(2, 0, PICK)
+        softsign(x1, 1, 0, PICK)
+        last = [pick(3, lo, BANK) for lo in range(0, PICK, BANK)]
+        softsign(x2, 2, 0, PICK)
+        for n, x in enumerate(last):
+            softsign(x, 3, n * BANK, BANK)

@@ -23,6 +23,7 @@ K_PASS = P * PACK
 PASSES = K // K_PASS
 QUADS = 4
 BANK = 512
+BANKS = 8
 PER_COL = 16
 HALVES = S // BANK
 CHUNKS = T2 // BANK
@@ -40,11 +41,26 @@ def tile_list_translator_brief_scores_kernel(
         ring = ctx.enter_context(tc.tile_pool(name="ring", bufs=1))
         psum = ctx.enter_context(tc.psum_pool(name="psum", bufs=1))
 
-        def big(shape, name):
-            return ring.tile(shape, F32, name=name, tag="big", bufs=6, align_bytes=64)
+        def big(shape, name, slot):
+            return ring.tile(shape, F32, name=name, tag=f"big{slot}", align_bytes=64)
 
-        def mid(shape, dtype, name):
-            return ring.tile(shape, dtype, name=name, tag="mid", bufs=4, align_bytes=64)
+        def mid(shape, dtype, name, slot):
+            return ring.tile(shape, dtype, name=name, tag=f"mid{slot}", align_bytes=64)
+
+        def late(shape, dtype, name, slot):
+            return ring.tile(shape, dtype, name=name, tag=f"late{slot}", align_bytes=64)
+
+        def small(shape, dtype, name, slot):
+            return ring.tile(shape, dtype, name=name, tag=f"small{slot}", align_bytes=64)
+
+        banks_taken = []
+
+        def numbered_bank(shape, number):
+            return psum.tile(shape, F32, name=f"bank{number}", tag=f"bank{number}")
+
+        def fresh_bank(shape):
+            banks_taken.append(shape)
+            return numbered_bank(shape, (len(banks_taken) - 1) % BANKS)
 
         def wide_codes(name):
             codes = ring.tile([P, BANK], U32, name=name + "_codes", tag="wide_codes", bufs=4, align_bytes=64)
@@ -66,13 +82,14 @@ def tile_list_translator_brief_scores_kernel(
         def load_rows(raw, src):
             nc.sync.dma_start(raw[:], src.rearrange("(p i) c -> p i c", i=PACK))
 
-        def round_and_interleave(copy, raw, width):
-            grouped = ring.tile([P, width, PACK], BF16, name="grouped", tag="grouped", bufs=3, align_bytes=64)
+        def staging():
+            return ring.tile([P, BANK, PACK], BF16, name="grouped", tag="grouped", bufs=3, align_bytes=64)
+
+        def round_and_interleave(copy, raw, grouped):
             copy(
-                grouped[:].rearrange("p (c n) i -> p c i n", n=4),
+                grouped.rearrange("p (c n) i -> p c i n", n=4),
                 raw[:].rearrange("p i (c n) -> p c i n", n=4),
             )
-            return grouped
 
         def quantize(grouped, codes, scales):
             nc.vector.quantize_mx(
@@ -84,7 +101,7 @@ def tile_list_translator_brief_scores_kernel(
         w2_plane = keep.tile([P, PASSES, H], U8, align_bytes=64)
         w3_plane = keep.tile([P, PASSES, H], U8, align_bytes=64)
         tab2_plane = keep.tile([P, 1, T3], U8, align_bytes=64)
-        nc.gpsimd.memset(w3_plane[:].bitcast(I32), 0)
+        nc.vector.memset(w3_plane[:].bitcast(I32), 0)
         nc.vector.memset(w2_plane[:].bitcast(I32), 0)
         nc.vector.memset(tab2_plane[:].bitcast(I32), 0)
         ones = keep.tile([P, 1], F32)
@@ -92,35 +109,35 @@ def tile_list_translator_brief_scores_kernel(
         warm = keep.tile([P, 1], F32)
 
         idx = load_list(offs, "idx")
-        load_scale_rows(nc.gpsimd, tab_plane, tab_scales)
         nc.scalar.activation(warm[:], ones[:], ACT.Abs_reciprocal_sqrt)
-        load_scale_rows(nc.gpsimd, w3_plane, w3_scales)
-        load_scale_rows(nc.gpsimd, w2_plane, w2_scales)
         ident = keep.tile([P, P], F32)
         make_identity(nc, ident[:])
 
         def load_words(words, src):
-            nc.sync.dma_start(words[:].bitcast(I32), src.rearrange("p t i -> p (t i)").bitcast(I32))
+            nc.sync.dma_start(words.bitcast(I32), src.rearrange("p t i -> p (t i)").bitcast(I32))
 
-        w1_raw, w4_raw, tab = [], [], []
-        for a in range(PASSES):
-            tab.append(keep.tile([P, T], U32, name=f"tab{a}", tag=f"tab{a}", align_bytes=64))
-            load_words(tab[a], tab_words[a])
+        tab = [keep.tile([P, T], U32, name=f"tab{a}", tag=f"tab{a}", align_bytes=64) for a in range(PASSES)]
+        load_words(tab[0][:], tab_words[0])
+        load_scale_rows(nc.scalar, tab_plane, tab_scales)
         w3_codes = keep.tile([P, PASSES, H], U32, align_bytes=64)
         nc.sync.dma_start(w3_codes[:].bitcast(I32), w3_words.rearrange("a p c i -> p a (c i)").bitcast(I32))
+        load_scale_rows(nc.scalar, w3_plane, w3_scales)
         w2_codes = keep.tile([P, PASSES, 2 * H], U8, align_bytes=64)
         nc.sync.dma_start(w2_codes[:].bitcast(I32), w2_words.rearrange("a p c -> p a c").bitcast(I32))
-        for w_raw, w, name in ((w1_raw, w1, "w1"), (w4_raw, w4, "w4")):
-            for a in range(PASSES):
-                w_raw.append(big([P, PACK, H], f"{name}_raw{a}"))
-                load_rows(w_raw[a], w[a * K_PASS : (a + 1) * K_PASS, :])
+        load_scale_rows(nc.scalar, w2_plane, w2_scales)
+        load_words(tab[1][:], tab_words[1])
 
-        weight, page = [], []
+        def load_weight_pass(w, a, name, slot):
+            raw = big([P, PACK, H], f"{name}_raw{a}", slot)
+            load_rows(raw, w[a * K_PASS : (a + 1) * K_PASS, :])
+            return raw
 
-        def load_board(i):
-            weight.append(keep.tile([P, S], F32, name=f"weight{i}"))
-            for q in (0, 2, 1, 3):
-                nc.sync.dma_start(weight[i][32 * q : 32 * q + 32], wgs.rearrange("(q i) j -> q i j", i=PACK)[:, i, :])
+        w1_raw = [load_weight_pass(w1, a, "w1", a) for a in range(PASSES)]
+        w4_raw = [load_weight_pass(w4, a, "w4", 2 + a) for a in range(PASSES)]
+
+        page = []
+
+        def load_page(i):
             page.append(keep.tile([P, T2], F32, name=f"page{i}"))
             nc.sync.dma_start(page[i][:], page0.rearrange("(p i) t -> p i t", i=PACK)[:, i, :])
 
@@ -128,35 +145,61 @@ def tile_list_translator_brief_scores_kernel(
 
         def load_briefs(s):
             for a in range(PASSES):
-                briefs_raw[s, a] = big([P, PACK, BANK], f"briefs_raw{s}{a}")
-                load_rows(briefs_raw[s, a], briefs[a * K_PASS : (a + 1) * K_PASS, s * BANK : (s + 1) * BANK])
+                rows = briefs[a * K_PASS : (a + 1) * K_PASS, s * BANK : (s + 1) * BANK]
+                if s == 0:
+                    briefs_raw[s, a] = [big([P, PACK, BANK], f"briefs_raw{s}{a}", 4 + a)]
+                else:
+                    briefs_raw[s, a] = [mid([P, PACK, BANK // 2], F32, f"briefs_raw{s}{a}{n}", 2 * a + n) for n in range(2)]
+                width = BANK // len(briefs_raw[s, a])
+                for n, raw in enumerate(briefs_raw[s, a]):
+                    load_rows(raw, rows[:, n * width : (n + 1) * width])
 
         load_briefs(0)
         idx3 = load_list(offs3, "idx3")
-        load_board(0)
+        weight = {}
+
+        def load_weight(lo, hi):
+            weight[lo] = keep.tile([P, PACK, hi - lo], F32, name=f"weight{lo}")
+            rows = wgs.rearrange("(q i) j -> q i j", i=PACK)[:, :, lo:hi]
+            for q in (0, 2, 1, 3):
+                nc.sync.dma_start(weight[lo][32 * q : 32 * q + 32], rows)
+
+        load_weight(0, BANK // 2)
+        load_page(0)
+        load_page(1)
+        load_weight(BANK // 2, BANK)
         load_briefs(1)
-        load_board(1)
-        load_board(2)
+        for i in range(2, PACK):
+            load_page(i)
         idx2 = load_list(offs2, "idx2")
-        tab2 = keep.tile([P, T3], U32, align_bytes=64)
-        load_words(tab2, tab2_words[0])
-        load_board(PACK - 1)
+        tab2 = keep.tile([P, T3], U32, name="tab2", align_bytes=64)
+        load_words(tab2[:], tab2_words[0])
+        load_weight(BANK, S)
         load_scale_rows(nc.sync, tab2_plane, tab2_scales)
         idx4 = load_list(offs4, "idx4")
         room_col = keep.tile([P, GROUPS], F32)
         with nc.allow_non_contiguous_dma(reason="one value of room for each partition and group"):
             nc.sync.dma_start(room_col[:], room.rearrange("(g p) -> p g", p=P))
 
-        v_scales = [keep.tile([P, S], U8, name=f"v_scales{a}", align_bytes=64) for a in range(PASSES)]
-        v_codes = [keep.tile([P, S], U32, name=f"v_codes{a}", align_bytes=64) for a in range(PASSES)]
+        v_codes, v_scales = {}, {}
+
+        def entries(lst, lo, hi):
+            return lst[:, lo // PER_COL : hi // PER_COL]
+
+        def gather_codes(s, a, dst):
+            v_codes[s, a] = dst
+            nc.vector.tensor_copy(dst[:], tab[a][:].indirect(entries(idx, s * BANK, (s + 1) * BANK)))
+
+        def gather_scales(s, a, dst):
+            v_scales[s, a] = dst
+            nc.vector.tensor_copy(dst[:], tab_plane[:, a, :].indirect(entries(idx, s * BANK, (s + 1) * BANK)))
+
         for a in range(PASSES):
-            nc.vector.tensor_copy(v_codes[a][:], tab[a][:].indirect(idx[:]))
-        for s in range(HALVES):
-            for a in range(PASSES):
-                nc.vector.tensor_copy(
-                    v_scales[a][:, s * BANK : (s + 1) * BANK],
-                    tab_plane[:, a, :].indirect(idx[:, s * BANK // PER_COL : (s + 1) * BANK // PER_COL]),
-                )
+            for s in range(HALVES):
+                gather_codes(s, a, keep.tile([P, BANK], U32, name=f"v_codes{s}{a}", align_bytes=64))
+            if a == 0:
+                for n in range(PASSES):
+                    gather_scales(0, n, keep.tile([P, BANK], U8, name=f"v_scales0{n}", align_bytes=64))
 
         def mx_sum(bank, lhs, rhs):
             for a in range(PASSES):
@@ -173,32 +216,37 @@ def tile_list_translator_brief_scores_kernel(
         prod = {}
 
         def table_sum(b, w_ops):
-            cols = slice(b * P, (b + 1) * P)
-            v_ops = [(v_codes[a][:, cols].bitcast(FP8X4), v_scales[a][:, cols]) for a in range(PASSES)]
-            bank = psum.tile([P, H], F32, name="f_bank", tag="f", bufs=5)
+            s, n = divmod(b, BANK // P)
+            cols = slice(n * P, (n + 1) * P)
+            v_ops = [(v_codes[s, a][:, cols].bitcast(FP8X4), v_scales[s, a][:, cols]) for a in range(PASSES)]
+            bank = fresh_bank([P, H])
             mx_sum(bank, v_ops, w_ops)
             return by_slot(bank)
 
-        def f2_times_f3(b):
-            f3 = ring.tile([P, PACK, P], F32, name="f3", bufs=2)
+        def f2_times_f3(b, f3):
             nc.scalar.copy(f3[:], table_sum(b, w3_ops))
             if b % 2 == 0:
                 prod[b // 2] = ring.tile([P, 2, PACK, P], F32, name="prod", tag="prod", bufs=4)
             nc.vector.tensor_tensor(prod[b // 2][:, b % 2], table_sum(b, w2_ops), f3[:], MULT)
 
-        def times_f1(b):
-            part = prod[b // 2][:, b % 2]
-            nc.vector.tensor_tensor(part, table_sum(b, w1_ops), part, MULT)
+        def times_f1(pair, dst):
+            for n in range(2):
+                nc.vector.tensor_tensor(dst[:, n], table_sum(2 * pair + n, w1_ops), prod[pair][:, n], MULT)
+            prod[pair] = dst
 
         def quantize_weight(raw, name, copy):
             codes, scales = wide_codes(name)
-            quantize(round_and_interleave(copy, raw, H), codes[:], scales[:])
+            grouped = staging()
+            round_and_interleave(copy, raw, grouped[:])
+            quantize(grouped, codes[:], scales[:])
             return codes[:].bitcast(FP8X4), scales[:]
 
         briefs_q = {}
 
-        def quantize_briefs(s, a, copy):
-            grouped = round_and_interleave(copy, briefs_raw[s, a], BANK)
+        def quantize_briefs(s, a, copy, grouped):
+            width = BANK // len(briefs_raw[s, a])
+            for n, raw in enumerate(briefs_raw[s, a]):
+                round_and_interleave(copy, raw, grouped[:, n * width : (n + 1) * width, :])
             codes = keep.tile([P, BANK], U32, name=f"briefs_codes{s}{a}", align_bytes=64)
             scales = keep.tile([P, BANK], U8, name=f"briefs_scales{s}{a}", align_bytes=64)
             quantize(grouped, codes[:], scales[:])
@@ -206,90 +254,94 @@ def tile_list_translator_brief_scores_kernel(
 
         h = {}
 
-        def features(s):
-            h[s] = big([P, PACK, BANK], f"h{s}")
-            for n in range(BANK // P):
-                b = s * BANK // P + n
-                cols = slice(n * P, (n + 1) * P)
-                b_ops = [(briefs_q[s, a][0][:, cols].bitcast(FP8X4), briefs_q[s, a][1][:, cols]) for a in range(PASSES)]
-                d_bank = psum.tile([P, H], F32, name="d_bank", tag="g", bufs=3)
-                mx_sum(d_bank, b_ops, w4_ops)
-                d = ring.tile([P, PACK, P], F32, name="d", bufs=2)
-                nc.scalar.copy(d[:], by_slot(d_bank))
-                h_bank = psum.tile([P, PACK, P], F32, name="h_bank", tag="g", bufs=3)
-                for i in range(PACK):
-                    nc.tensor.matmul(h_bank[:, i, :], prod[b // 2][:, b % 2, i, :], ident[:],
-                                     start=True, stop=False, is_transpose=True)
-                    nc.tensor.matmul(h_bank[:, i, :], d[:, i, :], ident[:],
-                                     start=False, stop=True, is_transpose=True)
-                nc.scalar.copy(h[s][:, :, cols], h_bank[:])
+        def features(s, d_numbers, h_numbers):
+            h[s] = big([P, PACK, BANK], f"h{s}", s)
+            for first in range(0, BANK // P, 2):
+                d_banks, h_banks = {}, {}
+                for n in (first, first + 1):
+                    cols = slice(n * P, (n + 1) * P)
+                    b_ops = [(briefs_q[s, a][0][:, cols].bitcast(FP8X4), briefs_q[s, a][1][:, cols]) for a in range(PASSES)]
+                    d_banks[n] = numbered_bank([P, H], d_numbers[n])
+                    mx_sum(d_banks[n], b_ops, w4_ops)
+                for n in (first, first + 1):
+                    b = s * BANK // P + n
+                    h_banks[n] = numbered_bank([P, PACK, P], h_numbers[n])
+                    for i in range(PACK):
+                        nc.tensor.matmul(h_banks[n][:, i, :], prod[b // 2][:, b % 2, i, :], ident[:],
+                                         start=(i == 0), stop=False, is_transpose=True)
+                    d = small([P, PACK, P], F32, "d", (4 + n) % 6 + 2 * (n // 2))
+                    nc.scalar.copy(d[:], by_slot(d_banks[n]))
+                    for i in range(PACK):
+                        nc.tensor.matmul(h_banks[n][:, i, :], d[:, i, :], ident[:],
+                                         start=False, stop=(i == PACK - 1), is_transpose=True)
+                for n in (first, first + 1):
+                    nc.scalar.copy(h[s][:, :, n * P : (n + 1) * P], h_banks[n][:])
 
         def amend(i, lo, hi):
             s, off = divmod(lo, BANK)
             nc.vector.tensor_tensor(
-                page[i][:].indirect(idx3[:, lo // PER_COL : hi // PER_COL]),
-                h[s][:, i, off : off + hi - lo], weight[i][:, lo:hi], MULT,
+                page[i][:].indirect(entries(idx3, lo, hi)),
+                h[s][:, i, off : off + hi - lo], weight[lo][:, i, :], MULT,
             )
 
-        w1_ops, w4_ops = [], []
-        for a in range(PASSES):
-            for b in range(2 * a, 2 * a + 2):
-                f2_times_f3(b)
-            w1_ops.append(quantize_weight(w1_raw[a], f"w1_{a}", nc.scalar.copy))
-        for a, copy in enumerate((nc.scalar.copy, nc.vector.tensor_copy)):
-            for b in range(4 + 2 * a, 6 + 2 * a):
-                f2_times_f3(b)
-            w4_ops.append(quantize_weight(w4_raw[a], f"w4_{a}", copy))
-        for b in range(4):
-            times_f1(b)
-        quantize_briefs(0, 0, nc.scalar.copy)
-        quantize_briefs(0, 1, nc.vector.tensor_copy)
+        for b in range(PASSES):
+            f2_times_f3(b, small([P, PACK, P], F32, "f3", b))
+            gather_scales(1, b, small([P, BANK], U8, f"v_scales1{b}", b))
+        for b in range(PASSES, 4):
+            f2_times_f3(b, small([P, PACK, P], F32, "f3", 2 + b % 2))
+        w1_ops = [quantize_weight(w1_raw[a], f"w1_{a}", nc.scalar.copy) for a in range(PASSES)]
         for b in range(4, 8):
-            times_f1(b)
-        features(0)
-        quantize_briefs(1, 0, nc.scalar.copy)
-        quantize_briefs(1, 1, nc.scalar.copy)
-        features(1)
-        amend(0, 0, BANK // 2)
-        amend(0, BANK // 2, BANK)
-        amend(1, 0, BANK)
+            f2_times_f3(b, small([P, PACK, P], F32, "f3", 2 + b % 2))
+        w4_ops = [quantize_weight(w4_raw[0], "w4_0", nc.scalar.copy), quantize_weight(w4_raw[1], "w4_1", nc.vector.tensor_copy)]
+        times_f1(0, prod[0])
+        quantize_briefs(0, 0, nc.scalar.copy, late([P, BANK, PACK], BF16, "grouped00", 0))
+        quantize_briefs(0, 1, nc.scalar.copy, late([P, BANK, PACK], BF16, "grouped01", 1))
+        times_f1(1, big([P, 2, PACK, P], "triple1", 5))
+        times_f1(2, late([P, 2, PACK, P], F32, "triple2", 1))
+        times_f1(3, late([P, 2, PACK, P], F32, "triple3", 0))
+        features(0, (0, 1, 0, 1), (2, 3, 2, 3))
+        for a in range(PASSES):
+            quantize_briefs(1, a, nc.scalar.copy, staging())
+        features(1, (6, 7, 0, 1), (2, 3, 4, 5))
+        for lo in (0, BANK // 2):
+            for i in range(2):
+                amend(i, lo, lo + BANK // 2)
+        for i in range(2, PACK):
+            for lo in (0, BANK // 2):
+                amend(i, lo, lo + BANK // 2)
 
         v2_codes = keep.tile([P, S2], U32, align_bytes=64)
         v2_scales = keep.tile([P, S2], U8, align_bytes=64)
-        pairs = [mid([P, 2, BANK, 2], BF16, f"pairs{c}") for c in range(CHUNKS)]
+        nc.vector.tensor_copy(v2_codes[:], tab2[:].indirect(idx2[:]))
+        pairs = [mid([P, 2, BANK, 2], BF16, f"pairs{c}", c) for c in range(CHUNKS)]
         for i in range(PACK):
-            if i == PACK - 1:
-                nc.vector.tensor_copy(v2_codes[:], tab2[:].indirect(idx2[:]))
-            if i >= 2:
-                amend(i, 0, BANK)
             amend(i, BANK, S)
             for c in range(CHUNKS):
                 nc.scalar.copy(pairs[c][:, i // 2, :, i % 2], page[i][:, c * BANK : (c + 1) * BANK])
         nc.vector.tensor_copy(v2_scales[:], tab2_plane[:, 0, :].indirect(idx2[:]))
 
-        page_q = []
-        for c in range(CHUNKS):
-            grouped = ring.tile([P, BANK, PACK], BF16, name="grouped", tag="grouped", bufs=3, align_bytes=64)
-            nc.vector.tensor_copy(
-                grouped[:].rearrange("p c i -> p (c i)").bitcast(F32).rearrange("p (c n u) -> p c u n", n=4, u=2),
-                pairs[c][:].rearrange("p u c e -> p u (c e)").bitcast(F32).rearrange("p u (c n) -> p c u n", n=4),
-            )
-            page_q.append(wide_codes(f"page_{c}"))
-            quantize(grouped, page_q[c][0][:], page_q[c][1][:])
+        page_grouped, page_q = [], []
+        for c in range(CHUNKS + 1):
+            if c < CHUNKS:
+                page_grouped.append(staging())
+                nc.vector.tensor_copy(
+                    page_grouped[c][:].rearrange("p c i -> p (c i)").bitcast(F32).rearrange("p (c n u) -> p c u n", n=4, u=2),
+                    pairs[c][:].rearrange("p u c e -> p u (c e)").bitcast(F32).rearrange("p u (c n) -> p c u n", n=4),
+                )
+            if c > 0:
+                page_q.append(wide_codes(f"page_{c - 1}"))
+                quantize(page_grouped[c - 1], page_q[c - 1][0][:], page_q[c - 1][1][:])
 
         e = {}
 
         def scores(g):
             rows = slice(g * P, (g + 1) * P)
             if g % 2 == 0:
-                e[g] = big([P, T2], f"e{g}")
+                e[g] = big([P, T2], f"e{g}", 2 + g // 2)
             else:
                 e[g] = keep.tile([P, T2], F32, name=f"e{g}", tag="tab0", align_bytes=64)
             for c in range(CHUNKS):
-                if c % 2 == 0:
-                    e_bank = psum.tile([P, BANK], F32, name="e_bank", tag="f", bufs=5)
-                else:
-                    e_bank = psum.tile([P, BANK], F32, name="e_bank", tag="g", bufs=3)
+                e_bank = fresh_bank([P, BANK])
                 nc.tensor.matmul_mx(
                     out=e_bank[:], lhsT=v2_codes[:, rows].bitcast(FP8X4), lhsT_scale=v2_scales[:, rows],
                     rhs=page_q[c][0][:].bitcast(FP8X4), rhs_scale=page_q[c][1][:], start=True, stop=True,
@@ -297,30 +349,47 @@ def tile_list_translator_brief_scores_kernel(
                 copy = nc.vector.tensor_copy if (g, c) in VECTOR_EVAC else nc.scalar.copy
                 copy(e[g][:, c * BANK : (c + 1) * BANK], e_bank[:])
 
-        def pick(g, lo, width):
-            x = ring.tile([P, width], F32, name="x", bufs=3)
-            nc.vector.tensor_copy(x[:], e[g][:].indirect(idx4[:, lo // PER_COL : (lo + width) // PER_COL]))
-            return x
+        x, inv = {}, {}
 
-        def softsign(x, g, lo, width):
-            inv = ring.tile([P, width], F32, name="inv", tag="prod", bufs=4)
-            nc.scalar.activation(inv[:], x[:], ACT.Abs)
-            nc.scalar.activation(inv[:], inv[:], ACT.Abs_reciprocal_sqrt, bias=room_col[:, g : g + 1])
-            nc.scalar.activation(inv[:], inv[:], ACT.Square)
-            result = mid([P, width], F32, "result")
-            nc.vector.tensor_tensor(result[:], x[:], inv[:], MULT)
-            nc.sync.dma_start(out[g * P : (g + 1) * P, lo : lo + width], result[:])
+        def pick(u):
+            g, s = divmod(u, HALVES)
+            x[u] = small([P, BANK], F32, "x", u % 6)
+            nc.vector.tensor_copy(x[u][:], e[g][:].indirect(entries(idx4, s * BANK, (s + 1) * BANK)))
 
+        def magnitude(u):
+            if u % HALVES == 0:
+                both = ring.tile([P, HALVES, BANK], F32, name="inv", tag="prod", bufs=4)
+                inv[u], inv[u + 1] = both[:, 0, :], both[:, 1, :]
+            nc.scalar.activation(inv[u], x[u][:], ACT.Abs)
+
+        def inverse_root(u):
+            g = u // HALVES
+            nc.scalar.activation(inv[u], inv[u], ACT.Abs_reciprocal_sqrt, bias=room_col[:, g : g + 1])
+
+        def finish(u):
+            g, s = divmod(u, HALVES)
+            nc.scalar.activation(inv[u], inv[u], ACT.Square)
+            result = mid([P, BANK], F32, "result", u % CHUNKS)
+            nc.vector.tensor_tensor(result[:], x[u][:], inv[u], MULT)
+            nc.sync.dma_start(out[g * P : (g + 1) * P, s * BANK : (s + 1) * BANK], result[:])
+
+        units = GROUPS * HALVES
         scores(0)
-        x0 = pick(0, 0, PICK)
+        pick(0)
+        pick(1)
         scores(1)
         scores(2)
-        x1 = pick(1, 0, PICK)
-        softsign(x0, 0, 0, PICK)
+        pick(2)
+        pick(3)
         scores(3)
-        x2 = pick(2, 0, PICK)
-        softsign(x1, 1, 0, PICK)
-        last = [pick(3, lo, BANK) for lo in range(0, PICK, BANK)]
-        softsign(x2, 2, 0, PICK)
-        for n, x in enumerate(last):
-            softsign(x, 3, n * BANK, BANK)
+        pick(4)
+        pick(5)
+        for step in range(units + 2):
+            if step < units:
+                magnitude(step)
+            if 1 <= step <= units:
+                inverse_root(step - 1)
+            if step >= 2:
+                finish(step - 2)
+            if 2 <= step < units - 4:
+                pick(step + 4)

@@ -28,7 +28,7 @@ PER_COL = 16
 HALVES = S // BANK
 CHUNKS = T2 // BANK
 GROUPS = S2 // P
-VECTOR_EVAC = ((0, 3), (3, 0), (3, 1), (3, 2), (3, 3))
+VECTOR_EVAC = ((0, 2), (0, 3), (3, 0), (3, 1), (3, 2), (3, 3))
 
 
 def tile_list_translator_brief_scores_kernel(
@@ -96,7 +96,7 @@ def tile_list_translator_brief_scores_kernel(
                 out=codes.bitcast(FP8X4), scales=scales, in_=grouped[:].rearrange("p c i -> p (c i)")
             )
 
-        tab_plane = keep.tile([P, PASSES, T], U8, align_bytes=64)
+        tab_plane = keep.tile([P, T], U8, name="tab_plane", align_bytes=64)
         nc.vector.memset(tab_plane[:].bitcast(I32), 0)
         w2_plane = keep.tile([P, PASSES, H], U8, align_bytes=64)
         w3_plane = keep.tile([P, PASSES, H], U8, align_bytes=64)
@@ -104,6 +104,8 @@ def tile_list_translator_brief_scores_kernel(
         nc.vector.memset(w3_plane[:].bitcast(I32), 0)
         nc.vector.memset(w2_plane[:].bitcast(I32), 0)
         nc.vector.memset(tab2_plane[:].bitcast(I32), 0)
+        v_scales_moved = keep.tile([P, S], U8, name="v_scales_moved", align_bytes=64)
+        nc.vector.memset(v_scales_moved[:].bitcast(I32), 0)
         ones = keep.tile([P, 1], F32)
         nc.vector.memset(ones[:], 1.0)
         warm = keep.tile([P, 1], F32)
@@ -118,21 +120,41 @@ def tile_list_translator_brief_scores_kernel(
 
         tab = [keep.tile([P, T], U32, name=f"tab{a}", tag=f"tab{a}", align_bytes=64) for a in range(PASSES)]
         load_words(tab[0][:], tab_words[0])
-        load_scale_rows(nc.scalar, tab_plane, tab_scales)
+        for q in range(QUADS):
+            nc.sync.dma_start(
+                tab_plane[32 * q : 32 * q + 4 * PASSES].bitcast(I32), tab_scales[:, 4 * q : 4 * q + 4, :].bitcast(I32)
+            )
         w3_codes = keep.tile([P, PASSES, H], U32, align_bytes=64)
         nc.sync.dma_start(w3_codes[:].bitcast(I32), w3_words.rearrange("a p c i -> p a (c i)").bitcast(I32))
-        load_scale_rows(nc.scalar, w3_plane, w3_scales)
+        load_scale_rows(nc.sync, w3_plane, w3_scales)
+        load_words(tab[1][:], tab_words[1])
         w2_codes = keep.tile([P, PASSES, 2 * H], U8, align_bytes=64)
         nc.sync.dma_start(w2_codes[:].bitcast(I32), w2_words.rearrange("a p c -> p a c").bitcast(I32))
-        load_scale_rows(nc.scalar, w2_plane, w2_scales)
-        load_words(tab[1][:], tab_words[1])
+        load_scale_rows(nc.sync, w2_plane, w2_scales)
 
         def load_weight_pass(w, a, name, slot):
             raw = big([P, PACK, H], f"{name}_raw{a}", slot)
             load_rows(raw, w[a * K_PASS : (a + 1) * K_PASS, :])
             return raw
 
-        w1_raw = [load_weight_pass(w1, a, "w1", a) for a in range(PASSES)]
+        w1_raw = [load_weight_pass(w1, 0, "w1", 0)]
+
+        def entries(lst, lo, hi):
+            return lst[:, lo // PER_COL : hi // PER_COL]
+
+        v_codes = [keep.tile([P, S], U32, name=f"v_codes{a}", align_bytes=64) for a in range(PASSES)]
+        v_scales = keep.tile([P, S], U8, name="v_scales", align_bytes=64)
+        nc.vector.tensor_copy(v_codes[0][:], tab[0][:].indirect(idx[:]))
+        nc.vector.tensor_copy(v_scales[:], tab_plane[:].indirect(idx[:]))
+        for q in range(QUADS):
+            nc.sync.dma_start(
+                v_scales_moved[32 * q : 32 * q + 4].bitcast(I32), v_scales[32 * q + 4 : 32 * q + 8].bitcast(I32)
+            )
+        for s in range(HALVES):
+            nc.vector.tensor_copy(
+                v_codes[1][:, s * BANK : (s + 1) * BANK], tab[1][:].indirect(entries(idx, s * BANK, (s + 1) * BANK))
+            )
+        w1_raw.append(load_weight_pass(w1, 1, "w1", 1))
         w4_raw = [load_weight_pass(w4, a, "w4", 2 + a) for a in range(PASSES)]
 
         page = []
@@ -145,67 +167,30 @@ def tile_list_translator_brief_scores_kernel(
 
         def load_briefs(s):
             for a in range(PASSES):
-                rows = briefs[a * K_PASS : (a + 1) * K_PASS, s * BANK : (s + 1) * BANK]
-                if s == 0:
-                    briefs_raw[s, a] = [big([P, PACK, BANK], f"briefs_raw{s}{a}", 4 + a)]
-                else:
-                    briefs_raw[s, a] = [mid([P, PACK, BANK // 2], F32, f"briefs_raw{s}{a}{n}", 2 * a + n) for n in range(2)]
-                width = BANK // len(briefs_raw[s, a])
-                for n, raw in enumerate(briefs_raw[s, a]):
-                    load_rows(raw, rows[:, n * width : (n + 1) * width])
+                briefs_raw[s, a] = big([P, PACK, BANK], f"briefs_raw{s}{a}", 4 - 2 * s + a)
+                load_rows(briefs_raw[s, a], briefs[a * K_PASS : (a + 1) * K_PASS, s * BANK : (s + 1) * BANK])
 
         load_briefs(0)
         idx3 = load_list(offs3, "idx3")
         weight = {}
 
-        def load_weight(lo, hi):
-            weight[lo] = keep.tile([P, PACK, hi - lo], F32, name=f"weight{lo}")
-            rows = wgs.rearrange("(q i) j -> q i j", i=PACK)[:, :, lo:hi]
+        def load_weight(lo, hi, slots):
+            tile = keep.tile([P, len(slots), hi - lo], F32, name=f"weight{lo}_{slots[0]}")
+            rows = wgs.rearrange("(q i) j -> q i j", i=PACK)[:, slots[0] : slots[-1] + 1, lo:hi]
             for q in (0, 2, 1, 3):
-                nc.sync.dma_start(weight[lo][32 * q : 32 * q + 32], rows)
+                nc.sync.dma_start(tile[32 * q : 32 * q + 32], rows)
+            for n, i in enumerate(slots):
+                weight[i, lo] = tile[:, n, :]
 
-        load_weight(0, BANK // 2)
+        load_weight(0, BANK // 2, range(2))
         load_page(0)
         load_page(1)
-        load_weight(BANK // 2, BANK)
-        load_briefs(1)
-        for i in range(2, PACK):
-            load_page(i)
-        idx2 = load_list(offs2, "idx2")
-        tab2 = keep.tile([P, T3], U32, name="tab2", align_bytes=64)
-        load_words(tab2[:], tab2_words[0])
-        load_weight(BANK, S)
-        load_scale_rows(nc.sync, tab2_plane, tab2_scales)
-        idx4 = load_list(offs4, "idx4")
-        room_col = keep.tile([P, GROUPS], F32)
-        with nc.allow_non_contiguous_dma(reason="one value of room for each partition and group"):
-            nc.sync.dma_start(room_col[:], room.rearrange("(g p) -> p g", p=P))
-
-        v_codes, v_scales = {}, {}
-
-        def entries(lst, lo, hi):
-            return lst[:, lo // PER_COL : hi // PER_COL]
-
-        def gather_codes(s, a, dst):
-            v_codes[s, a] = dst
-            nc.vector.tensor_copy(dst[:], tab[a][:].indirect(entries(idx, s * BANK, (s + 1) * BANK)))
-
-        def gather_scales(s, a, dst):
-            v_scales[s, a] = dst
-            nc.vector.tensor_copy(dst[:], tab_plane[:, a, :].indirect(entries(idx, s * BANK, (s + 1) * BANK)))
-
-        for a in range(PASSES):
-            for s in range(HALVES):
-                gather_codes(s, a, keep.tile([P, BANK], U32, name=f"v_codes{s}{a}", align_bytes=64))
-            if a == 0:
-                for n in range(PASSES):
-                    gather_scales(0, n, keep.tile([P, BANK], U8, name=f"v_scales0{n}", align_bytes=64))
-
-        def mx_sum(bank, lhs, rhs):
-            for a in range(PASSES):
+        load_weight(BANK // 2, BANK, range(2))
+        def mx_sum(bank, lhs, rhs, order=(0, 1)):
+            for n, a in enumerate(order):
                 nc.tensor.matmul_mx(
                     out=bank[:], lhsT=lhs[a][0], lhsT_scale=lhs[a][1], rhs=rhs[a][0], rhs_scale=rhs[a][1],
-                    start=(a == 0), stop=(a == PASSES - 1),
+                    start=(n == 0), stop=(n == PASSES - 1),
                 )
 
         def by_slot(bank):
@@ -215,23 +200,23 @@ def tile_list_translator_brief_scores_kernel(
         w3_ops = [(w3_codes[:, a, :].bitcast(FP8X4), w3_plane[:, a, :]) for a in range(PASSES)]
         prod = {}
 
-        def table_sum(b, w_ops):
-            s, n = divmod(b, BANK // P)
-            cols = slice(n * P, (n + 1) * P)
-            v_ops = [(v_codes[s, a][:, cols].bitcast(FP8X4), v_scales[s, a][:, cols]) for a in range(PASSES)]
-            bank = fresh_bank([P, H])
-            mx_sum(bank, v_ops, w_ops)
+        def table_sum(b, w_ops, second_plane, number, order=(0, 1)):
+            cols = slice(b * P, (b + 1) * P)
+            planes = (v_scales[:, cols], second_plane[:, cols])
+            v_ops = [(v_codes[a][:, cols].bitcast(FP8X4), planes[a]) for a in range(PASSES)]
+            bank = numbered_bank([P, H], number)
+            mx_sum(bank, v_ops, w_ops, order)
             return by_slot(bank)
 
         def f2_times_f3(b, f3):
-            nc.scalar.copy(f3[:], table_sum(b, w3_ops))
+            nc.scalar.copy(f3, table_sum(b, w3_ops, v_scales[4:P], 2 * (b % 4) + b // 4))
             if b % 2 == 0:
                 prod[b // 2] = ring.tile([P, 2, PACK, P], F32, name="prod", tag="prod", bufs=4)
-            nc.vector.tensor_tensor(prod[b // 2][:, b % 2], table_sum(b, w2_ops), f3[:], MULT)
+            nc.vector.tensor_tensor(prod[b // 2][:, b % 2], table_sum(b, w2_ops, v_scales_moved, 2 * (b % 4) + 1 - b // 4, (1, 0)), f3, MULT)
 
         def times_f1(pair, dst):
             for n in range(2):
-                nc.vector.tensor_tensor(dst[:, n], table_sum(2 * pair + n, w1_ops), prod[pair][:, n], MULT)
+                nc.vector.tensor_tensor(dst[:, n], table_sum(2 * pair + n, w1_ops, v_scales[4:P], 2 * pair + n), prod[pair][:, n], MULT)
             prod[pair] = dst
 
         def quantize_weight(raw, name, copy):
@@ -244,9 +229,7 @@ def tile_list_translator_brief_scores_kernel(
         briefs_q = {}
 
         def quantize_briefs(s, a, copy, grouped):
-            width = BANK // len(briefs_raw[s, a])
-            for n, raw in enumerate(briefs_raw[s, a]):
-                round_and_interleave(copy, raw, grouped[:, n * width : (n + 1) * width, :])
+            round_and_interleave(copy, briefs_raw[s, a], grouped[:])
             codes = keep.tile([P, BANK], U32, name=f"briefs_codes{s}{a}", align_bytes=64)
             scales = keep.tile([P, BANK], U8, name=f"briefs_scales{s}{a}", align_bytes=64)
             quantize(grouped, codes[:], scales[:])
@@ -281,20 +264,30 @@ def tile_list_translator_brief_scores_kernel(
             s, off = divmod(lo, BANK)
             nc.vector.tensor_tensor(
                 page[i][:].indirect(entries(idx3, lo, hi)),
-                h[s][:, i, off : off + hi - lo], weight[lo][:, i, :], MULT,
+                h[s][:, i, off : off + hi - lo], weight[i, lo], MULT,
             )
 
-        for b in range(PASSES):
-            f2_times_f3(b, small([P, PACK, P], F32, "f3", b))
-            gather_scales(1, b, small([P, BANK], U8, f"v_scales1{b}", b))
-        for b in range(PASSES, 4):
-            f2_times_f3(b, small([P, PACK, P], F32, "f3", 2 + b % 2))
-        w1_ops = [quantize_weight(w1_raw[a], f"w1_{a}", nc.scalar.copy) for a in range(PASSES)]
-        for b in range(4, 8):
-            f2_times_f3(b, small([P, PACK, P], F32, "f3", 2 + b % 2))
-        w4_ops = [quantize_weight(w4_raw[0], "w4_0", nc.scalar.copy), quantize_weight(w4_raw[1], "w4_1", nc.vector.tensor_copy)]
+        for b in range(S // P):
+            f2_times_f3(b, small([P, PACK, P], F32, "f3", b % 4)[:])
+        w1_ops = [quantize_weight(w1_raw[a], f"w1_{a}", nc.vector.tensor_copy) for a in range(PASSES)]
+        w4_ops = [quantize_weight(w4_raw[a], f"w4_{a}", nc.scalar.copy) for a in range(PASSES)]
+        load_briefs(1)
+        for i in range(2, PACK):
+            load_weight(0, BANK, range(i, i + 1))
+            load_page(i)
+        load_weight(BANK, S, range(2))
+        idx2 = load_list(offs2, "idx2")
+        tab2 = keep.tile([P, T3], U32, name="tab2", align_bytes=64)
+        load_words(tab2[:], tab2_words[0])
+        load_weight(BANK, S, range(2, PACK))
+        load_scale_rows(nc.sync, tab2_plane, tab2_scales)
+        idx4 = load_list(offs4, "idx4")
+        room_col = keep.tile([P, GROUPS], F32)
+        with nc.allow_non_contiguous_dma(reason="one value of room for each partition and group"):
+            nc.sync.dma_start(room_col[:], room.rearrange("(g p) -> p g", p=P))
+
         times_f1(0, prod[0])
-        quantize_briefs(0, 0, nc.scalar.copy, late([P, BANK, PACK], BF16, "grouped00", 0))
+        quantize_briefs(0, 0, nc.vector.tensor_copy, late([P, BANK, PACK], BF16, "grouped00", 0))
         quantize_briefs(0, 1, nc.scalar.copy, late([P, BANK, PACK], BF16, "grouped01", 1))
         times_f1(1, big([P, 2, PACK, P], "triple1", 5))
         times_f1(2, late([P, 2, PACK, P], F32, "triple2", 1))
@@ -307,8 +300,7 @@ def tile_list_translator_brief_scores_kernel(
             for i in range(2):
                 amend(i, lo, lo + BANK // 2)
         for i in range(2, PACK):
-            for lo in (0, BANK // 2):
-                amend(i, lo, lo + BANK // 2)
+            amend(i, 0, BANK)
 
         v2_codes = keep.tile([P, S2], U32, align_bytes=64)
         v2_scales = keep.tile([P, S2], U8, align_bytes=64)
@@ -336,10 +328,7 @@ def tile_list_translator_brief_scores_kernel(
 
         def scores(g):
             rows = slice(g * P, (g + 1) * P)
-            if g % 2 == 0:
-                e[g] = big([P, T2], f"e{g}", 2 + g // 2)
-            else:
-                e[g] = keep.tile([P, T2], F32, name=f"e{g}", tag="tab0", align_bytes=64)
+            e[g] = big([P, T2], f"e{g}", 2 + min(g, 2))
             for c in range(CHUNKS):
                 e_bank = fresh_bank([P, BANK])
                 nc.tensor.matmul_mx(
@@ -353,7 +342,7 @@ def tile_list_translator_brief_scores_kernel(
 
         def pick(u):
             g, s = divmod(u, HALVES)
-            x[u] = small([P, BANK], F32, "x", u % 6)
+            x[u] = small([P, BANK], F32, "x", u)
             nc.vector.tensor_copy(x[u][:], e[g][:].indirect(entries(idx4, s * BANK, (s + 1) * BANK)))
 
         def magnitude(u):
@@ -369,9 +358,8 @@ def tile_list_translator_brief_scores_kernel(
         def finish(u):
             g, s = divmod(u, HALVES)
             nc.scalar.activation(inv[u], inv[u], ACT.Square)
-            result = mid([P, BANK], F32, "result", u % CHUNKS)
-            nc.vector.tensor_tensor(result[:], x[u][:], inv[u], MULT)
-            nc.sync.dma_start(out[g * P : (g + 1) * P, s * BANK : (s + 1) * BANK], result[:])
+            nc.vector.tensor_tensor(x[u][:], x[u][:], inv[u], MULT)
+            nc.sync.dma_start(out[g * P : (g + 1) * P, s * BANK : (s + 1) * BANK], x[u][:])
 
         units = GROUPS * HALVES
         scores(0)
@@ -381,9 +369,11 @@ def tile_list_translator_brief_scores_kernel(
         scores(2)
         pick(2)
         pick(3)
-        scores(3)
         pick(4)
         pick(5)
+        scores(3)
+        pick(6)
+        pick(7)
         for step in range(units + 2):
             if step < units:
                 magnitude(step)
@@ -391,5 +381,3 @@ def tile_list_translator_brief_scores_kernel(
                 inverse_root(step - 1)
             if step >= 2:
                 finish(step - 2)
-            if 2 <= step < units - 4:
-                pick(step + 4)

@@ -3,7 +3,7 @@ from contextlib import ExitStack
 import concourse.mybir as mybir
 from concourse.masks import make_identity
 
-K, H, T, S, T2, T3, S2, PICK = 1024, 512, 2048, 1024, 2048, 2048, 512, 1024
+K, H, T, S, T2, T3, S2 = 1024, 512, 2048, 1024, 2048, 2048, 512
 FLOPS = 4 * 2 * K * H * S + 2 * H * S2 * T2
 
 F32 = mybir.dt.float32
@@ -18,17 +18,22 @@ MULT = mybir.AluOpType.mult
 ACT = mybir.ActivationFunctionType
 
 P = 128
-PACK = 4
-K_PASS = P * PACK
+SLOTS = 4
+K_PASS = P * SLOTS
 PASSES = K // K_PASS
-QUADS = 4
+QUADRANTS = 4
+SCALE_ROWS = 4
 BANK = 512
 BANKS = 8
-PER_COL = 16
-HALVES = S // BANK
+PER_COLUMN = 16
+HALF = S // 2
+QUARTER = S // 4
+BLOCKS = S // P
+HALF_BLOCKS = HALF // P
 CHUNKS = T2 // BANK
 GROUPS = S2 // P
-VECTOR_EVAC = ((0, 2), (0, 3), (3, 0), (3, 1), (3, 2), (3, 3))
+PIECES = 2 * GROUPS
+LINE = 4
 
 
 def tile_list_translator_brief_scores_kernel(
@@ -38,346 +43,343 @@ def tile_list_translator_brief_scores_kernel(
     nc = tc.nc
     with ExitStack() as ctx:
         keep = ctx.enter_context(tc.tile_pool(name="keep", bufs=1))
-        ring = ctx.enter_context(tc.tile_pool(name="ring", bufs=1))
+        reuse = ctx.enter_context(tc.tile_pool(name="reuse", bufs=1))
         psum = ctx.enter_context(tc.psum_pool(name="psum", bufs=1))
 
-        def big(shape, name, slot):
-            return ring.tile(shape, F32, name=name, tag=f"big{slot}", align_bytes=64)
+        def buffer8(number, shape, name):
+            return reuse.tile(shape, F32, name=name, tag=f"buffer8_{number}", align_bytes=64)
 
-        def mid(shape, dtype, name, slot):
-            return ring.tile(shape, dtype, name=name, tag=f"mid{slot}", align_bytes=64)
+        def buffer4(number, shape, dtype, name):
+            return reuse.tile(shape, dtype, name=name, tag=f"buffer4_{number}", align_bytes=64)
 
-        def late(shape, dtype, name, slot):
-            return ring.tile(shape, dtype, name=name, tag=f"late{slot}", align_bytes=64)
+        def buffer2(number, shape, name):
+            return reuse.tile(shape, F32, name=name, tag=f"buffer2_{number}", align_bytes=64)
 
-        def small(shape, dtype, name, slot):
-            return ring.tile(shape, dtype, name=name, tag=f"small{slot}", align_bytes=64)
-
-        banks_taken = []
-
-        def numbered_bank(shape, number):
+        def bank(number, shape):
             return psum.tile(shape, F32, name=f"bank{number}", tag=f"bank{number}")
 
-        def fresh_bank(shape):
-            banks_taken.append(shape)
-            return numbered_bank(shape, (len(banks_taken) - 1) % BANKS)
+        def staging():
+            return reuse.tile([P, BANK, SLOTS], BF16, name="staged", tag="staged", bufs=3, align_bytes=64)
 
-        def wide_codes(name):
-            codes = ring.tile([P, BANK], U32, name=name + "_codes", tag="wide_codes", bufs=4, align_bytes=64)
-            scales = ring.tile([P, BANK], U8, name=name + "_scales", tag="wide_scales", bufs=4, align_bytes=64)
-            return codes, scales
+        def moving_operand(name):
+            words = reuse.tile([P, BANK], U32, name=name + "_words", tag="moving_words", bufs=4, align_bytes=64)
+            scales = reuse.tile([P, BANK], U8, name=name + "_scales", tag="moving_scales", bufs=4, align_bytes=64)
+            return words, scales
+
+        def zeroed_scales(shape, name):
+            scales = keep.tile(shape, U8, name=name, align_bytes=64)
+            nc.vector.memset(scales[:].bitcast(I32), 0)
+            return scales
 
         def load_list(src, name):
             lst = keep.tile(list(src.shape), U16, name=name)
             nc.sync.dma_start(lst[:], src)
             return lst
 
-        def load_scale_rows(queue, plane, src):
-            for q in range(QUADS):
-                queue.dma_start(
-                    plane[32 * q : 32 * q + 4].bitcast(I32),
-                    src[:, 4 * q : 4 * q + 4, :].rearrange("a r c -> r a c").bitcast(I32),
-                )
-
-        def load_rows(raw, src):
-            nc.sync.dma_start(raw[:], src.rearrange("(p i) c -> p i c", i=PACK))
-
-        def staging():
-            return ring.tile([P, BANK, PACK], BF16, name="grouped", tag="grouped", bufs=3, align_bytes=64)
-
-        def round_and_interleave(copy, raw, grouped):
-            copy(
-                grouped.rearrange("p (c n) i -> p c i n", n=4),
-                raw[:].rearrange("p i (c n) -> p c i n", n=4),
-            )
-
-        def quantize(grouped, codes, scales):
-            nc.vector.quantize_mx(
-                out=codes.bitcast(FP8X4), scales=scales, in_=grouped[:].rearrange("p c i -> p (c i)")
-            )
-
-        tab_plane = keep.tile([P, T], U8, name="tab_plane", align_bytes=64)
-        nc.vector.memset(tab_plane[:].bitcast(I32), 0)
-        w2_plane = keep.tile([P, PASSES, H], U8, align_bytes=64)
-        w3_plane = keep.tile([P, PASSES, H], U8, align_bytes=64)
-        tab2_plane = keep.tile([P, 1, T3], U8, align_bytes=64)
-        nc.vector.memset(w3_plane[:].bitcast(I32), 0)
-        nc.vector.memset(w2_plane[:].bitcast(I32), 0)
-        nc.vector.memset(tab2_plane[:].bitcast(I32), 0)
-        v_scales_moved = keep.tile([P, S], U8, name="v_scales_moved", align_bytes=64)
-        nc.vector.memset(v_scales_moved[:].bitcast(I32), 0)
-        ones = keep.tile([P, 1], F32)
-        nc.vector.memset(ones[:], 1.0)
-        warm = keep.tile([P, 1], F32)
-
-        idx = load_list(offs, "idx")
-        nc.scalar.activation(warm[:], ones[:], ACT.Abs_reciprocal_sqrt)
-        ident = keep.tile([P, P], F32)
-        make_identity(nc, ident[:])
+        def entries(lst, lo, hi):
+            return lst[:, lo // PER_COLUMN : hi // PER_COLUMN]
 
         def load_words(words, src):
             nc.sync.dma_start(words.bitcast(I32), src.rearrange("p t i -> p (t i)").bitcast(I32))
 
-        tab = [keep.tile([P, T], U32, name=f"tab{a}", tag=f"tab{a}", align_bytes=64) for a in range(PASSES)]
-        load_words(tab[0][:], tab_words[0])
-        for q in range(QUADS):
-            nc.sync.dma_start(
-                tab_plane[32 * q : 32 * q + 4 * PASSES].bitcast(I32), tab_scales[:, 4 * q : 4 * q + 4, :].bitcast(I32)
-            )
-        w3_codes = keep.tile([P, PASSES, H], U32, align_bytes=64)
-        nc.sync.dma_start(w3_codes[:].bitcast(I32), w3_words.rearrange("a p c i -> p a (c i)").bitcast(I32))
-        load_scale_rows(nc.sync, w3_plane, w3_scales)
-        load_words(tab[1][:], tab_words[1])
-        w2_codes = keep.tile([P, PASSES, 2 * H], U8, align_bytes=64)
-        nc.sync.dma_start(w2_codes[:].bitcast(I32), w2_words.rearrange("a p c -> p a c").bitcast(I32))
-        load_scale_rows(nc.sync, w2_plane, w2_scales)
+        def load_scale_rows(scales, src):
+            for q in range(QUADRANTS):
+                nc.sync.dma_start(
+                    scales[32 * q : 32 * q + SCALE_ROWS].bitcast(I32),
+                    src[:, SCALE_ROWS * q : SCALE_ROWS * (q + 1), :].rearrange("a r c -> r a c").bitcast(I32),
+                )
 
-        def load_weight_pass(w, a, name, slot):
-            raw = big([P, PACK, H], f"{name}_raw{a}", slot)
-            load_rows(raw, w[a * K_PASS : (a + 1) * K_PASS, :])
+        def load_pass(number, src, name):
+            raw = buffer8(number, [P, SLOTS, BANK], name)
+            nc.sync.dma_start(raw[:], src.rearrange("(p i) c -> p i c", i=SLOTS))
             return raw
 
-        w1_raw = [load_weight_pass(w1, 0, "w1", 0)]
-
-        def entries(lst, lo, hi):
-            return lst[:, lo // PER_COL : hi // PER_COL]
-
-        v_codes = [keep.tile([P, S], U32, name=f"v_codes{a}", align_bytes=64) for a in range(PASSES)]
-        v_scales = keep.tile([P, S], U8, name="v_scales", align_bytes=64)
-        nc.vector.tensor_copy(v_codes[0][:], tab[0][:].indirect(idx[:]))
-        nc.vector.tensor_copy(v_scales[:], tab_plane[:].indirect(idx[:]))
-        for q in range(QUADS):
-            nc.sync.dma_start(
-                v_scales_moved[32 * q : 32 * q + 4].bitcast(I32), v_scales[32 * q + 4 : 32 * q + 8].bitcast(I32)
+        def interleave_on_scalar(raw, staged):
+            nc.scalar.copy(
+                staged[:].rearrange("p (c n) i -> p c i n", n=LINE),
+                raw[:].rearrange("p i (c n) -> p c i n", n=LINE),
             )
-        for s in range(HALVES):
-            nc.vector.tensor_copy(
-                v_codes[1][:, s * BANK : (s + 1) * BANK], tab[1][:].indirect(entries(idx, s * BANK, (s + 1) * BANK))
+
+        def interleave_on_vector(raw, staged):
+            nc.vector.tensor_copy(staged[:], raw[:].rearrange("p i c -> p c i"))
+
+        def quantize(staged, words, scales):
+            nc.vector.quantize_mx(
+                out=words[:].bitcast(FP8X4), scales=scales[:], in_=staged[:].rearrange("p c i -> p (c i)")
             )
-        w1_raw.append(load_weight_pass(w1, 1, "w1", 1))
-        w4_raw = [load_weight_pass(w4, a, "w4", 2 + a) for a in range(PASSES)]
 
-        page = []
-
-        def load_page(i):
-            page.append(keep.tile([P, T2], F32, name=f"page{i}"))
-            nc.sync.dma_start(page[i][:], page0.rearrange("(p i) t -> p i t", i=PACK)[:, i, :])
-
-        briefs_raw = {}
-
-        def load_briefs(s):
-            for a in range(PASSES):
-                briefs_raw[s, a] = big([P, PACK, BANK], f"briefs_raw{s}{a}", 4 - 2 * s + a)
-                load_rows(briefs_raw[s, a], briefs[a * K_PASS : (a + 1) * K_PASS, s * BANK : (s + 1) * BANK])
-
-        load_briefs(0)
-        idx3 = load_list(offs3, "idx3")
-        weight = {}
-
-        def load_weight(lo, hi, slots):
-            tile = keep.tile([P, len(slots), hi - lo], F32, name=f"weight{lo}_{slots[0]}")
-            rows = wgs.rearrange("(q i) j -> q i j", i=PACK)[:, slots[0] : slots[-1] + 1, lo:hi]
-            for q in (0, 2, 1, 3):
-                nc.sync.dma_start(tile[32 * q : 32 * q + 32], rows)
-            for n, i in enumerate(slots):
-                weight[i, lo] = tile[:, n, :]
-
-        load_weight(0, BANK // 2, range(2))
-        load_page(0)
-        load_page(1)
-        load_weight(BANK // 2, BANK, range(2))
-        def mx_sum(bank, lhs, rhs, order=(0, 1)):
-            for n, a in enumerate(order):
+        def mx_sum(acc, lhs, rhs, pass_order=(0, 1)):
+            for n, a in enumerate(pass_order):
                 nc.tensor.matmul_mx(
-                    out=bank[:], lhsT=lhs[a][0], lhsT_scale=lhs[a][1], rhs=rhs[a][0], rhs_scale=rhs[a][1],
+                    out=acc[:], lhsT=lhs[a][0], lhsT_scale=lhs[a][1], rhs=rhs[a][0], rhs_scale=rhs[a][1],
                     start=(n == 0), stop=(n == PASSES - 1),
                 )
 
-        def by_slot(bank):
-            return bank[:].rearrange("j (m i) -> j i m", i=PACK)
+        def by_slot(acc):
+            return acc[:].rearrange("j (p i) -> j i p", i=SLOTS)
 
-        w2_ops = [(w2_codes[:, a, :].bitcast(FP4X4), w2_plane[:, a, :]) for a in range(PASSES)]
-        w3_ops = [(w3_codes[:, a, :].bitcast(FP8X4), w3_plane[:, a, :]) for a in range(PASSES)]
-        prod = {}
+        tab_scale_rows = zeroed_scales([P, T], "tab_scale_rows")
+        w3_scale_rows = zeroed_scales([P, PASSES, H], "w3_scale_rows")
+        w2_scale_rows = zeroed_scales([P, PASSES, H], "w2_scale_rows")
+        tab2_scale_rows = zeroed_scales([P, 1, T3], "tab2_scale_rows")
+        v_scales_raised = zeroed_scales([P, S], "v_scales_raised")
+        ident = keep.tile([P, P], F32, name="ident")
+        make_identity(nc, ident[:])
 
-        def table_sum(b, w_ops, second_plane, number, order=(0, 1)):
-            cols = slice(b * P, (b + 1) * P)
-            planes = (v_scales[:, cols], second_plane[:, cols])
-            v_ops = [(v_codes[a][:, cols].bitcast(FP8X4), planes[a]) for a in range(PASSES)]
-            bank = numbered_bank([P, H], number)
-            mx_sum(bank, v_ops, w_ops, order)
-            return by_slot(bank)
-
-        def f2_times_f3(b, f3):
-            nc.scalar.copy(f3, table_sum(b, w3_ops, v_scales[4:P], 2 * (b % 4) + b // 4))
-            if b % 2 == 0:
-                prod[b // 2] = ring.tile([P, 2, PACK, P], F32, name="prod", tag="prod", bufs=4)
-            nc.vector.tensor_tensor(prod[b // 2][:, b % 2], table_sum(b, w2_ops, v_scales_moved, 2 * (b % 4) + 1 - b // 4, (1, 0)), f3, MULT)
-
-        def times_f1(pair, dst):
-            for n in range(2):
-                nc.vector.tensor_tensor(dst[:, n], table_sum(2 * pair + n, w1_ops, v_scales[4:P], 2 * pair + n), prod[pair][:, n], MULT)
-            prod[pair] = dst
-
-        def quantize_weight(raw, name, copy):
-            codes, scales = wide_codes(name)
-            grouped = staging()
-            round_and_interleave(copy, raw, grouped[:])
-            quantize(grouped, codes[:], scales[:])
-            return codes[:].bitcast(FP8X4), scales[:]
-
-        briefs_q = {}
-
-        def quantize_briefs(s, a, copy, grouped):
-            round_and_interleave(copy, briefs_raw[s, a], grouped[:])
-            codes = keep.tile([P, BANK], U32, name=f"briefs_codes{s}{a}", align_bytes=64)
-            scales = keep.tile([P, BANK], U8, name=f"briefs_scales{s}{a}", align_bytes=64)
-            quantize(grouped, codes[:], scales[:])
-            briefs_q[s, a] = codes, scales
-
-        h = {}
-
-        def features(s, d_numbers, h_numbers):
-            h[s] = big([P, PACK, BANK], f"h{s}", s)
-            for first in range(0, BANK // P, 2):
-                d_banks, h_banks = {}, {}
-                for n in (first, first + 1):
-                    cols = slice(n * P, (n + 1) * P)
-                    b_ops = [(briefs_q[s, a][0][:, cols].bitcast(FP8X4), briefs_q[s, a][1][:, cols]) for a in range(PASSES)]
-                    d_banks[n] = numbered_bank([P, H], d_numbers[n])
-                    mx_sum(d_banks[n], b_ops, w4_ops)
-                for n in (first, first + 1):
-                    b = s * BANK // P + n
-                    h_banks[n] = numbered_bank([P, PACK, P], h_numbers[n])
-                    for i in range(PACK):
-                        nc.tensor.matmul(h_banks[n][:, i, :], prod[b // 2][:, b % 2, i, :], ident[:],
-                                         start=(i == 0), stop=False, is_transpose=True)
-                    d = small([P, PACK, P], F32, "d", (4 + n) % 6 + 2 * (n // 2))
-                    nc.scalar.copy(d[:], by_slot(d_banks[n]))
-                    for i in range(PACK):
-                        nc.tensor.matmul(h_banks[n][:, i, :], d[:, i, :], ident[:],
-                                         start=False, stop=(i == PACK - 1), is_transpose=True)
-                for n in (first, first + 1):
-                    nc.scalar.copy(h[s][:, :, n * P : (n + 1) * P], h_banks[n][:])
-
-        def amend(i, lo, hi):
-            s, off = divmod(lo, BANK)
-            nc.vector.tensor_tensor(
-                page[i][:].indirect(entries(idx3, lo, hi)),
-                h[s][:, i, off : off + hi - lo], weight[i, lo], MULT,
+        idx = load_list(offs, "idx")
+        tab = [keep.tile([P, T], U32, name=f"tab{a}", align_bytes=64) for a in range(PASSES)]
+        load_words(tab[0][:], tab_words[0])
+        for q in range(QUADRANTS):
+            nc.sync.dma_start(
+                tab_scale_rows[32 * q : 32 * q + PASSES * SCALE_ROWS].bitcast(I32),
+                tab_scales[:, SCALE_ROWS * q : SCALE_ROWS * (q + 1), :].bitcast(I32),
             )
+        w3_codes = keep.tile([P, PASSES, H], U32, name="w3_codes", align_bytes=64)
+        nc.sync.dma_start(w3_codes[:].bitcast(I32), w3_words.rearrange("a p c i -> p a (c i)").bitcast(I32))
+        load_scale_rows(w3_scale_rows, w3_scales)
+        load_words(tab[1][:], tab_words[1])
+        w2_codes = keep.tile([P, PASSES, 2 * H], U8, name="w2_codes", align_bytes=64)
+        nc.sync.dma_start(w2_codes[:].bitcast(I32), w2_words.rearrange("a p c -> p a c").bitcast(I32))
+        load_scale_rows(w2_scale_rows, w2_scales)
+        w1_raw = [load_pass(0, w1[:K_PASS, :], "w1_raw0")]
 
-        for b in range(S // P):
-            f2_times_f3(b, small([P, PACK, P], F32, "f3", b % 4)[:])
-        w1_ops = [quantize_weight(w1_raw[a], f"w1_{a}", nc.vector.tensor_copy) for a in range(PASSES)]
-        w4_ops = [quantize_weight(w4_raw[a], f"w4_{a}", nc.scalar.copy) for a in range(PASSES)]
-        load_briefs(1)
-        for i in range(2, PACK):
-            load_weight(0, BANK, range(i, i + 1))
+        v_words = [keep.tile([P, S], U32, name=f"v_words{a}", align_bytes=64) for a in range(PASSES)]
+        v_scales = keep.tile([P, S], U8, name="v_scales", align_bytes=64)
+        nc.vector.tensor_copy(v_words[0][:], tab[0][:].indirect(idx[:]))
+        nc.vector.tensor_copy(v_scales[:], tab_scale_rows[:].indirect(idx[:]))
+        for q in range(QUADRANTS):
+            nc.sync.dma_start(
+                v_scales_raised[32 * q : 32 * q + SCALE_ROWS].bitcast(I32),
+                v_scales[32 * q + SCALE_ROWS : 32 * q + 2 * SCALE_ROWS].bitcast(I32),
+            )
+        for lo in (0, HALF):
+            nc.vector.tensor_copy(v_words[1][:, lo : lo + HALF], tab[1][:].indirect(entries(idx, lo, lo + HALF)))
+
+        w1_raw.append(load_pass(1, w1[K_PASS:, :], "w1_raw1"))
+        w4_raw = [load_pass(2 + a, w4[a * K_PASS : (a + 1) * K_PASS, :], f"w4_raw{a}") for a in range(PASSES)]
+
+        def load_briefs(half, first_buffer):
+            cols = slice(half * HALF, (half + 1) * HALF)
+            return [
+                load_pass(first_buffer + a, briefs[a * K_PASS : (a + 1) * K_PASS, cols], f"briefs_raw{half}{a}")
+                for a in range(PASSES)
+            ]
+
+        weight, page = {}, {}
+
+        def load_weight(lo, hi, slots):
+            rows = keep.tile([P, len(slots), hi - lo], F32, name=f"weight{lo}_{slots[0]}")
+            src = wgs.rearrange("(p i) j -> p i j", i=SLOTS)[:, slots[0] : slots[-1] + 1, lo:hi]
+            for q in (0, 2, 1, 3):
+                nc.sync.dma_start(rows[32 * q : 32 * (q + 1)], src)
+            for n, i in enumerate(slots):
+                weight[i, lo] = rows[:, n, :]
+
+        def load_page(i):
+            page[i] = keep.tile([P, T2], F32, name=f"page{i}")
+            nc.sync.dma_start(page[i][:], page0.rearrange("(p i) t -> p i t", i=SLOTS)[:, i, :])
+
+        briefs_raw = [load_briefs(0, 4)]
+        idx3 = load_list(offs3, "idx3")
+        room_col = keep.tile([P, GROUPS], F32, name="room_col")
+        with nc.allow_non_contiguous_dma(reason="one value of room for each partition and group"):
+            nc.sync.dma_start(room_col[:], room.rearrange("(g p) -> p g", p=P))
+        load_weight(0, QUARTER, range(2))
+        load_page(0)
+        load_page(1)
+        load_weight(QUARTER, HALF, range(2))
+
+        w2_ops = [(w2_codes[:, a, :].bitcast(FP4X4), w2_scale_rows[:, a, :]) for a in range(PASSES)]
+        w3_ops = [(w3_codes[:, a, :].bitcast(FP8X4), w3_scale_rows[:, a, :]) for a in range(PASSES)]
+        product = {}
+
+        def table_sum(b, w_ops, second_scales, bank_number, pass_order=(0, 1)):
+            cols = slice(b * P, (b + 1) * P)
+            scales = (v_scales[:, cols], second_scales[:, cols])
+            v_ops = [(v_words[a][:, cols].bitcast(FP8X4), scales[a]) for a in range(PASSES)]
+            acc = bank(bank_number, [P, H])
+            mx_sum(acc, v_ops, w_ops, pass_order)
+            return by_slot(acc)
+
+        def f2_times_f3(b):
+            first, swap = 2 * (b % HALF_BLOCKS), b // HALF_BLOCKS
+            f3 = buffer2(b % HALF_BLOCKS, [P, SLOTS, P], "f3")
+            nc.scalar.copy(f3[:], table_sum(b, w3_ops, v_scales[SCALE_ROWS:P], first + swap))
+            if b % 2 == 0:
+                product[b // 2] = reuse.tile([P, 2, SLOTS, P], F32, name="product", tag="product", bufs=BLOCKS // 2)
+            f2 = table_sum(b, w2_ops, v_scales_raised, first + 1 - swap, (1, 0))
+            nc.vector.tensor_tensor(product[b // 2][:, b % 2], f2, f3[:], MULT)
+
+        def quantize_weight(raw, name, interleave):
+            words, scales = moving_operand(name)
+            staged = staging()
+            interleave(raw, staged)
+            quantize(staged, words, scales)
+            return words[:].bitcast(FP8X4), scales[:]
+
+        for b in range(BLOCKS):
+            f2_times_f3(b)
+        w1_ops = [quantize_weight(w1_raw[a], f"w1_{a}", interleave_on_vector) for a in range(PASSES)]
+        w4_ops = [quantize_weight(w4_raw[a], f"w4_{a}", interleave_on_scalar) for a in range(PASSES)]
+
+        briefs_raw.append(load_briefs(1, 2))
+        for i in range(2, SLOTS):
+            load_weight(0, HALF, range(i, i + 1))
             load_page(i)
-        load_weight(BANK, S, range(2))
+        load_weight(HALF, S, range(2))
         idx2 = load_list(offs2, "idx2")
         tab2 = keep.tile([P, T3], U32, name="tab2", align_bytes=64)
         load_words(tab2[:], tab2_words[0])
-        load_weight(BANK, S, range(2, PACK))
-        load_scale_rows(nc.sync, tab2_plane, tab2_scales)
+        load_weight(HALF, S, range(2, SLOTS))
+        load_scale_rows(tab2_scale_rows, tab2_scales)
         idx4 = load_list(offs4, "idx4")
-        room_col = keep.tile([P, GROUPS], F32)
-        with nc.allow_non_contiguous_dma(reason="one value of room for each partition and group"):
-            nc.sync.dma_start(room_col[:], room.rearrange("(g p) -> p g", p=P))
 
-        times_f1(0, prod[0])
-        quantize_briefs(0, 0, nc.vector.tensor_copy, late([P, BANK, PACK], BF16, "grouped00", 0))
-        quantize_briefs(0, 1, nc.scalar.copy, late([P, BANK, PACK], BF16, "grouped01", 1))
-        times_f1(1, big([P, 2, PACK, P], "triple1", 5))
-        times_f1(2, late([P, 2, PACK, P], F32, "triple2", 1))
-        times_f1(3, late([P, 2, PACK, P], F32, "triple3", 0))
+        def times_f1(pair, triple):
+            for n in range(2):
+                b = 2 * pair + n
+                f1 = table_sum(b, w1_ops, v_scales[SCALE_ROWS:P], b)
+                nc.vector.tensor_tensor(triple[:, n], f1, product[pair][:, n], MULT)
+            product[pair] = triple
+
+        briefs_ops = {}
+
+        def quantize_briefs(half, a, interleave, staged):
+            interleave(briefs_raw[half][a], staged)
+            words = keep.tile([P, HALF], U32, name=f"briefs_words{half}{a}", align_bytes=64)
+            scales = keep.tile([P, HALF], U8, name=f"briefs_scales{half}{a}", align_bytes=64)
+            quantize(staged, words, scales)
+            briefs_ops[half, a] = words, scales
+
+        h = {}
+        d_buffers = (4, 5, 2, 3)
+
+        def features(half, d_banks, h_banks):
+            h[half] = buffer8(half, [P, SLOTS, HALF], f"h{half}")
+            for first in range(0, HALF_BLOCKS, 2):
+                d_acc, h_acc = {}, {}
+                for n in (first, first + 1):
+                    cols = slice(n * P, (n + 1) * P)
+                    ops = [briefs_ops[half, a] for a in range(PASSES)]
+                    d_acc[n] = bank(d_banks[n], [P, H])
+                    mx_sum(d_acc[n], [(words[:, cols].bitcast(FP8X4), scales[:, cols]) for words, scales in ops], w4_ops)
+                for n in (first, first + 1):
+                    b = half * HALF_BLOCKS + n
+                    h_acc[n] = bank(h_banks[n], [P, SLOTS, P])
+                    for i in range(SLOTS):
+                        nc.tensor.matmul(h_acc[n][:, i, :], product[b // 2][:, b % 2, i, :], ident[:],
+                                         start=(i == 0), stop=False, is_transpose=True)
+                    d = buffer2(d_buffers[n], [P, SLOTS, P], "d")
+                    nc.scalar.copy(d[:], by_slot(d_acc[n]))
+                    for i in range(SLOTS):
+                        nc.tensor.matmul(h_acc[n][:, i, :], d[:, i, :], ident[:],
+                                         start=False, stop=(i == SLOTS - 1), is_transpose=True)
+                for n in (first, first + 1):
+                    nc.scalar.copy(h[half][:, :, n * P : (n + 1) * P], h_acc[n][:])
+
+        times_f1(0, product[0])
+        quantize_briefs(0, 0, interleave_on_vector, buffer4(4, [P, HALF, SLOTS], BF16, "briefs_staged0"))
+        quantize_briefs(0, 1, interleave_on_scalar, buffer4(5, [P, HALF, SLOTS], BF16, "briefs_staged1"))
+        times_f1(1, buffer8(5, [P, 2, SLOTS, P], "triple1"))
+        times_f1(2, buffer4(5, [P, 2, SLOTS, P], F32, "triple2"))
+        times_f1(3, buffer4(4, [P, 2, SLOTS, P], F32, "triple3"))
+
+        root = keep.tile([P, GROUPS], F32, name="root")
+        unit = keep.tile([P, GROUPS], F32, name="unit")
+        unit_room = keep.tile([P, GROUPS], F32, name="unit_room")
+        nc.scalar.activation(root[:], room_col[:], ACT.Abs_reciprocal_sqrt)
+        nc.gpsimd.tensor_tensor(unit[:], root[:], root[:], MULT)
+        nc.gpsimd.tensor_tensor(unit_room[:], unit[:], room_col[:], MULT)
+
         features(0, (0, 1, 0, 1), (2, 3, 2, 3))
         for a in range(PASSES):
-            quantize_briefs(1, a, nc.scalar.copy, staging())
+            quantize_briefs(1, a, interleave_on_scalar, staging())
         features(1, (6, 7, 0, 1), (2, 3, 4, 5))
-        for lo in (0, BANK // 2):
-            for i in range(2):
-                amend(i, lo, lo + BANK // 2)
-        for i in range(2, PACK):
-            amend(i, 0, BANK)
 
-        v2_codes = keep.tile([P, S2], U32, align_bytes=64)
-        v2_scales = keep.tile([P, S2], U8, align_bytes=64)
-        nc.vector.tensor_copy(v2_codes[:], tab2[:].indirect(idx2[:]))
-        pairs = [mid([P, 2, BANK, 2], BF16, f"pairs{c}", c) for c in range(CHUNKS)]
-        for i in range(PACK):
-            amend(i, BANK, S)
+        def amend(i, lo, hi):
+            half, at = divmod(lo, HALF)
+            nc.vector.tensor_tensor(
+                page[i][:].indirect(entries(idx3, lo, hi)), h[half][:, i, at : at + hi - lo], weight[i, lo], MULT
+            )
+
+        for lo in (0, QUARTER):
+            for i in range(2):
+                amend(i, lo, lo + QUARTER)
+        for i in range(2, SLOTS):
+            amend(i, 0, HALF)
+
+        v2_words = keep.tile([P, S2], U32, name="v2_words", align_bytes=64)
+        v2_scales = keep.tile([P, S2], U8, name="v2_scales", align_bytes=64)
+        nc.vector.tensor_copy(v2_words[:], tab2[:].indirect(idx2[:]))
+        pairs = [buffer4(c, [P, 2, BANK, 2], BF16, f"pairs{c}") for c in range(CHUNKS)]
+        for i in range(SLOTS):
+            amend(i, HALF, S)
             for c in range(CHUNKS):
                 nc.scalar.copy(pairs[c][:, i // 2, :, i % 2], page[i][:, c * BANK : (c + 1) * BANK])
-        nc.vector.tensor_copy(v2_scales[:], tab2_plane[:, 0, :].indirect(idx2[:]))
+        nc.vector.tensor_copy(v2_scales[:], tab2_scale_rows[:, 0, :].indirect(idx2[:]))
 
-        page_grouped, page_q = [], []
-        for c in range(CHUNKS + 1):
-            if c < CHUNKS:
-                page_grouped.append(staging())
+        page_staged, page_ops = [], []
+        for step in range(CHUNKS + 1):
+            if step < CHUNKS:
+                page_staged.append(staging())
                 nc.vector.tensor_copy(
-                    page_grouped[c][:].rearrange("p c i -> p (c i)").bitcast(F32).rearrange("p (c n u) -> p c u n", n=4, u=2),
-                    pairs[c][:].rearrange("p u c e -> p u (c e)").bitcast(F32).rearrange("p u (c n) -> p c u n", n=4),
+                    page_staged[step][:].rearrange("p c i -> p (c i)").bitcast(F32).rearrange("p (c u) -> p c u", u=2),
+                    pairs[step][:].rearrange("p u c n -> p u (c n)").bitcast(F32).rearrange("p u c -> p c u"),
                 )
-            if c > 0:
-                page_q.append(wide_codes(f"page_{c - 1}"))
-                quantize(page_grouped[c - 1], page_q[c - 1][0][:], page_q[c - 1][1][:])
+            if step > 0:
+                page_ops.append(moving_operand(f"page_{step - 1}"))
+                quantize(page_staged[step - 1], *page_ops[step - 1])
 
-        e = {}
+        e, x, inverse = {}, {}, {}
 
         def scores(g):
             rows = slice(g * P, (g + 1) * P)
-            e[g] = big([P, T2], f"e{g}", 2 + min(g, 2))
+            last = g == GROUPS - 1
+            e[g] = buffer8(2 + g - last, [P, T2], f"e{g}")
             for c in range(CHUNKS):
-                e_bank = fresh_bank([P, BANK])
+                acc = bank((g * CHUNKS + c) % BANKS, [P, BANK])
                 nc.tensor.matmul_mx(
-                    out=e_bank[:], lhsT=v2_codes[:, rows].bitcast(FP8X4), lhsT_scale=v2_scales[:, rows],
-                    rhs=page_q[c][0][:].bitcast(FP8X4), rhs_scale=page_q[c][1][:], start=True, stop=True,
+                    out=acc[:], lhsT=v2_words[:, rows].bitcast(FP8X4), lhsT_scale=v2_scales[:, rows],
+                    rhs=page_ops[c][0][:].bitcast(FP8X4), rhs_scale=page_ops[c][1][:], start=True, stop=True,
                 )
-                copy = nc.vector.tensor_copy if (g, c) in VECTOR_EVAC else nc.scalar.copy
-                copy(e[g][:, c * BANK : (c + 1) * BANK], e_bank[:])
+                on_vector = last or (g == 0 and c >= CHUNKS // 2)
+                copy = nc.vector.tensor_copy if on_vector else nc.scalar.copy
+                copy(e[g][:, c * BANK : (c + 1) * BANK], acc[:])
 
-        x, inv = {}, {}
+        def pick(g):
+            for half in range(2):
+                piece = 2 * g + half
+                x[piece] = buffer2(piece, [P, HALF], "x")
+                nc.vector.tensor_copy(x[piece][:], e[g][:].indirect(entries(idx4, half * HALF, (half + 1) * HALF)))
 
-        def pick(u):
-            g, s = divmod(u, HALVES)
-            x[u] = small([P, BANK], F32, "x", u)
-            nc.vector.tensor_copy(x[u][:], e[g][:].indirect(entries(idx4, s * BANK, (s + 1) * BANK)))
+        def magnitude(piece):
+            g = piece // 2
+            if piece % 2 == 0:
+                both = reuse.tile([P, 2, HALF], F32, name="inverse", tag="product", bufs=BLOCKS // 2)
+                inverse[piece], inverse[piece + 1] = both[:, 0, :], both[:, 1, :]
+            nc.scalar.activation(inverse[piece], x[piece][:], ACT.Abs, scale=unit[:, g : g + 1])
 
-        def magnitude(u):
-            if u % HALVES == 0:
-                both = ring.tile([P, HALVES, BANK], F32, name="inv", tag="prod", bufs=4)
-                inv[u], inv[u + 1] = both[:, 0, :], both[:, 1, :]
-            nc.scalar.activation(inv[u], x[u][:], ACT.Abs)
+        def inverse_root(piece):
+            g = piece // 2
+            nc.scalar.activation(inverse[piece], inverse[piece], ACT.Abs_reciprocal_sqrt, bias=unit_room[:, g : g + 1])
 
-        def inverse_root(u):
-            g = u // HALVES
-            nc.scalar.activation(inv[u], inv[u], ACT.Abs_reciprocal_sqrt, bias=room_col[:, g : g + 1])
+        def finish(piece):
+            g, half = divmod(piece, 2)
+            nc.scalar.activation(inverse[piece], inverse[piece], ACT.Square, scale=root[:, g : g + 1])
+            nc.vector.tensor_tensor(x[piece][:], x[piece][:], inverse[piece], MULT)
+            nc.sync.dma_start(out[g * P : (g + 1) * P, half * HALF : (half + 1) * HALF], x[piece][:])
 
-        def finish(u):
-            g, s = divmod(u, HALVES)
-            nc.scalar.activation(inv[u], inv[u], ACT.Square)
-            nc.vector.tensor_tensor(x[u][:], x[u][:], inv[u], MULT)
-            nc.sync.dma_start(out[g * P : (g + 1) * P, s * BANK : (s + 1) * BANK], x[u][:])
-
-        units = GROUPS * HALVES
         scores(0)
         pick(0)
-        pick(1)
         scores(1)
         scores(2)
+        pick(1)
         pick(2)
-        pick(3)
-        pick(4)
-        pick(5)
         scores(3)
-        pick(6)
-        pick(7)
-        for step in range(units + 2):
-            if step < units:
+        pick(3)
+        for step in range(PIECES + 2):
+            if step < PIECES:
                 magnitude(step)
-            if 1 <= step <= units:
+            if 1 <= step <= PIECES:
                 inverse_root(step - 1)
             if step >= 2:
                 finish(step - 2)

@@ -82,9 +82,9 @@ def tile_list_translator_brief_scores_kernel(
         def load_words(words, src):
             nc.sync.dma_start(words.bitcast(I32), src.rearrange("p t i -> p (t i)").bitcast(I32))
 
-        def load_scale_rows(scales, src):
+        def load_scale_rows(queue, scales, src):
             for q in range(QUADRANTS):
-                nc.sync.dma_start(
+                queue.dma_start(
                     scales[32 * q : 32 * q + SCALE_ROWS].bitcast(I32),
                     src[:, SCALE_ROWS * q : SCALE_ROWS * (q + 1), :].rearrange("a r c -> r a c").bitcast(I32),
                 )
@@ -123,6 +123,7 @@ def tile_list_translator_brief_scores_kernel(
         w2_scale_rows = zeroed_scales([P, PASSES, H], "w2_scale_rows")
         tab2_scale_rows = zeroed_scales([P, 1, T3], "tab2_scale_rows")
         v_scales_raised = zeroed_scales([P, S], "v_scales_raised")
+        load_scale_rows(nc.gpsimd, w2_scale_rows, w2_scales)
         ident = keep.tile([P, P], F32, name="ident")
         make_identity(nc, ident[:])
 
@@ -136,11 +137,10 @@ def tile_list_translator_brief_scores_kernel(
             )
         w3_codes = keep.tile([P, PASSES, H], U32, name="w3_codes", align_bytes=64)
         nc.sync.dma_start(w3_codes[:].bitcast(I32), w3_words.rearrange("a p c i -> p a (c i)").bitcast(I32))
-        load_scale_rows(w3_scale_rows, w3_scales)
+        load_scale_rows(nc.sync, w3_scale_rows, w3_scales)
         load_words(tab[1][:], tab_words[1])
         w2_codes = keep.tile([P, PASSES, 2 * H], U8, name="w2_codes", align_bytes=64)
         nc.sync.dma_start(w2_codes[:].bitcast(I32), w2_words.rearrange("a p c -> p a c").bitcast(I32))
-        load_scale_rows(w2_scale_rows, w2_scales)
         w1_raw = [load_pass(0, w1[:K_PASS, :], "w1_raw0")]
 
         v_words = [keep.tile([P, S], U32, name=f"v_words{a}", align_bytes=64) for a in range(PASSES)]
@@ -231,7 +231,7 @@ def tile_list_translator_brief_scores_kernel(
         tab2 = keep.tile([P, T3], U32, name="tab2", align_bytes=64)
         load_words(tab2[:], tab2_words[0])
         load_weight(HALF, S, range(2, SLOTS))
-        load_scale_rows(tab2_scale_rows, tab2_scales)
+        load_scale_rows(nc.sync, tab2_scale_rows, tab2_scales)
         idx4 = load_list(offs4, "idx4")
 
         def times_f1(pair, triple):
@@ -321,7 +321,8 @@ def tile_list_translator_brief_scores_kernel(
         for step in range(CHUNKS + 1):
             if step < CHUNKS:
                 page_staged.append(staging())
-                nc.vector.tensor_copy(
+                copy = nc.scalar.copy if step == CHUNKS - 1 else nc.vector.tensor_copy
+                copy(
                     page_staged[step][:].rearrange("p c i -> p (c i)").bitcast(F32).rearrange("p (c u) -> p c u", u=2),
                     pairs[step][:].rearrange("p u c n -> p u (c n)").bitcast(F32).rearrange("p u c -> p c u"),
                 )
@@ -346,17 +347,17 @@ def tile_list_translator_brief_scores_kernel(
                 copy(e[g][:, c * BANK : (c + 1) * BANK], acc[:])
 
         def pick(g):
-            for half in range(2):
-                piece = 2 * g + half
-                x[piece] = buffer2(piece, [P, HALF], "x")
-                nc.vector.tensor_copy(x[piece][:], e[g][:].indirect(entries(idx4, half * HALF, (half + 1) * HALF)))
+            x[g] = buffer4(g, [P, S], F32, "x")
+            for lo in (0, HALF):
+                nc.vector.tensor_copy(x[g][:, lo : lo + HALF], e[g][:].indirect(entries(idx4, lo, lo + HALF)))
 
         def magnitude(piece):
-            g = piece // 2
-            if piece % 2 == 0:
+            g, half = divmod(piece, 2)
+            if half == 0:
                 both = reuse.tile([P, 2, HALF], F32, name="inverse", tag="product", bufs=BLOCKS // 2)
                 inverse[piece], inverse[piece + 1] = both[:, 0, :], both[:, 1, :]
-            nc.scalar.activation(inverse[piece], x[piece][:], ACT.Abs, scale=unit[:, g : g + 1])
+            cols = slice(half * HALF, (half + 1) * HALF)
+            nc.scalar.activation(inverse[piece], x[g][:, cols], ACT.Abs, scale=unit[:, g : g + 1])
 
         def inverse_root(piece):
             g = piece // 2
@@ -364,9 +365,13 @@ def tile_list_translator_brief_scores_kernel(
 
         def finish(piece):
             g, half = divmod(piece, 2)
+            rows, cols = slice(g * P, (g + 1) * P), slice(half * HALF, (half + 1) * HALF)
             nc.scalar.activation(inverse[piece], inverse[piece], ACT.Square, scale=root[:, g : g + 1])
-            nc.vector.tensor_tensor(x[piece][:], x[piece][:], inverse[piece], MULT)
-            nc.sync.dma_start(out[g * P : (g + 1) * P, half * HALF : (half + 1) * HALF], x[piece][:])
+            nc.vector.tensor_tensor(x[g][:, cols], x[g][:, cols], inverse[piece], MULT)
+            if g == GROUPS - 1:
+                nc.sync.dma_start(out[rows, cols], x[g][:, cols])
+            elif half == 1:
+                nc.sync.dma_start(out[rows, :], x[g][:])
 
         scores(0)
         pick(0)

@@ -32,7 +32,16 @@ BLOCKS = S // P
 HALF_BLOCKS = HALF // P
 CHUNKS = T2 // BANK
 GROUPS = S2 // P
-PIECES = 2 * GROUPS
+F3_BANKS = (0, 2, 4, 6, 0, 2, 4, 6)
+F2_BANKS = (1, 3, 5, 7, 1, 3, 5, 7)
+F1_BANKS = (4, 5, 6, 7, 0, 1, 2, 3)
+F3_BUFFERS = (0, 1, 2, 3, 0, 1, 2, 3)
+E_BUFFERS = (2, 3, 4, 5)
+SCALAR_WEAVES = True
+VECTOR_EMPTIES = ((0, 2), (0, 3), (1, 3), (2, 3), (3, 1), (3, 2), (3, 3))
+PICKS = [(g, lo, lo + HALF) for g in range(GROUPS) for lo in (0, HALF)]
+PIECES = [(g, lo, lo + HALF) for g in range(GROUPS) for lo in (0, HALF)]
+ON_GPSIMD = ()
 LINE = 4
 
 
@@ -52,8 +61,8 @@ def tile_list_translator_brief_scores_kernel(
         def buffer4(number, shape, dtype, name):
             return reuse.tile(shape, dtype, name=name, tag=f"buffer4_{number}", align_bytes=64)
 
-        def buffer2(number, shape, name):
-            return reuse.tile(shape, F32, name=name, tag=f"buffer2_{number}", align_bytes=64)
+        def buffer2(number, shape, name, dtype=F32):
+            return reuse.tile(shape, dtype, name=name, tag=f"buffer2_{number}", align_bytes=64)
 
         def bank(number, shape):
             return psum.tile(shape, F32, name=f"bank{number}", tag=f"bank{number}")
@@ -82,8 +91,8 @@ def tile_list_translator_brief_scores_kernel(
         def load_words(words, src):
             nc.sync.dma_start(words.bitcast(I32), src.rearrange("p t i -> p (t i)").bitcast(I32))
 
-        def load_scale_rows(queue, scales, src):
-            for q in range(QUADRANTS):
+        def load_scale_rows(queue, scales, src, quadrants=range(QUADRANTS)):
+            for q in quadrants:
                 queue.dma_start(
                     scales[32 * q : 32 * q + SCALE_ROWS].bitcast(I32),
                     src[:, SCALE_ROWS * q : SCALE_ROWS * (q + 1), :].rearrange("a r c -> r a c").bitcast(I32),
@@ -96,23 +105,23 @@ def tile_list_translator_brief_scores_kernel(
 
         def interleave_on_scalar(raw, staged):
             nc.scalar.copy(
-                staged[:].rearrange("p (c n) i -> p c i n", n=LINE),
-                raw[:].rearrange("p i (c n) -> p c i n", n=LINE),
+                staged.rearrange("p (c n) i -> p c i n", n=LINE),
+                raw.rearrange("p i (c n) -> p c i n", n=LINE),
             )
 
         def interleave_on_vector(raw, staged):
-            nc.vector.tensor_copy(staged[:], raw[:].rearrange("p i c -> p c i"))
+            nc.vector.tensor_copy(staged, raw.rearrange("p i c -> p c i"))
 
         def quantize(staged, words, scales):
             nc.vector.quantize_mx(
-                out=words[:].bitcast(FP8X4), scales=scales[:], in_=staged[:].rearrange("p c i -> p (c i)")
+                out=words[:].bitcast(FP8X4), scales=scales[:], in_=staged.rearrange("p c i -> p (c i)")
             )
 
-        def mx_sum(acc, lhs, rhs, pass_order=(0, 1)):
-            for n, a in enumerate(pass_order):
+        def mx_sum(acc, lhs, rhs):
+            for a in range(PASSES):
                 nc.tensor.matmul_mx(
                     out=acc[:], lhsT=lhs[a][0], lhsT_scale=lhs[a][1], rhs=rhs[a][0], rhs_scale=rhs[a][1],
-                    start=(n == 0), stop=(n == PASSES - 1),
+                    start=(a == 0), stop=(a == PASSES - 1),
                 )
 
         def by_slot(acc):
@@ -123,165 +132,13 @@ def tile_list_translator_brief_scores_kernel(
         w2_scale_rows = zeroed_scales([P, PASSES, H], "w2_scale_rows")
         tab2_scale_rows = zeroed_scales([P, 1, T3], "tab2_scale_rows")
         v_scales_raised = zeroed_scales([P, S], "v_scales_raised")
+
+        room_col = keep.tile([P, GROUPS], F32, name="room_col")
+        with nc.allow_non_contiguous_dma(reason="one value of room for each partition and group"):
+            nc.gpsimd.dma_start(room_col[:], room.rearrange("(g p) -> p g", p=P))
         load_scale_rows(nc.gpsimd, w2_scale_rows, w2_scales)
         ident = keep.tile([P, P], F32, name="ident")
         make_identity(nc, ident[:])
-
-        idx = load_list(offs, "idx")
-        tab = [keep.tile([P, T], U32, name=f"tab{a}", align_bytes=64) for a in range(PASSES)]
-        load_words(tab[0][:], tab_words[0])
-        for q in range(QUADRANTS):
-            nc.sync.dma_start(
-                tab_scale_rows[32 * q : 32 * q + PASSES * SCALE_ROWS].bitcast(I32),
-                tab_scales[:, SCALE_ROWS * q : SCALE_ROWS * (q + 1), :].bitcast(I32),
-            )
-        w3_codes = keep.tile([P, PASSES, H], U32, name="w3_codes", align_bytes=64)
-        nc.sync.dma_start(w3_codes[:].bitcast(I32), w3_words.rearrange("a p c i -> p a (c i)").bitcast(I32))
-        load_scale_rows(nc.sync, w3_scale_rows, w3_scales)
-        load_words(tab[1][:], tab_words[1])
-        w2_codes = keep.tile([P, PASSES, 2 * H], U8, name="w2_codes", align_bytes=64)
-        nc.sync.dma_start(w2_codes[:].bitcast(I32), w2_words.rearrange("a p c -> p a c").bitcast(I32))
-        w1_raw = [load_pass(0, w1[:K_PASS, :], "w1_raw0")]
-
-        v_words = [keep.tile([P, S], U32, name=f"v_words{a}", align_bytes=64) for a in range(PASSES)]
-        v_scales = keep.tile([P, S], U8, name="v_scales", align_bytes=64)
-        nc.vector.tensor_copy(v_words[0][:], tab[0][:].indirect(idx[:]))
-        nc.vector.tensor_copy(v_scales[:], tab_scale_rows[:].indirect(idx[:]))
-        for q in range(QUADRANTS):
-            nc.sync.dma_start(
-                v_scales_raised[32 * q : 32 * q + SCALE_ROWS].bitcast(I32),
-                v_scales[32 * q + SCALE_ROWS : 32 * q + 2 * SCALE_ROWS].bitcast(I32),
-            )
-        for lo in (0, HALF):
-            nc.vector.tensor_copy(v_words[1][:, lo : lo + HALF], tab[1][:].indirect(entries(idx, lo, lo + HALF)))
-
-        w1_raw.append(load_pass(1, w1[K_PASS:, :], "w1_raw1"))
-        w4_raw = [load_pass(2 + a, w4[a * K_PASS : (a + 1) * K_PASS, :], f"w4_raw{a}") for a in range(PASSES)]
-
-        def load_briefs(half, first_buffer):
-            cols = slice(half * HALF, (half + 1) * HALF)
-            return [
-                load_pass(first_buffer + a, briefs[a * K_PASS : (a + 1) * K_PASS, cols], f"briefs_raw{half}{a}")
-                for a in range(PASSES)
-            ]
-
-        weight, page = {}, {}
-
-        def load_weight(lo, hi, slots):
-            rows = keep.tile([P, len(slots), hi - lo], F32, name=f"weight{lo}_{slots[0]}")
-            src = wgs.rearrange("(p i) j -> p i j", i=SLOTS)[:, slots[0] : slots[-1] + 1, lo:hi]
-            for q in (0, 2, 1, 3):
-                nc.sync.dma_start(rows[32 * q : 32 * (q + 1)], src)
-            for n, i in enumerate(slots):
-                weight[i, lo] = rows[:, n, :]
-
-        def load_page(i):
-            page[i] = keep.tile([P, T2], F32, name=f"page{i}")
-            nc.sync.dma_start(page[i][:], page0.rearrange("(p i) t -> p i t", i=SLOTS)[:, i, :])
-
-        briefs_raw = [load_briefs(0, 4)]
-        idx3 = load_list(offs3, "idx3")
-        room_col = keep.tile([P, GROUPS], F32, name="room_col")
-        with nc.allow_non_contiguous_dma(reason="one value of room for each partition and group"):
-            nc.sync.dma_start(room_col[:], room.rearrange("(g p) -> p g", p=P))
-        load_weight(0, QUARTER, range(2))
-        load_page(0)
-        load_page(1)
-        load_weight(QUARTER, HALF, range(2))
-
-        w2_ops = [(w2_codes[:, a, :].bitcast(FP4X4), w2_scale_rows[:, a, :]) for a in range(PASSES)]
-        w3_ops = [(w3_codes[:, a, :].bitcast(FP8X4), w3_scale_rows[:, a, :]) for a in range(PASSES)]
-        product = {}
-
-        def table_sum(b, w_ops, second_scales, bank_number, pass_order=(0, 1)):
-            cols = slice(b * P, (b + 1) * P)
-            scales = (v_scales[:, cols], second_scales[:, cols])
-            v_ops = [(v_words[a][:, cols].bitcast(FP8X4), scales[a]) for a in range(PASSES)]
-            acc = bank(bank_number, [P, H])
-            mx_sum(acc, v_ops, w_ops, pass_order)
-            return by_slot(acc)
-
-        def f2_times_f3(b):
-            first, swap = 2 * (b % HALF_BLOCKS), b // HALF_BLOCKS
-            f3 = buffer2(b % HALF_BLOCKS, [P, SLOTS, P], "f3")
-            nc.scalar.copy(f3[:], table_sum(b, w3_ops, v_scales[SCALE_ROWS:P], first + swap))
-            if b % 2 == 0:
-                product[b // 2] = reuse.tile([P, 2, SLOTS, P], F32, name="product", tag="product", bufs=BLOCKS // 2)
-            f2 = table_sum(b, w2_ops, v_scales_raised, first + 1 - swap, (1, 0))
-            nc.vector.tensor_tensor(product[b // 2][:, b % 2], f2, f3[:], MULT)
-
-        def quantize_weight(raw, name, interleave):
-            words, scales = moving_operand(name)
-            staged = staging()
-            interleave(raw, staged)
-            quantize(staged, words, scales)
-            return words[:].bitcast(FP8X4), scales[:]
-
-        for b in range(BLOCKS):
-            f2_times_f3(b)
-        w1_ops = [quantize_weight(w1_raw[a], f"w1_{a}", interleave_on_vector) for a in range(PASSES)]
-        w4_ops = [quantize_weight(w4_raw[a], f"w4_{a}", interleave_on_scalar) for a in range(PASSES)]
-
-        briefs_raw.append(load_briefs(1, 2))
-        for i in range(2, SLOTS):
-            load_weight(0, HALF, range(i, i + 1))
-            load_page(i)
-        load_weight(HALF, S, range(2))
-        idx2 = load_list(offs2, "idx2")
-        tab2 = keep.tile([P, T3], U32, name="tab2", align_bytes=64)
-        load_words(tab2[:], tab2_words[0])
-        load_weight(HALF, S, range(2, SLOTS))
-        load_scale_rows(nc.sync, tab2_scale_rows, tab2_scales)
-        idx4 = load_list(offs4, "idx4")
-
-        def times_f1(pair, triple):
-            for n in range(2):
-                b = 2 * pair + n
-                f1 = table_sum(b, w1_ops, v_scales[SCALE_ROWS:P], b)
-                nc.vector.tensor_tensor(triple[:, n], f1, product[pair][:, n], MULT)
-            product[pair] = triple
-
-        briefs_ops = {}
-
-        def quantize_briefs(half, a, interleave, staged):
-            interleave(briefs_raw[half][a], staged)
-            words = keep.tile([P, HALF], U32, name=f"briefs_words{half}{a}", align_bytes=64)
-            scales = keep.tile([P, HALF], U8, name=f"briefs_scales{half}{a}", align_bytes=64)
-            quantize(staged, words, scales)
-            briefs_ops[half, a] = words, scales
-
-        h = {}
-        d_buffers = (4, 5, 2, 3)
-
-        def features(half, d_banks, h_banks):
-            h[half] = buffer8(half, [P, SLOTS, HALF], f"h{half}")
-            for first in range(0, HALF_BLOCKS, 2):
-                d_acc, h_acc = {}, {}
-                for n in (first, first + 1):
-                    cols = slice(n * P, (n + 1) * P)
-                    ops = [briefs_ops[half, a] for a in range(PASSES)]
-                    d_acc[n] = bank(d_banks[n], [P, H])
-                    mx_sum(d_acc[n], [(words[:, cols].bitcast(FP8X4), scales[:, cols]) for words, scales in ops], w4_ops)
-                for n in (first, first + 1):
-                    b = half * HALF_BLOCKS + n
-                    h_acc[n] = bank(h_banks[n], [P, SLOTS, P])
-                    for i in range(SLOTS):
-                        nc.tensor.matmul(h_acc[n][:, i, :], product[b // 2][:, b % 2, i, :], ident[:],
-                                         start=(i == 0), stop=False, is_transpose=True)
-                    d = buffer2(d_buffers[n], [P, SLOTS, P], "d")
-                    nc.scalar.copy(d[:], by_slot(d_acc[n]))
-                    for i in range(SLOTS):
-                        nc.tensor.matmul(h_acc[n][:, i, :], d[:, i, :], ident[:],
-                                         start=False, stop=(i == SLOTS - 1), is_transpose=True)
-                for n in (first, first + 1):
-                    nc.scalar.copy(h[half][:, :, n * P : (n + 1) * P], h_acc[n][:])
-
-        times_f1(0, product[0])
-        quantize_briefs(0, 0, interleave_on_vector, buffer4(4, [P, HALF, SLOTS], BF16, "briefs_staged0"))
-        quantize_briefs(0, 1, interleave_on_scalar, buffer4(5, [P, HALF, SLOTS], BF16, "briefs_staged1"))
-        times_f1(1, buffer8(5, [P, 2, SLOTS, P], "triple1"))
-        times_f1(2, buffer4(5, [P, 2, SLOTS, P], F32, "triple2"))
-        times_f1(3, buffer4(4, [P, 2, SLOTS, P], F32, "triple3"))
 
         root = keep.tile([P, GROUPS], F32, name="root")
         unit = keep.tile([P, GROUPS], F32, name="unit")
@@ -290,88 +147,243 @@ def tile_list_translator_brief_scores_kernel(
         nc.gpsimd.tensor_tensor(unit[:], root[:], root[:], MULT)
         nc.gpsimd.tensor_tensor(unit_room[:], unit[:], room_col[:], MULT)
 
-        features(0, (0, 1, 0, 1), (2, 3, 2, 3))
-        for a in range(PASSES):
-            quantize_briefs(1, a, interleave_on_scalar, staging())
-        features(1, (6, 7, 0, 1), (2, 3, 4, 5))
+        tab = [reuse.tile([P, T], U32, name=f"tab{a}", tag=f"tab{a}", align_bytes=64) for a in range(PASSES)]
+        load_words(tab[0][:], tab_words[0])
+        idx = load_list(offs, "idx")
+        for q in range(QUADRANTS):
+            nc.sync.dma_start(
+                tab_scale_rows[32 * q : 32 * q + PASSES * SCALE_ROWS].bitcast(I32),
+                tab_scales[:, SCALE_ROWS * q : SCALE_ROWS * (q + 1), :].bitcast(I32),
+            )
+        load_words(tab[1][:], tab_words[1])
+        w3_codes = keep.tile([P, PASSES, H], U32, name="w3_codes", align_bytes=64)
+        nc.sync.dma_start(w3_codes[:].bitcast(I32), w3_words.rearrange("a p c i -> p a (c i)").bitcast(I32))
+        load_scale_rows(nc.sync, w3_scale_rows, w3_scales)
+        w1_raw = [load_pass(0, w1[:K_PASS, :], "w1_raw0")]
+
+        v_words = [keep.tile([P, S], U32, name=f"v_words{a}", align_bytes=64) for a in range(PASSES)]
+        v_scales = keep.tile([P, S], U8, name="v_scales", align_bytes=64)
+        nc.vector.tensor_copy(v_words[0][:], tab[0][:].indirect(idx[:]))
+        nc.vector.tensor_copy(v_scales[:], tab_scale_rows[:].indirect(idx[:]))
+        for lo in (0, HALF):
+            nc.vector.tensor_copy(v_words[1][:, lo : lo + HALF], tab[1][:].indirect(entries(idx, lo, lo + HALF)))
+
+        for q in range(QUADRANTS):
+            nc.sync.dma_start(
+                v_scales_raised[32 * q : 32 * q + SCALE_ROWS].bitcast(I32),
+                v_scales[32 * q + SCALE_ROWS : 32 * q + 2 * SCALE_ROWS].bitcast(I32),
+            )
+        w1_raw.append(load_pass(1, w1[K_PASS:, :], "w1_raw1"))
+        w2_codes = keep.tile([P, PASSES, 2 * H], U8, name="w2_codes", align_bytes=64)
+        nc.sync.dma_start(w2_codes[:].bitcast(I32), w2_words.rearrange("a p c -> p a c").bitcast(I32))
+
+        w4_raw = [load_pass(2 + a, w4[a * K_PASS : (a + 1) * K_PASS, :], f"w4_raw{a}") for a in range(PASSES)]
+        briefs_raw, weight, page = {}, {}, {}
+
+        def load_briefs(half):
+            for a in range(PASSES):
+                src = briefs[a * K_PASS : (a + 1) * K_PASS, half * HALF : (half + 1) * HALF]
+                briefs_raw[half, a] = load_pass(4 + 2 * half + a, src, f"briefs_raw{half}{a}")
+
+        def load_weight(lo, hi, slots):
+            rows = keep.tile([P, len(slots), hi - lo], F32, name=f"weight{lo}_{slots[0]}")
+            src = wgs.rearrange("(p i) j -> p i j", i=SLOTS)[:, slots[0] : slots[-1] + 1, lo:hi]
+            for q in (0, 2, 1, 3):
+                nc.sync.dma_start(rows[32 * q : 32 * (q + 1)], src)
+            for n, i in enumerate(slots):
+                weight[i] = weight.get(i, []) + [(lo, hi, rows[:, n, :])]
+
+        def load_page(i):
+            page[i] = keep.tile([P, T2], F32, name=f"page{i}")
+            nc.sync.dma_start(page[i][:], page0.rearrange("(p i) t -> p i t", i=SLOTS)[:, i, :])
+
+        load_briefs(0)
+        load_briefs(1)
+        idx3 = load_list(offs3, "idx3")
+        load_page(0)
+        load_weight(0, HALF, range(1))
+        load_weight(0, HALF, range(1, 2))
+        load_page(1)
+        load_weight(HALF, S, range(2))
+        load_weight(0, HALF, range(2, SLOTS))
+        load_page(2)
+        load_page(3)
+        idx2 = load_list(offs2, "idx2")
+        tab2 = keep.tile([P, T3], U32, name="tab2", align_bytes=64)
+        load_words(tab2[:], tab2_words[0])
+        load_scale_rows(nc.sync, tab2_scale_rows, tab2_scales, range(QUADRANTS - 1))
+        load_weight(HALF, S, range(2, SLOTS))
+        load_scale_rows(nc.sync, tab2_scale_rows, tab2_scales, range(QUADRANTS - 1, QUADRANTS))
+        idx4 = load_list(offs4, "idx4")
+
+        w2_ops = [(w2_codes[:, a, :].bitcast(FP4X4), w2_scale_rows[:, a, :]) for a in range(PASSES)]
+        w3_ops = [(w3_codes[:, a, :].bitcast(FP8X4), w3_scale_rows[:, a, :]) for a in range(PASSES)]
+        product = {}
+
+        def table_sum(b, w_ops, second_scales, bank_number):
+            cols = slice(b * P, (b + 1) * P)
+            scales = (v_scales[:, cols], second_scales[:, cols])
+            v_ops = [(v_words[a][:, cols].bitcast(FP8X4), scales[a]) for a in range(PASSES)]
+            acc = bank(bank_number, [P, H])
+            mx_sum(acc, v_ops, w_ops)
+            return by_slot(acc)
+
+        f3 = {}
+
+        def fetch_f3(b):
+            f3[b] = reuse.tile([P, SLOTS, P], F32, name="f3", tag=f"f3_{b}")
+            nc.scalar.copy(f3[b][:], table_sum(b, w3_ops, v_scales[SCALE_ROWS:P], b))
+
+        def times_f2(b):
+            if b % 2 == 0:
+                product[b // 2] = reuse.tile([P, 2, SLOTS, P], F32, name="product", tag="product", bufs=BLOCKS // 2)
+            f2 = table_sum(b, w2_ops, v_scales_raised, b)
+            nc.vector.tensor_tensor(product[b // 2][:, b % 2], f2, f3[b][:], MULT)
+
+        def quantize_weight(raw, name, interleave):
+            words, scales = moving_operand(name)
+            staged = staging()
+            interleave(raw[:], staged[:])
+            quantize(staged[:], words, scales)
+            return words[:].bitcast(FP8X4), scales[:]
+
+        def times_f1(pair, triple):
+            for n in range(2):
+                b = 2 * pair + n
+                f1 = table_sum(b, w1_ops, v_scales[SCALE_ROWS:P], F1_BANKS[b])
+                nc.vector.tensor_tensor(triple[:, n], f1, product[pair][:, n], MULT)
+            product[pair] = triple
+
+        briefs_ops = {}
+
+        def quantize_briefs(half, a, interleave, staged):
+            interleave(briefs_raw[half, a][:], staged[:])
+            words = keep.tile([P, HALF], U32, name=f"briefs_words{half}{a}", align_bytes=64)
+            scales = keep.tile([P, HALF], U8, name=f"briefs_scales{half}{a}", align_bytes=64)
+            quantize(staged[:], words, scales)
+            briefs_ops[half, a] = words, scales
+
+        h = {}
+
+        def features(half):
+            ops = [briefs_ops[half, a] for a in range(PASSES)]
+            d_acc, d = [], []
+            for n in range(HALF_BLOCKS):
+                cols = slice(n * P, (n + 1) * P)
+                d_acc.append(bank(SLOTS + n, [P, H]))
+                mx_sum(d_acc[n], [(words[:, cols].bitcast(FP8X4), scales[:, cols]) for words, scales in ops], w4_ops)
+            h_acc = [bank(i, [P, HALF_BLOCKS, P]) for i in range(SLOTS)]
+            for i in range(SLOTS):
+                for n in range(HALF_BLOCKS):
+                    b = half * HALF_BLOCKS + n
+                    nc.tensor.matmul(h_acc[i][:, n, :], product[b // 2][:, b % 2, i, :], ident[:],
+                                     start=(n == 0), stop=False, is_transpose=True)
+            for n in range(HALF_BLOCKS):
+                d.append(reuse.tile([P, SLOTS, P], F32, name="d", tag=f"f3_{n}"))
+                nc.scalar.copy(d[n][:], by_slot(d_acc[n]))
+            rows = buffer8(half, [P, SLOTS, HALF], f"h{half}")
+            for i in range(SLOTS):
+                for n in range(HALF_BLOCKS):
+                    nc.tensor.matmul(h_acc[i][:, n, :], d[n][:, i, :], ident[:],
+                                     start=False, stop=(n == HALF_BLOCKS - 1), is_transpose=True)
+                nc.scalar.copy(rows[:, i, :], h_acc[i][:].rearrange("p n j -> p (n j)"))
+            h[half] = rows
 
         def amend(i, lo, hi):
             half, at = divmod(lo, HALF)
+            first, rows = [(a, w) for a, b, w in weight[i] if a <= lo and hi <= b][0]
             nc.vector.tensor_tensor(
-                page[i][:].indirect(entries(idx3, lo, hi)), h[half][:, i, at : at + hi - lo], weight[i, lo], MULT
+                page[i][:].indirect(entries(idx3, lo, hi)), h[half][:, i, at : at + hi - lo],
+                rows[:, lo - first : hi - first], MULT,
             )
 
-        for lo in (0, QUARTER):
-            for i in range(2):
-                amend(i, lo, lo + QUARTER)
-        for i in range(2, SLOTS):
-            amend(i, 0, HALF)
+        w1_ops = [quantize_weight(w1_raw[0], "w1_0", interleave_on_vector)]
+        for b in range(BLOCKS):
+            fetch_f3(b)
+        w1_ops.append(quantize_weight(w1_raw[1], "w1_1", interleave_on_vector))
+        for b in range(BLOCKS):
+            times_f2(b)
+        w4_ops = [quantize_weight(w4_raw[a], f"w4_{a}", interleave_on_scalar) for a in range(PASSES)]
+        quantize_briefs(0, 0, interleave_on_scalar, reuse.tile([P, BANK, SLOTS], BF16, name="staged", tag="late", align_bytes=64))
+        quantize_briefs(0, 1, interleave_on_scalar, staging())
+        late = reuse.tile([P, 2, 2, SLOTS, P], F32, name="late", tag="late", align_bytes=64)
+        for pair in range(BLOCKS // 2):
+            times_f1(pair, product[pair] if pair < 2 else late[:, pair - 2])
+        features(0)
+        for a in range(PASSES):
+            quantize_briefs(1, a, interleave_on_vector, staging())
+        features(1)
+        amend(0, 0, HALF)
+        amend(1, 0, HALF)
 
         v2_words = keep.tile([P, S2], U32, name="v2_words", align_bytes=64)
         v2_scales = keep.tile([P, S2], U8, name="v2_scales", align_bytes=64)
         nc.vector.tensor_copy(v2_words[:], tab2[:].indirect(idx2[:]))
-        pairs = [buffer4(c, [P, 2, BANK, 2], BF16, f"pairs{c}") for c in range(CHUNKS)]
+        pairs = [
+            reuse.tile([P, 2, 2, BANK, 2], BF16, name=f"pairs{c}", tag=f"tab{c}", align_bytes=64) for c in range(CHUNKS // 2)
+        ]
         for i in range(SLOTS):
+            if i == 2:
+                amend(2, 0, HALF)
+                amend(3, 0, HALF)
             amend(i, HALF, S)
             for c in range(CHUNKS):
-                nc.scalar.copy(pairs[c][:, i // 2, :, i % 2], page[i][:, c * BANK : (c + 1) * BANK])
+                nc.scalar.copy(pairs[c // 2][:, c % 2, i // 2, :, i % 2], page[i][:, c * BANK : (c + 1) * BANK])
         nc.vector.tensor_copy(v2_scales[:], tab2_scale_rows[:, 0, :].indirect(idx2[:]))
 
         page_staged, page_ops = [], []
         for step in range(CHUNKS + 1):
             if step < CHUNKS:
                 page_staged.append(staging())
-                copy = nc.scalar.copy if step == CHUNKS - 1 else nc.vector.tensor_copy
+                copy = nc.scalar.copy if step == CHUNKS - 1 and SCALAR_WEAVES else nc.vector.tensor_copy
                 copy(
                     page_staged[step][:].rearrange("p c i -> p (c i)").bitcast(F32).rearrange("p (c u) -> p c u", u=2),
-                    pairs[step][:].rearrange("p u c n -> p u (c n)").bitcast(F32).rearrange("p u c -> p c u"),
+                    pairs[step // 2][:, step % 2].rearrange("p u c n -> p u (c n)").bitcast(F32).rearrange("p u c -> p c u"),
                 )
             if step > 0:
                 page_ops.append(moving_operand(f"page_{step - 1}"))
-                quantize(page_staged[step - 1], *page_ops[step - 1])
+                quantize(page_staged[step - 1][:], *page_ops[step - 1])
 
         e, x, inverse = {}, {}, {}
 
         def scores(g):
             rows = slice(g * P, (g + 1) * P)
-            last = g == GROUPS - 1
-            e[g] = buffer8(2 + g - last, [P, T2], f"e{g}")
+            e[g] = buffer8(E_BUFFERS[g], [P, T2], f"e{g}")
             for c in range(CHUNKS):
                 acc = bank((g * CHUNKS + c) % BANKS, [P, BANK])
                 nc.tensor.matmul_mx(
                     out=acc[:], lhsT=v2_words[:, rows].bitcast(FP8X4), lhsT_scale=v2_scales[:, rows],
                     rhs=page_ops[c][0][:].bitcast(FP8X4), rhs_scale=page_ops[c][1][:], start=True, stop=True,
                 )
-                on_vector = last or (g == 0 and c >= CHUNKS // 2)
-                copy = nc.vector.tensor_copy if on_vector else nc.scalar.copy
+                copy = nc.vector.tensor_copy if (g, c) in VECTOR_EMPTIES else nc.scalar.copy
                 copy(e[g][:, c * BANK : (c + 1) * BANK], acc[:])
 
         def pick(g):
-            x[g] = buffer4(g, [P, S], F32, "x")
-            for lo in (0, HALF):
-                nc.vector.tensor_copy(x[g][:, lo : lo + HALF], e[g][:].indirect(entries(idx4, lo, lo + HALF)))
+            if g % 2 == 0:
+                both = buffer8(6 + g // 2, [P, 2, S], "x")
+                x[g], x[g + 1] = both[:, 0, :], both[:, 1, :]
+            for group, lo, hi in PICKS:
+                if group == g:
+                    nc.vector.tensor_copy(x[g][:, lo:hi], e[g][:].indirect(entries(idx4, lo, hi)))
 
-        def magnitude(piece):
-            g, half = divmod(piece, 2)
-            if half == 0:
-                both = reuse.tile([P, 2, HALF], F32, name="inverse", tag="product", bufs=BLOCKS // 2)
-                inverse[piece], inverse[piece + 1] = both[:, 0, :], both[:, 1, :]
-            cols = slice(half * HALF, (half + 1) * HALF)
-            nc.scalar.activation(inverse[piece], x[g][:, cols], ACT.Abs, scale=unit[:, g : g + 1])
+        def magnitude(g, lo, hi):
+            if lo == 0:
+                inverse[g] = reuse.tile([P, S], F32, name="inverse", tag="product", bufs=BLOCKS // 2)
+            nc.scalar.activation(inverse[g][:, lo:hi], x[g][:, lo:hi], ACT.Abs, scale=unit[:, g : g + 1])
 
-        def inverse_root(piece):
-            g = piece // 2
-            nc.scalar.activation(inverse[piece], inverse[piece], ACT.Abs_reciprocal_sqrt, bias=unit_room[:, g : g + 1])
+        def inverse_root(g, lo, hi):
+            part = inverse[g][:, lo:hi]
+            nc.scalar.activation(part, part, ACT.Abs_reciprocal_sqrt, bias=unit_room[:, g : g + 1])
 
-        def finish(piece):
-            g, half = divmod(piece, 2)
-            rows, cols = slice(g * P, (g + 1) * P), slice(half * HALF, (half + 1) * HALF)
-            nc.scalar.activation(inverse[piece], inverse[piece], ACT.Square, scale=root[:, g : g + 1])
-            nc.vector.tensor_tensor(x[g][:, cols], x[g][:, cols], inverse[piece], MULT)
+        def finish(g, lo, hi):
+            rows, part = slice(g * P, (g + 1) * P), inverse[g][:, lo:hi]
+            nc.scalar.activation(part, part, ACT.Square, scale=root[:, g : g + 1])
+            engine = nc.gpsimd if (g, lo) in ON_GPSIMD else nc.vector
+            engine.tensor_tensor(x[g][:, lo:hi], x[g][:, lo:hi], part, MULT)
             if g == GROUPS - 1:
-                nc.sync.dma_start(out[rows, cols], x[g][:, cols])
-            elif half == 1:
-                nc.sync.dma_start(out[rows, :], x[g][:])
+                nc.sync.dma_start(out[rows, lo:hi], x[g][:, lo:hi])
+            elif hi == S:
+                nc.sync.dma_start(out[rows, :], x[g])
 
         scores(0)
         pick(0)
@@ -381,10 +393,10 @@ def tile_list_translator_brief_scores_kernel(
         pick(2)
         scores(3)
         pick(3)
-        for step in range(PIECES + 2):
-            if step < PIECES:
-                magnitude(step)
-            if 1 <= step <= PIECES:
-                inverse_root(step - 1)
+        for step in range(len(PIECES) + 2):
+            if step < len(PIECES):
+                magnitude(*PIECES[step])
+            if 1 <= step <= len(PIECES):
+                inverse_root(*PIECES[step - 1])
             if step >= 2:
-                finish(step - 2)
+                finish(*PIECES[step - 2])

@@ -15,6 +15,7 @@ U8 = mybir.dt.uint8
 FP8X4 = mybir.dt.float8_e4m3fn_x4
 FP4X4 = mybir.dt.float4_e2m1fn_x4
 MULT = mybir.AluOpType.mult
+MAX = mybir.AluOpType.max
 ACT = mybir.ActivationFunctionType
 
 P = 128
@@ -34,14 +35,21 @@ CHUNKS = T2 // BANK
 GROUPS = S2 // P
 F3_BANKS = (0, 2, 4, 6, 0, 2, 4, 6)
 F2_BANKS = (1, 3, 5, 7, 1, 3, 5, 7)
-F1_BANKS = (4, 5, 6, 7, 0, 1, 2, 3)
+F1_BANKS = (4, 5, 6, 7, 1, 2, 3, 1)
 F3_BUFFERS = (0, 1, 2, 3, 0, 1, 2, 3)
 E_BUFFERS = (2, 3, 4, 5)
 SCALAR_WEAVES = True
-VECTOR_EMPTIES = ((0, 2), (0, 3), (1, 3), (2, 3), (3, 1), (3, 2), (3, 3))
+VECTOR_EMPTIES = ((1, 0), (1, 1), (1, 2), (2, 3), (3, 1), (3, 2), (3, 3))
 PICKS = [(g, lo, lo + HALF) for g in range(GROUPS) for lo in (0, HALF)]
 PIECES = [(g, lo, lo + HALF) for g in range(GROUPS) for lo in (0, HALF)]
 ON_GPSIMD = ()
+E_BANKS = ((0, 1, 2, 3), (4, 5, 6, 7), (2, 3, 0, 1), (6, 7, 4, 5))
+SCALAR_ROUNDS = 1
+TWO_PRODUCTS = ()
+VECTOR_FETCHES_D = ((0, 1), (0, 3))
+VECTOR_ROUNDS = 0
+STAGING = 3
+ABS_ON_VECTOR = ()
 LINE = 4
 
 
@@ -68,7 +76,7 @@ def tile_list_translator_brief_scores_kernel(
             return psum.tile(shape, F32, name=f"bank{number}", tag=f"bank{number}")
 
         def staging():
-            return reuse.tile([P, BANK, SLOTS], BF16, name="staged", tag="staged", bufs=3, align_bytes=64)
+            return reuse.tile([P, BANK, SLOTS], BF16, name="staged", tag="staged", bufs=STAGING, align_bytes=64)
 
         def moving_operand(name):
             words = reuse.tile([P, BANK], U32, name=name + "_words", tag="moving_words", bufs=4, align_bytes=64)
@@ -198,16 +206,15 @@ def tile_list_translator_brief_scores_kernel(
             nc.sync.dma_start(page[i][:], page0.rearrange("(p i) t -> p i t", i=SLOTS)[:, i, :])
 
         load_briefs(0)
-        load_briefs(1)
         idx3 = load_list(offs3, "idx3")
         load_page(0)
-        load_weight(0, HALF, range(1))
-        load_weight(0, HALF, range(1, 2))
+        load_weight(0, HALF, range(2))
         load_page(1)
+        load_briefs(1)
+        for i in range(2, SLOTS):
+            load_weight(0, HALF, range(i, i + 1))
+            load_page(i)
         load_weight(HALF, S, range(2))
-        load_weight(0, HALF, range(2, SLOTS))
-        load_page(2)
-        load_page(3)
         idx2 = load_list(offs2, "idx2")
         tab2 = keep.tile([P, T3], U32, name="tab2", align_bytes=64)
         load_words(tab2[:], tab2_words[0])
@@ -256,11 +263,13 @@ def tile_list_translator_brief_scores_kernel(
 
         briefs_ops = {}
 
-        def quantize_briefs(half, a, interleave, staged):
-            interleave(briefs_raw[half, a][:], staged[:])
+        def quantize_briefs(half, a, interleave, staged, width=HALF):
             words = keep.tile([P, HALF], U32, name=f"briefs_words{half}{a}", align_bytes=64)
             scales = keep.tile([P, HALF], U8, name=f"briefs_scales{half}{a}", align_bytes=64)
-            quantize(staged[:], words, scales)
+            for lo in range(0, HALF, width):
+                cols = slice(lo, lo + width)
+                interleave(briefs_raw[half, a][:, :, cols], staged[:, cols, :])
+                quantize(staged[:, cols, :], words[:, cols], scales[:, cols])
             briefs_ops[half, a] = words, scales
 
         h = {}
@@ -273,16 +282,16 @@ def tile_list_translator_brief_scores_kernel(
                 d_acc.append(bank(SLOTS + n, [P, H]))
                 mx_sum(d_acc[n], [(words[:, cols].bitcast(FP8X4), scales[:, cols]) for words, scales in ops], w4_ops)
             h_acc = [bank(i, [P, HALF_BLOCKS, P]) for i in range(SLOTS)]
+            for n in range(HALF_BLOCKS):
+                d.append(reuse.tile([P, SLOTS, P], F32, name="d", tag=f"f3_{n}"))
+                copy = nc.vector.tensor_copy if (half, n) in VECTOR_FETCHES_D else nc.scalar.copy
+                copy(d[n][:], by_slot(d_acc[n]))
+            rows = buffer8(half, [P, SLOTS, HALF], f"h{half}")
             for i in range(SLOTS):
                 for n in range(HALF_BLOCKS):
                     b = half * HALF_BLOCKS + n
                     nc.tensor.matmul(h_acc[i][:, n, :], product[b // 2][:, b % 2, i, :], ident[:],
                                      start=(n == 0), stop=False, is_transpose=True)
-            for n in range(HALF_BLOCKS):
-                d.append(reuse.tile([P, SLOTS, P], F32, name="d", tag=f"f3_{n}"))
-                nc.scalar.copy(d[n][:], by_slot(d_acc[n]))
-            rows = buffer8(half, [P, SLOTS, HALF], f"h{half}")
-            for i in range(SLOTS):
                 for n in range(HALF_BLOCKS):
                     nc.tensor.matmul(h_acc[i][:, n, :], d[n][:, i, :], ident[:],
                                      start=False, stop=(n == HALF_BLOCKS - 1), is_transpose=True)
@@ -305,16 +314,16 @@ def tile_list_translator_brief_scores_kernel(
             times_f2(b)
         w4_ops = [quantize_weight(w4_raw[a], f"w4_{a}", interleave_on_scalar) for a in range(PASSES)]
         quantize_briefs(0, 0, interleave_on_scalar, reuse.tile([P, BANK, SLOTS], BF16, name="staged", tag="late", align_bytes=64))
-        quantize_briefs(0, 1, interleave_on_scalar, staging())
+        quantize_briefs(0, 1, interleave_on_scalar, staging(), QUARTER)
         late = reuse.tile([P, 2, 2, SLOTS, P], F32, name="late", tag="late", align_bytes=64)
         for pair in range(BLOCKS // 2):
             times_f1(pair, product[pair] if pair < 2 else late[:, pair - 2])
         features(0)
         for a in range(PASSES):
-            quantize_briefs(1, a, interleave_on_vector, staging())
+            quantize_briefs(1, a, interleave_on_scalar, staging())
         features(1)
-        amend(0, 0, HALF)
-        amend(1, 0, HALF)
+        for i in range(SLOTS):
+            amend(i, 0, HALF)
 
         v2_words = keep.tile([P, S2], U32, name="v2_words", align_bytes=64)
         v2_scales = keep.tile([P, S2], U8, name="v2_scales", align_bytes=64)
@@ -323,9 +332,6 @@ def tile_list_translator_brief_scores_kernel(
             reuse.tile([P, 2, 2, BANK, 2], BF16, name=f"pairs{c}", tag=f"tab{c}", align_bytes=64) for c in range(CHUNKS // 2)
         ]
         for i in range(SLOTS):
-            if i == 2:
-                amend(2, 0, HALF)
-                amend(3, 0, HALF)
             amend(i, HALF, S)
             for c in range(CHUNKS):
                 nc.scalar.copy(pairs[c // 2][:, c % 2, i // 2, :, i % 2], page[i][:, c * BANK : (c + 1) * BANK])
@@ -350,7 +356,7 @@ def tile_list_translator_brief_scores_kernel(
             rows = slice(g * P, (g + 1) * P)
             e[g] = buffer8(E_BUFFERS[g], [P, T2], f"e{g}")
             for c in range(CHUNKS):
-                acc = bank((g * CHUNKS + c) % BANKS, [P, BANK])
+                acc = bank(E_BANKS[g][c], [P, BANK])
                 nc.tensor.matmul_mx(
                     out=acc[:], lhsT=v2_words[:, rows].bitcast(FP8X4), lhsT_scale=v2_scales[:, rows],
                     rhs=page_ops[c][0][:].bitcast(FP8X4), rhs_scale=page_ops[c][1][:], start=True, stop=True,
@@ -369,16 +375,22 @@ def tile_list_translator_brief_scores_kernel(
         def magnitude(g, lo, hi):
             if lo == 0:
                 inverse[g] = reuse.tile([P, S], F32, name="inverse", tag="product", bufs=BLOCKS // 2)
-            nc.scalar.activation(inverse[g][:, lo:hi], x[g][:, lo:hi], ACT.Abs, scale=unit[:, g : g + 1])
+            if (g, lo) in ABS_ON_VECTOR:
+                nc.vector.scalar_tensor_tensor(inverse[g][:, lo:hi], x[g][:, lo:hi], -1.0, x[g][:, lo:hi], MULT, MAX)
+            else:
+                nc.scalar.activation(inverse[g][:, lo:hi], x[g][:, lo:hi], ACT.Abs)
 
         def inverse_root(g, lo, hi):
             part = inverse[g][:, lo:hi]
-            nc.scalar.activation(part, part, ACT.Abs_reciprocal_sqrt, bias=unit_room[:, g : g + 1])
+            nc.scalar.activation(part, part, ACT.Abs_reciprocal_sqrt, bias=unit_room[:, g : g + 1], scale=unit[:, g : g + 1])
 
         def finish(g, lo, hi):
             rows, part = slice(g * P, (g + 1) * P), inverse[g][:, lo:hi]
-            nc.scalar.activation(part, part, ACT.Square, scale=root[:, g : g + 1])
             engine = nc.gpsimd if (g, lo) in ON_GPSIMD else nc.vector
+            if (g, lo) in TWO_PRODUCTS:
+                nc.vector.scalar_tensor_tensor(x[g][:, lo:hi], x[g][:, lo:hi], unit[:, g : g + 1], part, MULT, MULT)
+            else:
+                nc.scalar.activation(part, part, ACT.Square, scale=root[:, g : g + 1])
             engine.tensor_tensor(x[g][:, lo:hi], x[g][:, lo:hi], part, MULT)
             if g == GROUPS - 1:
                 nc.sync.dma_start(out[rows, lo:hi], x[g][:, lo:hi])

@@ -50,6 +50,11 @@ VECTOR_FETCHES_D = ((0, 1), (0, 3))
 VECTOR_ROUNDS = 0
 STAGING = 3
 ABS_ON_VECTOR = ()
+BOTH_ON_GPSIMD = ()
+BANKS_AHEAD = 16
+BANKS_A_STEP = 1
+SPREAD_BANKS = (7, 3, 4, 5, 6)
+SPREAD_BUFFER = 7
 LINE = 4
 
 
@@ -141,12 +146,12 @@ def tile_list_translator_brief_scores_kernel(
         tab2_scale_rows = zeroed_scales([P, 1, T3], "tab2_scale_rows")
         v_scales_raised = zeroed_scales([P, S], "v_scales_raised")
 
+        ident = keep.tile([P, P], F32, name="ident")
+        make_identity(nc, ident[:])
         room_col = keep.tile([P, GROUPS], F32, name="room_col")
         with nc.allow_non_contiguous_dma(reason="one value of room for each partition and group"):
             nc.gpsimd.dma_start(room_col[:], room.rearrange("(g p) -> p g", p=P))
         load_scale_rows(nc.gpsimd, w2_scale_rows, w2_scales)
-        ident = keep.tile([P, P], F32, name="ident")
-        make_identity(nc, ident[:])
 
         root = keep.tile([P, GROUPS], F32, name="root")
         unit = keep.tile([P, GROUPS], F32, name="unit")
@@ -163,6 +168,8 @@ def tile_list_translator_brief_scores_kernel(
                 tab_scale_rows[32 * q : 32 * q + PASSES * SCALE_ROWS].bitcast(I32),
                 tab_scales[:, SCALE_ROWS * q : SCALE_ROWS * (q + 1), :].bitcast(I32),
             )
+        wgs_rows = {0: keep.tile([P, HALF], F32, name="wgs_rows0")}
+        nc.sync.dma_start(wgs_rows[0][:], wgs[:, :HALF])
         load_words(tab[1][:], tab_words[1])
         w3_codes = keep.tile([P, PASSES, H], U32, name="w3_codes", align_bytes=64)
         nc.sync.dma_start(w3_codes[:].bitcast(I32), w3_words.rearrange("a p c i -> p a (c i)").bitcast(I32))
@@ -201,19 +208,36 @@ def tile_list_translator_brief_scores_kernel(
             for n, i in enumerate(slots):
                 weight[i] = weight.get(i, []) + [(lo, hi, rows[:, n, :])]
 
+        def spread_weight(half):
+            turned = bank(SPREAD_BANKS[0], [P, HALF_BLOCKS, P])
+            for n in range(HALF_BLOCKS):
+                nc.tensor.matmul(turned[:, n, :], wgs_rows[half][:, n * P : (n + 1) * P], ident[:],
+                                 start=(n == 0), stop=(n == HALF_BLOCKS - 1), is_transpose=True)
+            repeated = buffer8(SPREAD_BUFFER, [P, SLOTS, HALF_BLOCKS, QUADRANTS, 32], "repeated")
+            rows = keep.tile([P, SLOTS, HALF], F32, name=f"weight{half}")
+            for i in range(SLOTS):
+                src = turned[:].rearrange("j n (p i) -> j i n p", i=SLOTS)[:, i]
+                nc.scalar.copy(repeated[:, i], src.unsqueeze(2).to_broadcast([P, HALF_BLOCKS, QUADRANTS, 32]))
+            for i in range(SLOTS):
+                back = bank(SPREAD_BANKS[1 + i], [P, HALF_BLOCKS, P])
+                for n in range(HALF_BLOCKS):
+                    nc.tensor.matmul(back[:, n, :], repeated[:, i, n].rearrange("j q p -> j (q p)"), ident[:],
+                                     start=(n == 0), stop=(n == HALF_BLOCKS - 1), is_transpose=True)
+                nc.scalar.copy(rows[:, i, :], back[:].rearrange("p n j -> p (n j)"))
+                weight[i] = weight.get(i, []) + [(half * HALF, (half + 1) * HALF, rows[:, i, :])]
+
         def load_page(i):
             page[i] = keep.tile([P, T2], F32, name=f"page{i}")
             nc.sync.dma_start(page[i][:], page0.rearrange("(p i) t -> p i t", i=SLOTS)[:, i, :])
 
+        spread_weight(0)
         load_briefs(0)
         idx3 = load_list(offs3, "idx3")
         load_page(0)
-        load_weight(0, HALF, range(2))
         load_page(1)
         load_briefs(1)
-        for i in range(2, SLOTS):
-            load_weight(0, HALF, range(i, i + 1))
-            load_page(i)
+        load_page(2)
+        load_page(3)
         load_weight(HALF, S, range(2))
         idx2 = load_list(offs2, "idx2")
         tab2 = keep.tile([P, T3], U32, name="tab2", align_bytes=64)
@@ -352,17 +376,19 @@ def tile_list_translator_brief_scores_kernel(
 
         e, x, inverse = {}, {}, {}
 
-        def scores(g):
+        def score(g, c):
             rows = slice(g * P, (g + 1) * P)
-            e[g] = buffer8(E_BUFFERS[g], [P, T2], f"e{g}")
-            for c in range(CHUNKS):
-                acc = bank(E_BANKS[g][c], [P, BANK])
-                nc.tensor.matmul_mx(
-                    out=acc[:], lhsT=v2_words[:, rows].bitcast(FP8X4), lhsT_scale=v2_scales[:, rows],
-                    rhs=page_ops[c][0][:].bitcast(FP8X4), rhs_scale=page_ops[c][1][:], start=True, stop=True,
-                )
-                copy = nc.vector.tensor_copy if (g, c) in VECTOR_EMPTIES else nc.scalar.copy
-                copy(e[g][:, c * BANK : (c + 1) * BANK], acc[:])
+            if c == 0:
+                e[g] = buffer8(E_BUFFERS[g], [P, T2], f"e{g}")
+            acc = bank(E_BANKS[g][c], [P, BANK])
+            nc.tensor.matmul_mx(
+                out=acc[:], lhsT=v2_words[:, rows].bitcast(FP8X4), lhsT_scale=v2_scales[:, rows],
+                rhs=page_ops[c][0][:].bitcast(FP8X4), rhs_scale=page_ops[c][1][:], start=True, stop=True,
+            )
+            copy = nc.vector.tensor_copy if (g, c) in VECTOR_EMPTIES else nc.scalar.copy
+            copy(e[g][:, c * BANK : (c + 1) * BANK], acc[:])
+            if c == CHUNKS - 1:
+                pick(g)
 
         def pick(g):
             if g % 2 == 0:
@@ -382,12 +408,18 @@ def tile_list_translator_brief_scores_kernel(
 
         def inverse_root(g, lo, hi):
             part = inverse[g][:, lo:hi]
-            nc.scalar.activation(part, part, ACT.Abs_reciprocal_sqrt, bias=unit_room[:, g : g + 1], scale=unit[:, g : g + 1])
+            if (g, lo) in BOTH_ON_GPSIMD:
+                nc.scalar.activation(part, part, ACT.Abs_reciprocal_sqrt, bias=room_col[:, g : g + 1])
+            else:
+                nc.scalar.activation(part, part, ACT.Abs_reciprocal_sqrt, bias=unit_room[:, g : g + 1], scale=unit[:, g : g + 1])
 
         def finish(g, lo, hi):
             rows, part = slice(g * P, (g + 1) * P), inverse[g][:, lo:hi]
             engine = nc.gpsimd if (g, lo) in ON_GPSIMD else nc.vector
-            if (g, lo) in TWO_PRODUCTS:
+            if (g, lo) in BOTH_ON_GPSIMD:
+                engine = nc.gpsimd
+                engine.tensor_tensor(x[g][:, lo:hi], x[g][:, lo:hi], part, MULT)
+            elif (g, lo) in TWO_PRODUCTS:
                 nc.vector.scalar_tensor_tensor(x[g][:, lo:hi], x[g][:, lo:hi], unit[:, g : g + 1], part, MULT, MULT)
             else:
                 nc.scalar.activation(part, part, ACT.Square, scale=root[:, g : g + 1])
@@ -397,17 +429,14 @@ def tile_list_translator_brief_scores_kernel(
             elif hi == S:
                 nc.sync.dma_start(out[rows, :], x[g])
 
-        scores(0)
-        pick(0)
-        scores(1)
-        scores(2)
-        pick(1)
-        pick(2)
-        scores(3)
-        pick(3)
+        banks_of_e = [(g, c) for g in range(GROUPS) for c in range(CHUNKS)]
+        for g, c in banks_of_e[:BANKS_AHEAD]:
+            score(g, c)
         for step in range(len(PIECES) + 2):
             if step < len(PIECES):
                 magnitude(*PIECES[step])
+            for g, c in banks_of_e[BANKS_AHEAD + BANKS_A_STEP * step : BANKS_AHEAD + BANKS_A_STEP * (step + 1)]:
+                score(g, c)
             if 1 <= step <= len(PIECES):
                 inverse_root(*PIECES[step - 1])
             if step >= 2:

@@ -55,6 +55,8 @@ BANKS_AHEAD = 16
 BANKS_A_STEP = 1
 SPREAD_BANKS = (7, 3, 4, 5, 6)
 SPREAD_BUFFER = 7
+MOVES_ON_SCALAR = 4
+W3_AHEAD = 3
 LINE = 4
 
 
@@ -143,7 +145,8 @@ def tile_list_translator_brief_scores_kernel(
         tab_scale_rows = zeroed_scales([P, T], "tab_scale_rows")
         w3_scale_rows = zeroed_scales([P, PASSES, H], "w3_scale_rows")
         w2_scale_rows = zeroed_scales([P, PASSES, H], "w2_scale_rows")
-        tab2_scale_rows = zeroed_scales([P, 1, T3], "tab2_scale_rows")
+        tab2_scale_rows = zeroed_scales([P, T3], "tab2_scale_rows")
+        v2_scales = zeroed_scales([P, S2], "v2_scales")
         v_scales_raised = zeroed_scales([P, S], "v_scales_raised")
 
         ident = keep.tile([P, P], F32, name="ident")
@@ -163,7 +166,7 @@ def tile_list_translator_brief_scores_kernel(
         tab = [reuse.tile([P, T], U32, name=f"tab{a}", tag=f"tab{a}", align_bytes=64) for a in range(PASSES)]
         load_words(tab[0][:], tab_words[0])
         idx = load_list(offs, "idx")
-        for q in range(QUADRANTS):
+        for q in (0, 2, 1, 3):
             nc.sync.dma_start(
                 tab_scale_rows[32 * q : 32 * q + PASSES * SCALE_ROWS].bitcast(I32),
                 tab_scales[:, SCALE_ROWS * q : SCALE_ROWS * (q + 1), :].bitcast(I32),
@@ -234,17 +237,16 @@ def tile_list_translator_brief_scores_kernel(
         load_briefs(0)
         idx3 = load_list(offs3, "idx3")
         load_page(0)
+        idx2 = load_list(offs2, "idx2")
+        nc.sync.dma_start(tab2_scale_rows[0:P:8].bitcast(I32), tab2_scales[0].bitcast(I32))
         load_page(1)
         load_briefs(1)
         load_page(2)
         load_page(3)
         load_weight(HALF, S, range(2))
-        idx2 = load_list(offs2, "idx2")
         tab2 = keep.tile([P, T3], U32, name="tab2", align_bytes=64)
-        load_words(tab2[:], tab2_words[0])
-        load_scale_rows(nc.sync, tab2_scale_rows, tab2_scales, range(QUADRANTS - 1))
         load_weight(HALF, S, range(2, SLOTS))
-        load_scale_rows(nc.sync, tab2_scale_rows, tab2_scales, range(QUADRANTS - 1, QUADRANTS))
+        load_words(tab2[:], tab2_words[0])
         idx4 = load_list(offs4, "idx4")
 
         w2_ops = [(w2_codes[:, a, :].bitcast(FP4X4), w2_scale_rows[:, a, :]) for a in range(PASSES)]
@@ -296,6 +298,15 @@ def tile_list_translator_brief_scores_kernel(
                 quantize(staged[:, cols, :], words[:, cols], scales[:, cols])
             briefs_ops[half, a] = words, scales
 
+        def quantize_briefs_together(half, interleave):
+            staged = reuse.tile([P, PASSES, HALF, SLOTS], BF16, name="staged_both", tag="buffer8_2", align_bytes=64)
+            words = keep.tile([P, PASSES, HALF], U32, name=f"briefs_words{half}", align_bytes=64)
+            scales = keep.tile([P, PASSES, HALF], U8, name=f"briefs_scales{half}", align_bytes=64)
+            for a in range(PASSES):
+                interleave(briefs_raw[half, a][:], staged[:, a])
+                briefs_ops[half, a] = words[:, a], scales[:, a]
+            quantize(staged[:].rearrange("p a c i -> p (a c) i"), words[:].rearrange("p a c -> p (a c)"), scales[:].rearrange("p a c -> p (a c)"))
+
         h = {}
 
         def features(half):
@@ -343,15 +354,16 @@ def tile_list_translator_brief_scores_kernel(
         for pair in range(BLOCKS // 2):
             times_f1(pair, product[pair] if pair < 2 else late[:, pair - 2])
         features(0)
-        for a in range(PASSES):
-            quantize_briefs(1, a, interleave_on_scalar, staging())
+        picked2_scales = keep.tile([P, S2], U8, name="picked2_scales", align_bytes=64)
+        nc.vector.tensor_copy(picked2_scales[:], tab2_scale_rows[:].indirect(idx2[:]))
+        for q in range(QUADRANTS):
+            nc.sync.dma_start(v2_scales[32 * q : 32 * q + SCALE_ROWS].bitcast(I32), picked2_scales[32 * q : 32 * (q + 1) : 8].bitcast(I32))
+        quantize_briefs_together(1, interleave_on_scalar)
         features(1)
         for i in range(SLOTS):
             amend(i, 0, HALF)
 
         v2_words = keep.tile([P, S2], U32, name="v2_words", align_bytes=64)
-        v2_scales = keep.tile([P, S2], U8, name="v2_scales", align_bytes=64)
-        nc.vector.tensor_copy(v2_words[:], tab2[:].indirect(idx2[:]))
         pairs = [
             reuse.tile([P, 2, 2, BANK, 2], BF16, name=f"pairs{c}", tag=f"tab{c}", align_bytes=64) for c in range(CHUNKS // 2)
         ]
@@ -359,7 +371,7 @@ def tile_list_translator_brief_scores_kernel(
             amend(i, HALF, S)
             for c in range(CHUNKS):
                 nc.scalar.copy(pairs[c // 2][:, c % 2, i // 2, :, i % 2], page[i][:, c * BANK : (c + 1) * BANK])
-        nc.vector.tensor_copy(v2_scales[:], tab2_scale_rows[:, 0, :].indirect(idx2[:]))
+        nc.vector.tensor_copy(v2_words[:], tab2[:].indirect(idx2[:]))
 
         page_staged, page_ops = [], []
         for step in range(CHUNKS + 1):

@@ -16,6 +16,7 @@ FP8X4 = mybir.dt.float8_e4m3fn_x4
 FP4X4 = mybir.dt.float4_e2m1fn_x4
 MULT = mybir.AluOpType.mult
 MAX = mybir.AluOpType.max
+ADD = mybir.AluOpType.add
 ACT = mybir.ActivationFunctionType
 
 P = 128
@@ -57,6 +58,8 @@ SPREAD_BANKS = (7, 3, 4, 5, 6)
 SPREAD_BUFFER = 7
 MOVES_ON_SCALAR = 4
 W3_AHEAD = 3
+V2_TAG = "weight12"
+V2_AFTER = 3
 LINE = 4
 
 
@@ -163,6 +166,8 @@ def tile_list_translator_brief_scores_kernel(
         nc.gpsimd.tensor_tensor(unit[:], root[:], root[:], MULT)
         nc.gpsimd.tensor_tensor(unit_room[:], unit[:], room_col[:], MULT)
 
+        wgs_rows = {0: keep.tile([P, HALF], F32, name="wgs_rows0")}
+        nc.sync.dma_start(wgs_rows[0][:], wgs[:, :HALF])
         tab = [reuse.tile([P, T], U32, name=f"tab{a}", tag=f"tab{a}", align_bytes=64) for a in range(PASSES)]
         load_words(tab[0][:], tab_words[0])
         idx = load_list(offs, "idx")
@@ -171,12 +176,10 @@ def tile_list_translator_brief_scores_kernel(
                 tab_scale_rows[32 * q : 32 * q + PASSES * SCALE_ROWS].bitcast(I32),
                 tab_scales[:, SCALE_ROWS * q : SCALE_ROWS * (q + 1), :].bitcast(I32),
             )
-        wgs_rows = {0: keep.tile([P, HALF], F32, name="wgs_rows0")}
-        nc.sync.dma_start(wgs_rows[0][:], wgs[:, :HALF])
-        load_words(tab[1][:], tab_words[1])
         w3_codes = keep.tile([P, PASSES, H], U32, name="w3_codes", align_bytes=64)
         nc.sync.dma_start(w3_codes[:].bitcast(I32), w3_words.rearrange("a p c i -> p a (c i)").bitcast(I32))
         load_scale_rows(nc.sync, w3_scale_rows, w3_scales)
+        load_words(tab[1][:], tab_words[1])
         w1_raw = [load_pass(0, w1[:K_PASS, :], "w1_raw0")]
 
         v_words = [keep.tile([P, S], U32, name=f"v_words{a}", align_bytes=64) for a in range(PASSES)]
@@ -294,7 +297,7 @@ def tile_list_translator_brief_scores_kernel(
             scales = keep.tile([P, HALF], U8, name=f"briefs_scales{half}{a}", align_bytes=64)
             for lo in range(0, HALF, width):
                 cols = slice(lo, lo + width)
-                interleave(briefs_raw[half, a][:, :, cols], staged[:, cols, :])
+                interleave[lo // width](briefs_raw[half, a][:, :, cols], staged[:, cols, :])
                 quantize(staged[:, cols, :], words[:, cols], scales[:, cols])
             briefs_ops[half, a] = words, scales
 
@@ -348,8 +351,8 @@ def tile_list_translator_brief_scores_kernel(
         for b in range(BLOCKS):
             times_f2(b)
         w4_ops = [quantize_weight(w4_raw[a], f"w4_{a}", interleave_on_scalar) for a in range(PASSES)]
-        quantize_briefs(0, 0, interleave_on_scalar, reuse.tile([P, BANK, SLOTS], BF16, name="staged", tag="late", align_bytes=64))
-        quantize_briefs(0, 1, interleave_on_scalar, staging(), QUARTER)
+        quantize_briefs(0, 0, [interleave_on_scalar], reuse.tile([P, BANK, SLOTS], BF16, name="staged", tag="late", align_bytes=64))
+        quantize_briefs(0, 1, [interleave_on_scalar] * 2, staging(), QUARTER)
         late = reuse.tile([P, 2, 2, SLOTS, P], F32, name="late", tag="late", align_bytes=64)
         for pair in range(BLOCKS // 2):
             times_f1(pair, product[pair] if pair < 2 else late[:, pair - 2])

@@ -43,10 +43,10 @@ SCALAR_WEAVES = True
 VECTOR_EMPTIES = ((1, 0), (1, 1), (1, 2), (2, 3), (3, 1), (3, 2), (3, 3))
 PICKS = [(g, lo, lo + HALF) for g in range(GROUPS) for lo in (0, HALF)]
 PIECES = [(g, lo, lo + HALF) for g in range(GROUPS) for lo in (0, HALF)]
-ON_GPSIMD = ()
+ON_GPSIMD = ((0, 0), (0, HALF), (1, 0), (1, HALF))
 E_BANKS = ((0, 1, 2, 3), (4, 5, 6, 7), (2, 3, 0, 1), (6, 7, 4, 5))
 SCALAR_ROUNDS = 1
-TWO_PRODUCTS = ()
+TWO_PRODUCTS = ((2, HALF), (3, 0))
 VECTOR_FETCHES_D = ((0, 1), (0, 3))
 VECTOR_ROUNDS = 0
 STAGING = 3
@@ -60,6 +60,7 @@ MOVES_ON_SCALAR = 4
 W3_AHEAD = 3
 V2_TAG = "weight12"
 V2_AFTER = 3
+WHOLE_ROWS = 0
 LINE = 4
 
 
@@ -439,7 +440,7 @@ def tile_list_translator_brief_scores_kernel(
             else:
                 nc.scalar.activation(part, part, ACT.Square, scale=root[:, g : g + 1])
             engine.tensor_tensor(x[g][:, lo:hi], x[g][:, lo:hi], part, MULT)
-            if g == GROUPS - 1:
+            if g >= WHOLE_ROWS:
                 nc.sync.dma_start(out[rows, lo:hi], x[g][:, lo:hi])
             elif hi == S:
                 nc.sync.dma_start(out[rows, :], x[g])

@@ -42,7 +42,7 @@ E_BUFFERS = (2, 3, 4, 5)
 SCALAR_WEAVES = True
 VECTOR_EMPTIES = ((1, 0), (1, 1), (1, 2), (2, 3), (3, 1), (3, 2), (3, 3))
 PICKS = [(g, lo, lo + HALF) for g in range(GROUPS) for lo in (0, HALF)]
-PIECES = [(g, lo, lo + HALF) for g in range(GROUPS) for lo in (0, HALF)]
+PIECES = [(g, lo, lo + HALF) for g in range(GROUPS) for lo in (0, HALF)][:-1] + [(GROUPS - 1, HALF, HALF + QUARTER), (GROUPS - 1, HALF + QUARTER, S)]
 ON_GPSIMD = ((0, 0), (0, HALF), (1, 0), (1, HALF))
 E_BANKS = ((0, 1, 2, 3), (4, 5, 6, 7), (2, 3, 0, 1), (6, 7, 4, 5))
 SCALAR_ROUNDS = 1
@@ -60,7 +60,7 @@ MOVES_ON_SCALAR = 4
 W3_AHEAD = 3
 V2_TAG = "weight12"
 V2_AFTER = 3
-WHOLE_ROWS = 0
+WHOLE_ROWS = 3
 LINE = 4
 
 

@@ -15,8 +15,6 @@ U8 = mybir.dt.uint8
 FP8X4 = mybir.dt.float8_e4m3fn_x4
 FP4X4 = mybir.dt.float4_e2m1fn_x4
 MULT = mybir.AluOpType.mult
-MAX = mybir.AluOpType.max
-ADD = mybir.AluOpType.add
 ACT = mybir.ActivationFunctionType
 
 P = 128
@@ -26,7 +24,6 @@ PASSES = K // K_PASS
 QUADRANTS = 4
 SCALE_ROWS = 4
 BANK = 512
-BANKS = 8
 PER_COLUMN = 16
 HALF = S // 2
 QUARTER = S // 4
@@ -34,34 +31,14 @@ BLOCKS = S // P
 HALF_BLOCKS = HALF // P
 CHUNKS = T2 // BANK
 GROUPS = S2 // P
-F3_BANKS = (0, 2, 4, 6, 0, 2, 4, 6)
-F2_BANKS = (1, 3, 5, 7, 1, 3, 5, 7)
-F1_BANKS = (4, 5, 6, 7, 1, 2, 3, 1)
-F3_BUFFERS = (0, 1, 2, 3, 0, 1, 2, 3)
-E_BUFFERS = (2, 3, 4, 5)
-SCALAR_WEAVES = True
-VECTOR_EMPTIES = ((1, 0), (1, 1), (1, 2), (2, 3), (3, 1), (3, 2), (3, 3))
-PICKS = [(g, lo, lo + HALF) for g in range(GROUPS) for lo in (0, HALF)]
-PIECES = [(g, lo, lo + HALF) for g in range(GROUPS) for lo in (0, HALF)][:-1] + [(GROUPS - 1, HALF, HALF + QUARTER), (GROUPS - 1, HALF + QUARTER, S)]
-ON_GPSIMD = ((0, 0), (0, HALF), (1, 0), (1, HALF))
-E_BANKS = ((0, 1, 2, 3), (4, 5, 6, 7), (2, 3, 0, 1), (6, 7, 4, 5))
-SCALAR_ROUNDS = 1
-TWO_PRODUCTS = ((2, HALF), (3, 0))
-VECTOR_FETCHES_D = ((0, 1), (0, 3))
-VECTOR_ROUNDS = 0
-STAGING = 3
-ABS_ON_VECTOR = ()
-BOTH_ON_GPSIMD = ()
-BANKS_AHEAD = 16
-BANKS_A_STEP = 1
-SPREAD_BANKS = (7, 3, 4, 5, 6)
-SPREAD_BUFFER = 7
-MOVES_ON_SCALAR = 4
-W3_AHEAD = 3
-V2_TAG = "weight12"
-V2_AFTER = 3
-WHOLE_ROWS = 3
+HALVES_IN_TURN = (0, 2, 1, 3)
 LINE = 4
+PIECES = [(g, lo, lo + HALF) for g in range(GROUPS) for lo in (0, HALF)][:-1] + [
+    (GROUPS - 1, lo, lo + QUARTER) for lo in (HALF, HALF + QUARTER)
+]
+VECTOR_LAST_BANKS = 3
+GPSIMD_GROUPS = 2
+TWO_PRODUCTS = PIECES[5:7]
 
 
 def tile_list_translator_brief_scores_kernel(
@@ -77,17 +54,11 @@ def tile_list_translator_brief_scores_kernel(
         def buffer8(number, shape, name):
             return reuse.tile(shape, F32, name=name, tag=f"buffer8_{number}", align_bytes=64)
 
-        def buffer4(number, shape, dtype, name):
-            return reuse.tile(shape, dtype, name=name, tag=f"buffer4_{number}", align_bytes=64)
-
-        def buffer2(number, shape, name, dtype=F32):
-            return reuse.tile(shape, dtype, name=name, tag=f"buffer2_{number}", align_bytes=64)
-
         def bank(number, shape):
             return psum.tile(shape, F32, name=f"bank{number}", tag=f"bank{number}")
 
         def staging():
-            return reuse.tile([P, BANK, SLOTS], BF16, name="staged", tag="staged", bufs=STAGING, align_bytes=64)
+            return reuse.tile([P, BANK, SLOTS], BF16, name="staged", tag="staged", bufs=3, align_bytes=64)
 
         def moving_operand(name):
             words = reuse.tile([P, BANK], U32, name=name + "_words", tag="moving_words", bufs=4, align_bytes=64)
@@ -110,8 +81,8 @@ def tile_list_translator_brief_scores_kernel(
         def load_words(words, src):
             nc.sync.dma_start(words.bitcast(I32), src.rearrange("p t i -> p (t i)").bitcast(I32))
 
-        def load_scale_rows(queue, scales, src, quadrants=range(QUADRANTS)):
-            for q in quadrants:
+        def load_scale_rows(queue, scales, src):
+            for q in range(QUADRANTS):
                 queue.dma_start(
                     scales[32 * q : 32 * q + SCALE_ROWS].bitcast(I32),
                     src[:, SCALE_ROWS * q : SCALE_ROWS * (q + 1), :].rearrange("a r c -> r a c").bitcast(I32),
@@ -167,12 +138,12 @@ def tile_list_translator_brief_scores_kernel(
         nc.gpsimd.tensor_tensor(unit[:], root[:], root[:], MULT)
         nc.gpsimd.tensor_tensor(unit_room[:], unit[:], room_col[:], MULT)
 
-        wgs_rows = {0: keep.tile([P, HALF], F32, name="wgs_rows0")}
-        nc.sync.dma_start(wgs_rows[0][:], wgs[:, :HALF])
+        wgs_rows = keep.tile([P, HALF], F32, name="wgs_rows0")
+        nc.sync.dma_start(wgs_rows[:], wgs[:, :HALF])
         tab = [reuse.tile([P, T], U32, name=f"tab{a}", tag=f"tab{a}", align_bytes=64) for a in range(PASSES)]
         load_words(tab[0][:], tab_words[0])
         idx = load_list(offs, "idx")
-        for q in (0, 2, 1, 3):
+        for q in HALVES_IN_TURN:
             nc.sync.dma_start(
                 tab_scale_rows[32 * q : 32 * q + PASSES * SCALE_ROWS].bitcast(I32),
                 tab_scales[:, SCALE_ROWS * q : SCALE_ROWS * (q + 1), :].bitcast(I32),
@@ -207,37 +178,37 @@ def tile_list_translator_brief_scores_kernel(
                 src = briefs[a * K_PASS : (a + 1) * K_PASS, half * HALF : (half + 1) * HALF]
                 briefs_raw[half, a] = load_pass(4 + 2 * half + a, src, f"briefs_raw{half}{a}")
 
-        def load_weight(lo, hi, slots):
-            rows = keep.tile([P, len(slots), hi - lo], F32, name=f"weight{lo}_{slots[0]}")
-            src = wgs.rearrange("(p i) j -> p i j", i=SLOTS)[:, slots[0] : slots[-1] + 1, lo:hi]
-            for q in (0, 2, 1, 3):
+        def load_weight(slots):
+            rows = keep.tile([P, len(slots), HALF], F32, name=f"weight1_{slots[0]}")
+            src = wgs.rearrange("(p i) j -> p i j", i=SLOTS)[:, slots[0] : slots[-1] + 1, HALF:]
+            for q in HALVES_IN_TURN:
                 nc.sync.dma_start(rows[32 * q : 32 * (q + 1)], src)
             for n, i in enumerate(slots):
-                weight[i] = weight.get(i, []) + [(lo, hi, rows[:, n, :])]
+                weight[i, 1] = rows[:, n, :]
 
-        def spread_weight(half):
-            turned = bank(SPREAD_BANKS[0], [P, HALF_BLOCKS, P])
+        def spread_weight():
+            turned = bank(7, [P, HALF_BLOCKS, P])
             for n in range(HALF_BLOCKS):
-                nc.tensor.matmul(turned[:, n, :], wgs_rows[half][:, n * P : (n + 1) * P], ident[:],
+                nc.tensor.matmul(turned[:, n, :], wgs_rows[:, n * P : (n + 1) * P], ident[:],
                                  start=(n == 0), stop=(n == HALF_BLOCKS - 1), is_transpose=True)
-            repeated = buffer8(SPREAD_BUFFER, [P, SLOTS, HALF_BLOCKS, QUADRANTS, 32], "repeated")
-            rows = keep.tile([P, SLOTS, HALF], F32, name=f"weight{half}")
+            repeated = buffer8(7, [P, SLOTS, HALF_BLOCKS, QUADRANTS, 32], "repeated")
+            rows = keep.tile([P, SLOTS, HALF], F32, name="weight0")
             for i in range(SLOTS):
                 src = turned[:].rearrange("j n (p i) -> j i n p", i=SLOTS)[:, i]
                 nc.scalar.copy(repeated[:, i], src.unsqueeze(2).to_broadcast([P, HALF_BLOCKS, QUADRANTS, 32]))
             for i in range(SLOTS):
-                back = bank(SPREAD_BANKS[1 + i], [P, HALF_BLOCKS, P])
+                back = bank(3 + i, [P, HALF_BLOCKS, P])
                 for n in range(HALF_BLOCKS):
                     nc.tensor.matmul(back[:, n, :], repeated[:, i, n].rearrange("j q p -> j (q p)"), ident[:],
                                      start=(n == 0), stop=(n == HALF_BLOCKS - 1), is_transpose=True)
                 nc.scalar.copy(rows[:, i, :], back[:].rearrange("p n j -> p (n j)"))
-                weight[i] = weight.get(i, []) + [(half * HALF, (half + 1) * HALF, rows[:, i, :])]
+                weight[i, 0] = rows[:, i, :]
 
         def load_page(i):
             page[i] = keep.tile([P, T2], F32, name=f"page{i}")
             nc.sync.dma_start(page[i][:], page0.rearrange("(p i) t -> p i t", i=SLOTS)[:, i, :])
 
-        spread_weight(0)
+        spread_weight()
         load_briefs(0)
         idx3 = load_list(offs3, "idx3")
         load_page(0)
@@ -247,9 +218,9 @@ def tile_list_translator_brief_scores_kernel(
         load_briefs(1)
         load_page(2)
         load_page(3)
-        load_weight(HALF, S, range(2))
+        load_weight(range(2))
         tab2 = keep.tile([P, T3], U32, name="tab2", align_bytes=64)
-        load_weight(HALF, S, range(2, SLOTS))
+        load_weight(range(2, SLOTS))
         load_words(tab2[:], tab2_words[0])
         idx4 = load_list(offs4, "idx4")
 
@@ -287,29 +258,33 @@ def tile_list_translator_brief_scores_kernel(
         def times_f1(pair, triple):
             for n in range(2):
                 b = 2 * pair + n
-                f1 = table_sum(b, w1_ops, v_scales[SCALE_ROWS:P], F1_BANKS[b])
+                f1 = table_sum(b, w1_ops, v_scales[SCALE_ROWS:P], 4 + b % HALF_BLOCKS)
                 nc.vector.tensor_tensor(triple[:, n], f1, product[pair][:, n], MULT)
             product[pair] = triple
 
         briefs_ops = {}
 
-        def quantize_briefs(half, a, interleave, staged, width=HALF):
+        def quantize_briefs(half, a, staged, width):
             words = keep.tile([P, HALF], U32, name=f"briefs_words{half}{a}", align_bytes=64)
             scales = keep.tile([P, HALF], U8, name=f"briefs_scales{half}{a}", align_bytes=64)
             for lo in range(0, HALF, width):
                 cols = slice(lo, lo + width)
-                interleave[lo // width](briefs_raw[half, a][:, :, cols], staged[:, cols, :])
+                interleave_on_scalar(briefs_raw[half, a][:, :, cols], staged[:, cols, :])
                 quantize(staged[:, cols, :], words[:, cols], scales[:, cols])
             briefs_ops[half, a] = words, scales
 
-        def quantize_briefs_together(half, interleave):
+        def quantize_briefs_together(half):
             staged = reuse.tile([P, PASSES, HALF, SLOTS], BF16, name="staged_both", tag="buffer8_2", align_bytes=64)
             words = keep.tile([P, PASSES, HALF], U32, name=f"briefs_words{half}", align_bytes=64)
             scales = keep.tile([P, PASSES, HALF], U8, name=f"briefs_scales{half}", align_bytes=64)
             for a in range(PASSES):
-                interleave(briefs_raw[half, a][:], staged[:, a])
+                interleave_on_scalar(briefs_raw[half, a][:], staged[:, a])
                 briefs_ops[half, a] = words[:, a], scales[:, a]
-            quantize(staged[:].rearrange("p a c i -> p (a c) i"), words[:].rearrange("p a c -> p (a c)"), scales[:].rearrange("p a c -> p (a c)"))
+            quantize(
+                staged[:].rearrange("p a c i -> p (a c) i"),
+                words[:].rearrange("p a c -> p (a c)"),
+                scales[:].rearrange("p a c -> p (a c)"),
+            )
 
         h = {}
 
@@ -318,12 +293,12 @@ def tile_list_translator_brief_scores_kernel(
             d_acc, d = [], []
             for n in range(HALF_BLOCKS):
                 cols = slice(n * P, (n + 1) * P)
-                d_acc.append(bank(SLOTS + n, [P, H]))
+                d_acc.append(bank(1 + n, [P, H]))
                 mx_sum(d_acc[n], [(words[:, cols].bitcast(FP8X4), scales[:, cols]) for words, scales in ops], w4_ops)
-            h_acc = [bank(i, [P, HALF_BLOCKS, P]) for i in range(SLOTS)]
+            h_acc = [bank(4 + i if i else 0, [P, HALF_BLOCKS, P]) for i in range(SLOTS)]
             for n in range(HALF_BLOCKS):
                 d.append(reuse.tile([P, SLOTS, P], F32, name="d", tag=f"f3_{n}"))
-                copy = nc.vector.tensor_copy if (half, n) in VECTOR_FETCHES_D else nc.scalar.copy
+                copy = nc.vector.tensor_copy if half == 0 and n % 2 else nc.scalar.copy
                 copy(d[n][:], by_slot(d_acc[n]))
             rows = buffer8(half, [P, SLOTS, HALF], f"h{half}")
             for i in range(SLOTS):
@@ -337,13 +312,9 @@ def tile_list_translator_brief_scores_kernel(
                 nc.scalar.copy(rows[:, i, :], h_acc[i][:].rearrange("p n j -> p (n j)"))
             h[half] = rows
 
-        def amend(i, lo, hi):
-            half, at = divmod(lo, HALF)
-            first, rows = [(a, w) for a, b, w in weight[i] if a <= lo and hi <= b][0]
-            nc.vector.tensor_tensor(
-                page[i][:].indirect(entries(idx3, lo, hi)), h[half][:, i, at : at + hi - lo],
-                rows[:, lo - first : hi - first], MULT,
-            )
+        def amend(i, half):
+            window = page[i][:].indirect(entries(idx3, half * HALF, (half + 1) * HALF))
+            nc.vector.tensor_tensor(window, h[half][:, i, :], weight[i, half], MULT)
 
         w1_ops = [quantize_weight(w1_raw[0], "w1_0", interleave_on_vector)]
         for b in range(BLOCKS):
@@ -352,8 +323,8 @@ def tile_list_translator_brief_scores_kernel(
         for b in range(BLOCKS):
             times_f2(b)
         w4_ops = [quantize_weight(w4_raw[a], f"w4_{a}", interleave_on_scalar) for a in range(PASSES)]
-        quantize_briefs(0, 0, [interleave_on_scalar], reuse.tile([P, BANK, SLOTS], BF16, name="staged", tag="late", align_bytes=64))
-        quantize_briefs(0, 1, [interleave_on_scalar] * 2, staging(), QUARTER)
+        quantize_briefs(0, 0, reuse.tile([P, BANK, SLOTS], BF16, name="staged", tag="late", align_bytes=64), HALF)
+        quantize_briefs(0, 1, staging(), QUARTER)
         late = reuse.tile([P, 2, 2, SLOTS, P], F32, name="late", tag="late", align_bytes=64)
         for pair in range(BLOCKS // 2):
             times_f1(pair, product[pair] if pair < 2 else late[:, pair - 2])
@@ -361,18 +332,22 @@ def tile_list_translator_brief_scores_kernel(
         picked2_scales = keep.tile([P, S2], U8, name="picked2_scales", align_bytes=64)
         nc.vector.tensor_copy(picked2_scales[:], tab2_scale_rows[:].indirect(idx2[:]))
         for q in range(QUADRANTS):
-            nc.sync.dma_start(v2_scales[32 * q : 32 * q + SCALE_ROWS].bitcast(I32), picked2_scales[32 * q : 32 * (q + 1) : 8].bitcast(I32))
-        quantize_briefs_together(1, interleave_on_scalar)
+            nc.sync.dma_start(
+                v2_scales[32 * q : 32 * q + SCALE_ROWS].bitcast(I32),
+                picked2_scales[32 * q : 32 * (q + 1) : 8].bitcast(I32),
+            )
+        quantize_briefs_together(1)
         features(1)
         for i in range(SLOTS):
-            amend(i, 0, HALF)
+            amend(i, 0)
 
         v2_words = keep.tile([P, S2], U32, name="v2_words", align_bytes=64)
         pairs = [
-            reuse.tile([P, 2, 2, BANK, 2], BF16, name=f"pairs{c}", tag=f"tab{c}", align_bytes=64) for c in range(CHUNKS // 2)
+            reuse.tile([P, 2, 2, BANK, 2], BF16, name=f"pairs{u}", tag=f"tab{u}", align_bytes=64)
+            for u in range(CHUNKS // 2)
         ]
         for i in range(SLOTS):
-            amend(i, HALF, S)
+            amend(i, 1)
             for c in range(CHUNKS):
                 nc.scalar.copy(pairs[c // 2][:, c % 2, i // 2, :, i % 2], page[i][:, c * BANK : (c + 1) * BANK])
         nc.vector.tensor_copy(v2_words[:], tab2[:].indirect(idx2[:]))
@@ -381,10 +356,11 @@ def tile_list_translator_brief_scores_kernel(
         for step in range(CHUNKS + 1):
             if step < CHUNKS:
                 page_staged.append(staging())
-                copy = nc.scalar.copy if step == CHUNKS - 1 and SCALAR_WEAVES else nc.vector.tensor_copy
+                copy = nc.scalar.copy if step == CHUNKS - 1 else nc.vector.tensor_copy
+                words = pairs[step // 2][:, step % 2].rearrange("p u c n -> p u (c n)").bitcast(F32)
                 copy(
                     page_staged[step][:].rearrange("p c i -> p (c i)").bitcast(F32).rearrange("p (c u) -> p c u", u=2),
-                    pairs[step // 2][:, step % 2].rearrange("p u c n -> p u (c n)").bitcast(F32).rearrange("p u c -> p c u"),
+                    words.rearrange("p u c -> p c u"),
                 )
             if step > 0:
                 page_ops.append(moving_operand(f"page_{step - 1}"))
@@ -392,67 +368,58 @@ def tile_list_translator_brief_scores_kernel(
 
         e, x, inverse = {}, {}, {}
 
-        def score(g, c):
+        def vector_empties(g, c):
+            return g == 1 or g * CHUNKS + c >= GROUPS * CHUNKS - VECTOR_LAST_BANKS
+
+        def scores(g):
             rows = slice(g * P, (g + 1) * P)
-            if c == 0:
-                e[g] = buffer8(E_BUFFERS[g], [P, T2], f"e{g}")
-            acc = bank(E_BANKS[g][c], [P, BANK])
-            nc.tensor.matmul_mx(
-                out=acc[:], lhsT=v2_words[:, rows].bitcast(FP8X4), lhsT_scale=v2_scales[:, rows],
-                rhs=page_ops[c][0][:].bitcast(FP8X4), rhs_scale=page_ops[c][1][:], start=True, stop=True,
-            )
-            copy = nc.vector.tensor_copy if (g, c) in VECTOR_EMPTIES else nc.scalar.copy
-            copy(e[g][:, c * BANK : (c + 1) * BANK], acc[:])
-            if c == CHUNKS - 1:
-                pick(g)
+            e[g] = buffer8(2 + g, [P, T2], f"e{g}")
+            for c in range(CHUNKS):
+                acc = bank(CHUNKS * (g % 2) + (c + 2 * (g // 2)) % CHUNKS, [P, BANK])
+                nc.tensor.matmul_mx(
+                    out=acc[:], lhsT=v2_words[:, rows].bitcast(FP8X4), lhsT_scale=v2_scales[:, rows],
+                    rhs=page_ops[c][0][:].bitcast(FP8X4), rhs_scale=page_ops[c][1][:], start=True, stop=True,
+                )
+                copy = nc.vector.tensor_copy if vector_empties(g, c) else nc.scalar.copy
+                copy(e[g][:, c * BANK : (c + 1) * BANK], acc[:])
 
         def pick(g):
             if g % 2 == 0:
                 both = buffer8(6 + g // 2, [P, 2, S], "x")
                 x[g], x[g + 1] = both[:, 0, :], both[:, 1, :]
-            for group, lo, hi in PICKS:
-                if group == g:
-                    nc.vector.tensor_copy(x[g][:, lo:hi], e[g][:].indirect(entries(idx4, lo, hi)))
+            for lo in (0, HALF):
+                nc.vector.tensor_copy(x[g][:, lo : lo + HALF], e[g][:].indirect(entries(idx4, lo, lo + HALF)))
 
         def magnitude(g, lo, hi):
             if lo == 0:
                 inverse[g] = reuse.tile([P, S], F32, name="inverse", tag="product", bufs=BLOCKS // 2)
-            if (g, lo) in ABS_ON_VECTOR:
-                nc.vector.scalar_tensor_tensor(inverse[g][:, lo:hi], x[g][:, lo:hi], -1.0, x[g][:, lo:hi], MULT, MAX)
-            else:
-                nc.scalar.activation(inverse[g][:, lo:hi], x[g][:, lo:hi], ACT.Abs)
+            nc.scalar.activation(inverse[g][:, lo:hi], x[g][:, lo:hi], ACT.Abs)
 
         def inverse_root(g, lo, hi):
             part = inverse[g][:, lo:hi]
-            if (g, lo) in BOTH_ON_GPSIMD:
-                nc.scalar.activation(part, part, ACT.Abs_reciprocal_sqrt, bias=room_col[:, g : g + 1])
-            else:
-                nc.scalar.activation(part, part, ACT.Abs_reciprocal_sqrt, bias=unit_room[:, g : g + 1], scale=unit[:, g : g + 1])
+            nc.scalar.activation(
+                part, part, ACT.Abs_reciprocal_sqrt, bias=unit_room[:, g : g + 1], scale=unit[:, g : g + 1]
+            )
 
         def finish(g, lo, hi):
-            rows, part = slice(g * P, (g + 1) * P), inverse[g][:, lo:hi]
-            engine = nc.gpsimd if (g, lo) in ON_GPSIMD else nc.vector
-            if (g, lo) in BOTH_ON_GPSIMD:
-                engine = nc.gpsimd
-                engine.tensor_tensor(x[g][:, lo:hi], x[g][:, lo:hi], part, MULT)
-            elif (g, lo) in TWO_PRODUCTS:
-                nc.vector.scalar_tensor_tensor(x[g][:, lo:hi], x[g][:, lo:hi], unit[:, g : g + 1], part, MULT, MULT)
+            rows, part, piece = slice(g * P, (g + 1) * P), inverse[g][:, lo:hi], x[g][:, lo:hi]
+            if (g, lo, hi) in TWO_PRODUCTS:
+                nc.vector.scalar_tensor_tensor(piece, piece, unit[:, g : g + 1], part, MULT, MULT)
             else:
                 nc.scalar.activation(part, part, ACT.Square, scale=root[:, g : g + 1])
-            engine.tensor_tensor(x[g][:, lo:hi], x[g][:, lo:hi], part, MULT)
-            if g >= WHOLE_ROWS:
-                nc.sync.dma_start(out[rows, lo:hi], x[g][:, lo:hi])
+            engine = nc.gpsimd if g < GPSIMD_GROUPS else nc.vector
+            engine.tensor_tensor(piece, piece, part, MULT)
+            if g == GROUPS - 1:
+                nc.sync.dma_start(out[rows, lo:hi], piece)
             elif hi == S:
                 nc.sync.dma_start(out[rows, :], x[g])
 
-        banks_of_e = [(g, c) for g in range(GROUPS) for c in range(CHUNKS)]
-        for g, c in banks_of_e[:BANKS_AHEAD]:
-            score(g, c)
+        for g in range(GROUPS):
+            scores(g)
+            pick(g)
         for step in range(len(PIECES) + 2):
             if step < len(PIECES):
                 magnitude(*PIECES[step])
-            for g, c in banks_of_e[BANKS_AHEAD + BANKS_A_STEP * step : BANKS_AHEAD + BANKS_A_STEP * (step + 1)]:
-                score(g, c)
             if 1 <= step <= len(PIECES):
                 inverse_root(*PIECES[step - 1])
             if step >= 2:

@@ -117,6 +117,8 @@ def tile_list_translator_brief_scores_kernel(
         def by_slot(acc):
             return acc[:].rearrange("j (p i) -> j i p", i=SLOTS)
 
+        room_rows = keep.tile([P, P], F32, name="room_rows")
+        nc.vector.memset(room_rows[:], 0.0)
         tab_scale_rows = zeroed_scales([P, T], "tab_scale_rows")
         w3_scale_rows = zeroed_scales([P, PASSES, H], "w3_scale_rows")
         w2_scale_rows = zeroed_scales([P, PASSES, H], "w2_scale_rows")
@@ -126,15 +128,17 @@ def tile_list_translator_brief_scores_kernel(
 
         ident = keep.tile([P, P], F32, name="ident")
         make_identity(nc, ident[:])
+        nc.sync.dma_start(room_rows[:GROUPS], room.rearrange("(g p) -> g p", p=P))
+        room_turned = bank(0, [P, P])
+        nc.tensor.matmul(room_turned[:], room_rows[:], ident[:], start=True, stop=True, is_transpose=True)
         room_col = keep.tile([P, GROUPS], F32, name="room_col")
-        with nc.allow_non_contiguous_dma(reason="one value of room for each partition and group"):
-            nc.gpsimd.dma_start(room_col[:], room.rearrange("(g p) -> p g", p=P))
         load_scale_rows(nc.gpsimd, w2_scale_rows, w2_scales)
 
         root = keep.tile([P, GROUPS], F32, name="root")
         unit = keep.tile([P, GROUPS], F32, name="unit")
         unit_room = keep.tile([P, GROUPS], F32, name="unit_room")
-        nc.scalar.activation(root[:], room_col[:], ACT.Abs_reciprocal_sqrt)
+        nc.scalar.activation(root[:], room_turned[:, :GROUPS], ACT.Abs_reciprocal_sqrt)
+        nc.scalar.copy(room_col[:], room_turned[:, :GROUPS])
         nc.gpsimd.tensor_tensor(unit[:], root[:], root[:], MULT)
         nc.gpsimd.tensor_tensor(unit_room[:], unit[:], room_col[:], MULT)
 

@@ -144,24 +144,28 @@ def tile_list_translator_brief_scores_kernel(
 
         wgs_rows = keep.tile([P, HALF], F32, name="wgs_rows0")
         nc.sync.dma_start(wgs_rows[:], wgs[:, :HALF])
-        tab = [reuse.tile([P, T], U32, name=f"tab{a}", tag=f"tab{a}", align_bytes=64) for a in range(PASSES)]
-        load_words(tab[0][:], tab_words[0])
-        idx = load_list(offs, "idx")
         for q in HALVES_IN_TURN:
             nc.sync.dma_start(
                 tab_scale_rows[32 * q : 32 * q + PASSES * SCALE_ROWS].bitcast(I32),
                 tab_scales[:, SCALE_ROWS * q : SCALE_ROWS * (q + 1), :].bitcast(I32),
             )
+        idx = load_list(offs, "idx")
+        tab = [reuse.tile([P, T], U32, name=f"tab{a}", tag=f"tab{a}", align_bytes=64) for a in range(PASSES)]
+        load_words(tab[0][:], tab_words[0])
+        idx2 = load_list(offs2, "idx2")
+        nc.sync.dma_start(tab2_scale_rows[0:P:8].bitcast(I32), tab2_scales[0].bitcast(I32))
         w3_codes = keep.tile([P, PASSES, H], U32, name="w3_codes", align_bytes=64)
         nc.sync.dma_start(w3_codes[:].bitcast(I32), w3_words.rearrange("a p c i -> p a (c i)").bitcast(I32))
-        load_scale_rows(nc.sync, w3_scale_rows, w3_scales)
         load_words(tab[1][:], tab_words[1])
-        w1_raw = [load_pass(0, w1[:K_PASS, :], "w1_raw0")]
+        load_scale_rows(nc.sync, w3_scale_rows, w3_scales)
+        w1_raw = [load_pass(a, w1[a * K_PASS : (a + 1) * K_PASS, :], f"w1_raw{a}") for a in range(PASSES)]
 
         v_words = [keep.tile([P, S], U32, name=f"v_words{a}", align_bytes=64) for a in range(PASSES)]
         v_scales = keep.tile([P, S], U8, name="v_scales", align_bytes=64)
-        nc.vector.tensor_copy(v_words[0][:], tab[0][:].indirect(idx[:]))
         nc.vector.tensor_copy(v_scales[:], tab_scale_rows[:].indirect(idx[:]))
+        nc.vector.tensor_copy(v_words[0][:], tab[0][:].indirect(idx[:]))
+        picked2_scales = keep.tile([P, S2], U8, name="picked2_scales", align_bytes=64)
+        nc.vector.tensor_copy(picked2_scales[:], tab2_scale_rows[:].indirect(idx2[:]))
         for lo in (0, HALF):
             nc.vector.tensor_copy(v_words[1][:, lo : lo + HALF], tab[1][:].indirect(entries(idx, lo, lo + HALF)))
 
@@ -170,7 +174,6 @@ def tile_list_translator_brief_scores_kernel(
                 v_scales_raised[32 * q : 32 * q + SCALE_ROWS].bitcast(I32),
                 v_scales[32 * q + SCALE_ROWS : 32 * q + 2 * SCALE_ROWS].bitcast(I32),
             )
-        w1_raw.append(load_pass(1, w1[K_PASS:, :], "w1_raw1"))
         w2_codes = keep.tile([P, PASSES, 2 * H], U8, name="w2_codes", align_bytes=64)
         nc.sync.dma_start(w2_codes[:].bitcast(I32), w2_words.rearrange("a p c -> p a c").bitcast(I32))
 
@@ -216,8 +219,6 @@ def tile_list_translator_brief_scores_kernel(
         load_briefs(0)
         idx3 = load_list(offs3, "idx3")
         load_page(0)
-        idx2 = load_list(offs2, "idx2")
-        nc.sync.dma_start(tab2_scale_rows[0:P:8].bitcast(I32), tab2_scales[0].bitcast(I32))
         load_page(1)
         load_briefs(1)
         load_page(2)
@@ -231,6 +232,7 @@ def tile_list_translator_brief_scores_kernel(
         w2_ops = [(w2_codes[:, a, :].bitcast(FP4X4), w2_scale_rows[:, a, :]) for a in range(PASSES)]
         w3_ops = [(w3_codes[:, a, :].bitcast(FP8X4), w3_scale_rows[:, a, :]) for a in range(PASSES)]
         product = {}
+        triple = {}
 
         def table_sum(b, w_ops, second_scales, bank_number):
             cols = slice(b * P, (b + 1) * P)
@@ -259,21 +261,20 @@ def tile_list_translator_brief_scores_kernel(
             quantize(staged[:], words, scales)
             return words[:].bitcast(FP8X4), scales[:]
 
-        def times_f1(pair, triple):
-            for n in range(2):
-                b = 2 * pair + n
-                f1 = table_sum(b, w1_ops, v_scales[SCALE_ROWS:P], 4 + b % HALF_BLOCKS)
-                nc.vector.tensor_tensor(triple[:, n], f1, product[pair][:, n], MULT)
-            product[pair] = triple
+        def times_f1(b, triples):
+            f1 = table_sum(b, w1_ops, v_scales[SCALE_ROWS:P], 4 + b % HALF_BLOCKS)
+            nc.vector.tensor_tensor(triples[:, b % 2], f1, product[b // 2][:, b % 2], MULT)
+            triple[b] = triples[:, b % 2]
 
         briefs_ops = {}
 
-        def quantize_briefs(half, a, staged, width):
+        def quantize_briefs(half, a, staged, interleaves):
             words = keep.tile([P, HALF], U32, name=f"briefs_words{half}{a}", align_bytes=64)
             scales = keep.tile([P, HALF], U8, name=f"briefs_scales{half}{a}", align_bytes=64)
-            for lo in range(0, HALF, width):
-                cols = slice(lo, lo + width)
-                interleave_on_scalar(briefs_raw[half, a][:, :, cols], staged[:, cols, :])
+            width = HALF // len(interleaves)
+            for n, interleave in enumerate(interleaves):
+                cols = slice(n * width, (n + 1) * width)
+                interleave(briefs_raw[half, a][:, :, cols], staged[:, cols, :])
                 quantize(staged[:, cols, :], words[:, cols], scales[:, cols])
             briefs_ops[half, a] = words, scales
 
@@ -292,23 +293,26 @@ def tile_list_translator_brief_scores_kernel(
 
         h = {}
 
-        def features(half):
+        def projected(half):
             ops = [briefs_ops[half, a] for a in range(PASSES)]
             d_acc, d = [], []
             for n in range(HALF_BLOCKS):
                 cols = slice(n * P, (n + 1) * P)
                 d_acc.append(bank(1 + n, [P, H]))
                 mx_sum(d_acc[n], [(words[:, cols].bitcast(FP8X4), scales[:, cols]) for words, scales in ops], w4_ops)
-            h_acc = [bank(4 + i if i else 0, [P, HALF_BLOCKS, P]) for i in range(SLOTS)]
             for n in range(HALF_BLOCKS):
                 d.append(reuse.tile([P, SLOTS, P], F32, name="d", tag=f"f3_{n}"))
                 copy = nc.vector.tensor_copy if half == 0 and n % 2 else nc.scalar.copy
                 copy(d[n][:], by_slot(d_acc[n]))
+            return d
+
+        def features(half, d):
+            h_acc = [bank(4 + i if i else 0, [P, HALF_BLOCKS, P]) for i in range(SLOTS)]
             rows = buffer8(half, [P, SLOTS, HALF], f"h{half}")
             for i in range(SLOTS):
                 for n in range(HALF_BLOCKS):
                     b = half * HALF_BLOCKS + n
-                    nc.tensor.matmul(h_acc[i][:, n, :], product[b // 2][:, b % 2, i, :], ident[:],
+                    nc.tensor.matmul(h_acc[i][:, n, :], triple[b][:, i, :], ident[:],
                                      start=(n == 0), stop=False, is_transpose=True)
                 for n in range(HALF_BLOCKS):
                     nc.tensor.matmul(h_acc[i][:, n, :], d[n][:, i, :], ident[:],
@@ -327,21 +331,22 @@ def tile_list_translator_brief_scores_kernel(
         for b in range(BLOCKS):
             times_f2(b)
         w4_ops = [quantize_weight(w4_raw[a], f"w4_{a}", interleave_on_scalar) for a in range(PASSES)]
-        quantize_briefs(0, 0, reuse.tile([P, BANK, SLOTS], BF16, name="staged", tag="late", align_bytes=64), HALF)
-        quantize_briefs(0, 1, staging(), QUARTER)
+        quantize_briefs(0, 0, reuse.tile([P, BANK, SLOTS], BF16, name="staged", tag="late", align_bytes=64), [interleave_on_scalar])
+        quantize_briefs(0, 1, staging(), [interleave_on_vector, interleave_on_scalar])
         late = reuse.tile([P, 2, 2, SLOTS, P], F32, name="late", tag="late", align_bytes=64)
-        for pair in range(BLOCKS // 2):
-            times_f1(pair, product[pair] if pair < 2 else late[:, pair - 2])
-        features(0)
-        picked2_scales = keep.tile([P, S2], U8, name="picked2_scales", align_bytes=64)
-        nc.vector.tensor_copy(picked2_scales[:], tab2_scale_rows[:].indirect(idx2[:]))
+        for b in range(HALF_BLOCKS + 1):
+            times_f1(b, product[b // 2] if b < HALF_BLOCKS else late[:, 0])
+        d = projected(0)
+        for b in range(HALF_BLOCKS + 1, BLOCKS):
+            times_f1(b, late[:, b // 2 - 2])
+        features(0, d)
         for q in range(QUADRANTS):
             nc.sync.dma_start(
                 v2_scales[32 * q : 32 * q + SCALE_ROWS].bitcast(I32),
                 picked2_scales[32 * q : 32 * (q + 1) : 8].bitcast(I32),
             )
         quantize_briefs_together(1)
-        features(1)
+        features(1, projected(1))
         for i in range(SLOTS):
             amend(i, 0)
 

@@ -32,6 +32,7 @@ HALF_BLOCKS = HALF // P
 CHUNKS = T2 // BANK
 GROUPS = S2 // P
 HALVES_IN_TURN = (0, 2, 1, 3)
+SHARE = 256
 LINE = 4
 PIECES = [(g, lo, lo + HALF) for g in range(GROUPS) for lo in (0, HALF)][:-1] + [
     (GROUPS - 1, lo, lo + QUARTER) for lo in (HALF, HALF + QUARTER)
@@ -180,10 +181,17 @@ def tile_list_translator_brief_scores_kernel(
         w4_raw = [load_pass(2 + a, w4[a * K_PASS : (a + 1) * K_PASS, :], f"w4_raw{a}") for a in range(PASSES)]
         briefs_raw, weight, page = {}, {}, {}
 
-        def load_briefs(half):
+        def load_briefs(quarter):
+            raw = buffer8(4 + quarter, [P, PASSES, SLOTS, QUARTER], f"briefs_raw{quarter}")
             for a in range(PASSES):
-                src = briefs[a * K_PASS : (a + 1) * K_PASS, half * HALF : (half + 1) * HALF]
-                briefs_raw[half, a] = load_pass(4 + 2 * half + a, src, f"briefs_raw{half}{a}")
+                src = briefs[a * K_PASS : (a + 1) * K_PASS, quarter * QUARTER : (quarter + 1) * QUARTER]
+                nc.sync.dma_start(raw[:, a], src.rearrange("(p i) c -> p i c", i=SLOTS))
+            briefs_raw[quarter] = raw
+
+        def load_late_briefs():
+            for a in range(PASSES):
+                src = briefs[a * K_PASS : (a + 1) * K_PASS, HALF:]
+                briefs_raw[2 + a] = load_pass(6 + a, src, f"late_briefs_raw{a}")
 
         def load_weight(slots):
             rows = keep.tile([P, len(slots), HALF], F32, name=f"weight1_{slots[0]}")
@@ -217,10 +225,11 @@ def tile_list_translator_brief_scores_kernel(
 
         spread_weight()
         load_briefs(0)
+        load_briefs(1)
         idx3 = load_list(offs3, "idx3")
         load_page(0)
         load_page(1)
-        load_briefs(1)
+        load_late_briefs()
         load_page(2)
         load_page(3)
         load_weight(range(2))
@@ -261,68 +270,83 @@ def tile_list_translator_brief_scores_kernel(
             quantize(staged[:], words, scales)
             return words[:].bitcast(FP8X4), scales[:]
 
-        def times_f1(b, triples):
-            f1 = table_sum(b, w1_ops, v_scales[SCALE_ROWS:P], 4 + b % HALF_BLOCKS)
-            nc.vector.tensor_tensor(triples[:, b % 2], f1, product[b // 2][:, b % 2], MULT)
-            triple[b] = triples[:, b % 2]
+        def times_f1(b, out_tile, bank_number):
+            f1 = table_sum(b, w1_ops, v_scales[SCALE_ROWS:P], bank_number)
+            nc.vector.tensor_tensor(out_tile, f1, product[b // 2][:, b % 2], MULT)
+            triple[b] = out_tile
 
         briefs_ops = {}
 
-        def quantize_briefs(half, a, staged, interleaves):
-            words = keep.tile([P, HALF], U32, name=f"briefs_words{half}{a}", align_bytes=64)
-            scales = keep.tile([P, HALF], U8, name=f"briefs_scales{half}{a}", align_bytes=64)
-            width = HALF // len(interleaves)
-            for n, interleave in enumerate(interleaves):
-                cols = slice(n * width, (n + 1) * width)
-                interleave(briefs_raw[half, a][:, :, cols], staged[:, cols, :])
-                quantize(staged[:, cols, :], words[:, cols], scales[:, cols])
-            briefs_ops[half, a] = words, scales
-
-        def quantize_briefs_together(half):
-            staged = reuse.tile([P, PASSES, HALF, SLOTS], BF16, name="staged_both", tag="buffer8_2", align_bytes=64)
-            words = keep.tile([P, PASSES, HALF], U32, name=f"briefs_words{half}", align_bytes=64)
-            scales = keep.tile([P, PASSES, HALF], U8, name=f"briefs_scales{half}", align_bytes=64)
+        def quantize_briefs(quarter, staged, interleave):
+            words = keep.tile([P, PASSES, QUARTER], U32, name=f"briefs_words{quarter}", align_bytes=64)
+            scales = keep.tile([P, PASSES, QUARTER], U8, name=f"briefs_scales{quarter}", align_bytes=64)
             for a in range(PASSES):
-                interleave_on_scalar(briefs_raw[half, a][:], staged[:, a])
-                briefs_ops[half, a] = words[:, a], scales[:, a]
+                interleave[a](briefs_raw[quarter][:, a], staged[:, a])
             quantize(
                 staged[:].rearrange("p a c i -> p (a c) i"),
                 words[:].rearrange("p a c -> p (a c)"),
                 scales[:].rearrange("p a c -> p (a c)"),
             )
+            briefs_ops[quarter] = words, scales
 
         h = {}
 
-        def projected(half):
-            ops = [briefs_ops[half, a] for a in range(PASSES)]
-            d_acc, d = [], []
+        def features(quarter, fetch):
+            words, scales = briefs_ops[quarter]
+            first_bank = 4 * (quarter % 2)
+            d = []
+            for n in range(2):
+                cols = slice(n * P, (n + 1) * P)
+                acc = bank(first_bank + n, [P, H])
+                mx_sum(acc, [(words[:, a, cols].bitcast(FP8X4), scales[:, a, cols]) for a in range(PASSES)], w4_ops)
+                d.append(reuse.tile([P, SLOTS, P], F32, name="d", tag=f"f3_{2 * quarter + n}"))
+                fetch[n](d[n][:], by_slot(acc))
+            half, lo = quarter // 2, quarter % 2 * QUARTER
+            if lo == 0:
+                h[half] = buffer8(0, [P, SLOTS, HALF], f"h{half}")
+            for u in range(2):
+                acc = bank(first_bank + 2 + u, [P, 2, 2, P])
+                terms = [triple[2 * quarter + n] for n in range(2)] + [d[n][:] for n in range(2)]
+                for k, term in enumerate(terms):
+                    for m in range(2):
+                        nc.tensor.matmul(acc[:, m, k % 2, :], term[:, 2 * u + m, :], ident[:],
+                                         start=(k + m == 0), stop=(k + m == 4), is_transpose=True)
+                nc.scalar.copy(h[half][:, 2 * u : 2 * u + 2, lo : lo + QUARTER], acc[:].rearrange("p m n j -> p m (n j)"))
+
+        def late_features():
+            ops = []
+            for a in range(PASSES):
+                words = keep.tile([P, HALF], U32, name=f"late_words{a}", align_bytes=64)
+                scales = keep.tile([P, HALF], U8, name=f"late_scales{a}", align_bytes=64)
+                staged = staging()
+                if a == 0:
+                    interleave_on_scalar(briefs_raw[2 + a][:], staged[:])
+                else:
+                    interleave_on_scalar(briefs_raw[2 + a][:, :, :SHARE], staged[:, :SHARE, :])
+                    interleave_on_vector(briefs_raw[2 + a][:, :, SHARE:], staged[:, SHARE:, :])
+                quantize(staged[:], words, scales)
+                ops.append((words, scales))
+            d = []
             for n in range(HALF_BLOCKS):
                 cols = slice(n * P, (n + 1) * P)
-                d_acc.append(bank(1 + n, [P, H]))
-                mx_sum(d_acc[n], [(words[:, cols].bitcast(FP8X4), scales[:, cols]) for words, scales in ops], w4_ops)
-            for n in range(HALF_BLOCKS):
-                d.append(reuse.tile([P, SLOTS, P], F32, name="d", tag=f"f3_{n}"))
-                copy = nc.vector.tensor_copy if half == 0 and n % 2 else nc.scalar.copy
-                copy(d[n][:], by_slot(d_acc[n]))
-            return d
-
-        def features(half, d):
-            h_acc = [bank(4 + i if i else 0, [P, HALF_BLOCKS, P]) for i in range(SLOTS)]
-            rows = buffer8(half, [P, SLOTS, HALF], f"h{half}")
+                acc = bank(n, [P, H])
+                mx_sum(acc, [(words[:, cols].bitcast(FP8X4), scales[:, cols]) for words, scales in ops], w4_ops)
+                d.append(reuse.tile([P, SLOTS, P], F32, name="d", tag=f"f3_{HALF_BLOCKS + n}"))
+                nc.scalar.copy(d[n][:], by_slot(acc))
+            h[1] = buffer8(1, [P, SLOTS, HALF], "h1")
             for i in range(SLOTS):
-                for n in range(HALF_BLOCKS):
-                    b = half * HALF_BLOCKS + n
-                    nc.tensor.matmul(h_acc[i][:, n, :], triple[b][:, i, :], ident[:],
-                                     start=(n == 0), stop=False, is_transpose=True)
-                for n in range(HALF_BLOCKS):
-                    nc.tensor.matmul(h_acc[i][:, n, :], d[n][:, i, :], ident[:],
-                                     start=False, stop=(n == HALF_BLOCKS - 1), is_transpose=True)
-                nc.scalar.copy(rows[:, i, :], h_acc[i][:].rearrange("p n j -> p (n j)"))
-            h[half] = rows
+                acc = bank(HALF_BLOCKS + i, [P, HALF_BLOCKS, P])
+                terms = [triple[HALF_BLOCKS + n] for n in range(HALF_BLOCKS)] + [part[:] for part in d]
+                for k, term in enumerate(terms):
+                    nc.tensor.matmul(acc[:, k % HALF_BLOCKS, :], term[:, i, :], ident[:],
+                                     start=(k == 0), stop=(k == len(terms) - 1), is_transpose=True)
+                nc.scalar.copy(h[1][:, i, :], acc[:].rearrange("p n j -> p (n j)"))
 
-        def amend(i, half):
-            window = page[i][:].indirect(entries(idx3, half * HALF, (half + 1) * HALF))
-            nc.vector.tensor_tensor(window, h[half][:, i, :], weight[i, half], MULT)
+        def amend(i, lo, hi):
+            half, first = lo // HALF, lo % HALF
+            cols = slice(first, first + hi - lo)
+            window = page[i][:].indirect(entries(idx3, lo, hi))
+            nc.vector.tensor_tensor(window, h[half][:, i, cols], weight[i, half][:, cols], MULT)
 
         w1_ops = [quantize_weight(w1_raw[0], "w1_0", interleave_on_vector)]
         for b in range(BLOCKS):
@@ -331,24 +355,31 @@ def tile_list_translator_brief_scores_kernel(
         for b in range(BLOCKS):
             times_f2(b)
         w4_ops = [quantize_weight(w4_raw[a], f"w4_{a}", interleave_on_scalar) for a in range(PASSES)]
-        quantize_briefs(0, 0, reuse.tile([P, BANK, SLOTS], BF16, name="staged", tag="late", align_bytes=64), [interleave_on_scalar])
-        quantize_briefs(0, 1, staging(), [interleave_on_vector, interleave_on_scalar])
-        late = reuse.tile([P, 2, 2, SLOTS, P], F32, name="late", tag="late", align_bytes=64)
-        for b in range(HALF_BLOCKS + 1):
-            times_f1(b, product[b // 2] if b < HALF_BLOCKS else late[:, 0])
-        d = projected(0)
-        for b in range(HALF_BLOCKS + 1, BLOCKS):
-            times_f1(b, late[:, b // 2 - 2])
-        features(0, d)
+        shape = [P, PASSES, QUARTER, SLOTS]
+        quantize_briefs(0, reuse.tile(shape, BF16, name="staged", tag="late", align_bytes=64),
+                        (interleave_on_scalar, interleave_on_vector))
+        late = reuse.tile([P, HALF_BLOCKS, SLOTS, P], F32, name="late", tag="late", align_bytes=64)
+        for b in range(2):
+            times_f1(b, product[0][:, b], 4 + b)
+        features(0, (nc.scalar.copy, nc.scalar.copy))
+        for b in range(2, 2 + HALF_BLOCKS):
+            times_f1(b, late[:, b - 2], 4 + b % HALF_BLOCKS)
+        staged = reuse.tile(shape, BF16, name="staged", tag="staged", bufs=3, align_bytes=64)
+        quantize_briefs(1, staged, (interleave_on_scalar, interleave_on_scalar))
+        for b in range(2 + HALF_BLOCKS, BLOCKS):
+            times_f1(b, product[b // 2][:, b % 2], b)
+        features(1, (nc.scalar.copy, nc.scalar.copy))
+        for quarter in range(2):
+            for i in range(2):
+                amend(i, quarter * QUARTER, (quarter + 1) * QUARTER)
         for q in range(QUADRANTS):
             nc.sync.dma_start(
                 v2_scales[32 * q : 32 * q + SCALE_ROWS].bitcast(I32),
                 picked2_scales[32 * q : 32 * (q + 1) : 8].bitcast(I32),
             )
-        quantize_briefs_together(1)
-        features(1, projected(1))
-        for i in range(SLOTS):
-            amend(i, 0)
+        late_features()
+        for i in range(2, SLOTS):
+            amend(i, 0, HALF)
 
         v2_words = keep.tile([P, S2], U32, name="v2_words", align_bytes=64)
         pairs = [
@@ -356,7 +387,7 @@ def tile_list_translator_brief_scores_kernel(
             for u in range(CHUNKS // 2)
         ]
         for i in range(SLOTS):
-            amend(i, 1)
+            amend(i, HALF, S)
             for c in range(CHUNKS):
                 nc.scalar.copy(pairs[c // 2][:, c % 2, i // 2, :, i % 2], page[i][:, c * BANK : (c + 1) * BANK])
         nc.vector.tensor_copy(v2_words[:], tab2[:].indirect(idx2[:]))

@@ -32,7 +32,6 @@ HALF_BLOCKS = HALF // P
 CHUNKS = T2 // BANK
 GROUPS = S2 // P
 HALVES_IN_TURN = (0, 2, 1, 3)
-SHARE = 256
 LINE = 4
 PIECES = [(g, lo, lo + HALF) for g in range(GROUPS) for lo in (0, HALF)][:-1] + [
     (GROUPS - 1, lo, lo + QUARTER) for lo in (HALF, HALF + QUARTER)
@@ -188,11 +187,6 @@ def tile_list_translator_brief_scores_kernel(
                 nc.sync.dma_start(raw[:, a], src.rearrange("(p i) c -> p i c", i=SLOTS))
             briefs_raw[quarter] = raw
 
-        def load_late_briefs():
-            for a in range(PASSES):
-                src = briefs[a * K_PASS : (a + 1) * K_PASS, HALF:]
-                briefs_raw[2 + a] = load_pass(6 + a, src, f"late_briefs_raw{a}")
-
         def load_weight(slots):
             rows = keep.tile([P, len(slots), HALF], F32, name=f"weight1_{slots[0]}")
             src = wgs.rearrange("(p i) j -> p i j", i=SLOTS)[:, slots[0] : slots[-1] + 1, HALF:]
@@ -229,12 +223,13 @@ def tile_list_translator_brief_scores_kernel(
         idx3 = load_list(offs3, "idx3")
         load_page(0)
         load_page(1)
-        load_late_briefs()
+        load_briefs(2)
         load_page(2)
+        load_briefs(3)
         load_page(3)
-        load_weight(range(2))
+        load_weight(range(1))
+        load_weight(range(1, SLOTS))
         tab2 = keep.tile([P, T3], U32, name="tab2", align_bytes=64)
-        load_weight(range(2, SLOTS))
         load_words(tab2[:], tab2_words[0])
         idx4 = load_list(offs4, "idx4")
 
@@ -297,50 +292,25 @@ def tile_list_translator_brief_scores_kernel(
             d = []
             for n in range(2):
                 cols = slice(n * P, (n + 1) * P)
-                acc = bank(first_bank + n, [P, H])
+                acc = bank((0 if quarter >= 2 else first_bank) + n, [P, H])
                 mx_sum(acc, [(words[:, a, cols].bitcast(FP8X4), scales[:, a, cols]) for a in range(PASSES)], w4_ops)
-                d.append(reuse.tile([P, SLOTS, P], F32, name="d", tag=f"f3_{2 * quarter + n}"))
-                fetch[n](d[n][:], by_slot(acc))
+                if quarter == 2:
+                    both = buffer8(7, [P, 2, SLOTS, P], "d") if n == 0 else both
+                    d.append(both[:, n])
+                else:
+                    d.append(reuse.tile([P, SLOTS, P], F32, name="d", tag=f"f3_{2 * quarter + n}")[:])
+                fetch[n](d[n], by_slot(acc))
             half, lo = quarter // 2, quarter % 2 * QUARTER
             if lo == 0:
-                h[half] = buffer8(0, [P, SLOTS, HALF], f"h{half}")
+                h[half] = buffer8(half, [P, SLOTS, HALF], f"h{half}")
             for u in range(2):
                 acc = bank(first_bank + 2 + u, [P, 2, 2, P])
-                terms = [triple[2 * quarter + n] for n in range(2)] + [d[n][:] for n in range(2)]
+                terms = [triple[2 * quarter + n] for n in range(2)] + d
                 for k, term in enumerate(terms):
                     for m in range(2):
                         nc.tensor.matmul(acc[:, m, k % 2, :], term[:, 2 * u + m, :], ident[:],
                                          start=(k + m == 0), stop=(k + m == 4), is_transpose=True)
                 nc.scalar.copy(h[half][:, 2 * u : 2 * u + 2, lo : lo + QUARTER], acc[:].rearrange("p m n j -> p m (n j)"))
-
-        def late_features():
-            ops = []
-            for a in range(PASSES):
-                words = keep.tile([P, HALF], U32, name=f"late_words{a}", align_bytes=64)
-                scales = keep.tile([P, HALF], U8, name=f"late_scales{a}", align_bytes=64)
-                staged = staging()
-                if a == 0:
-                    interleave_on_scalar(briefs_raw[2 + a][:], staged[:])
-                else:
-                    interleave_on_scalar(briefs_raw[2 + a][:, :, :SHARE], staged[:, :SHARE, :])
-                    interleave_on_vector(briefs_raw[2 + a][:, :, SHARE:], staged[:, SHARE:, :])
-                quantize(staged[:], words, scales)
-                ops.append((words, scales))
-            d = []
-            for n in range(HALF_BLOCKS):
-                cols = slice(n * P, (n + 1) * P)
-                acc = bank(n, [P, H])
-                mx_sum(acc, [(words[:, cols].bitcast(FP8X4), scales[:, cols]) for words, scales in ops], w4_ops)
-                d.append(reuse.tile([P, SLOTS, P], F32, name="d", tag=f"f3_{HALF_BLOCKS + n}"))
-                nc.scalar.copy(d[n][:], by_slot(acc))
-            h[1] = buffer8(1, [P, SLOTS, HALF], "h1")
-            for i in range(SLOTS):
-                acc = bank(HALF_BLOCKS + i, [P, HALF_BLOCKS, P])
-                terms = [triple[HALF_BLOCKS + n] for n in range(HALF_BLOCKS)] + [part[:] for part in d]
-                for k, term in enumerate(terms):
-                    nc.tensor.matmul(acc[:, k % HALF_BLOCKS, :], term[:, i, :], ident[:],
-                                     start=(k == 0), stop=(k == len(terms) - 1), is_transpose=True)
-                nc.scalar.copy(h[1][:, i, :], acc[:].rearrange("p n j -> p (n j)"))
 
         def amend(i, lo, hi):
             half, first = lo // HALF, lo % HALF
@@ -377,9 +347,17 @@ def tile_list_translator_brief_scores_kernel(
                 v2_scales[32 * q : 32 * q + SCALE_ROWS].bitcast(I32),
                 picked2_scales[32 * q : 32 * (q + 1) : 8].bitcast(I32),
             )
-        late_features()
-        for i in range(2, SLOTS):
-            amend(i, 0, HALF)
+        amend(2, 0, HALF)
+        for quarter in range(2, 4):
+            staged = reuse.tile(shape, BF16, name="staged", tag="staged", bufs=3, align_bytes=64)
+            quantize_briefs(quarter, staged, (interleave_on_scalar, interleave_on_scalar))
+        for quarter in range(2, 4):
+            features(quarter, (nc.scalar.copy, nc.scalar.copy))
+            if quarter == 2:
+                amend(3, 0, HALF)
+            amend(0, quarter * QUARTER, (quarter + 1) * QUARTER)
+        for i in range(1, SLOTS):
+            amend(i, HALF, S)
 
         v2_words = keep.tile([P, S2], U32, name="v2_words", align_bytes=64)
         pairs = [
@@ -387,7 +365,6 @@ def tile_list_translator_brief_scores_kernel(
             for u in range(CHUNKS // 2)
         ]
         for i in range(SLOTS):
-            amend(i, HALF, S)
             for c in range(CHUNKS):
                 nc.scalar.copy(pairs[c // 2][:, c % 2, i // 2, :, i % 2], page[i][:, c * BANK : (c + 1) * BANK])
         nc.vector.tensor_copy(v2_words[:], tab2[:].indirect(idx2[:]))

@@ -32,13 +32,15 @@ HALF_BLOCKS = HALF // P
 CHUNKS = T2 // BANK
 GROUPS = S2 // P
 HALVES_IN_TURN = (0, 2, 1, 3)
+WARM_UPS = 3
 LINE = 4
 PIECES = [(g, lo, lo + HALF) for g in range(GROUPS) for lo in (0, HALF)][:-1] + [
     (GROUPS - 1, lo, lo + QUARTER) for lo in (HALF, HALF + QUARTER)
 ]
 VECTOR_LAST_BANKS = 3
-GPSIMD_GROUPS = 2
-TWO_PRODUCTS = PIECES[5:7]
+GPSIMD_TWICE = PIECES[:1]
+GPSIMD_ONCE = PIECES[1:4]
+VECTOR_TWICE = PIECES[5:6]
 
 
 def tile_list_translator_brief_scores_kernel(
@@ -108,10 +110,10 @@ def tile_list_translator_brief_scores_kernel(
             )
 
         def mx_sum(acc, lhs, rhs):
-            for a in range(PASSES):
+            for a in range(len(rhs)):
                 nc.tensor.matmul_mx(
                     out=acc[:], lhsT=lhs[a][0], lhsT_scale=lhs[a][1], rhs=rhs[a][0], rhs_scale=rhs[a][1],
-                    start=(a == 0), stop=(a == PASSES - 1),
+                    start=(a == 0), stop=(a == len(rhs) - 1),
                 )
 
         def by_slot(acc):
@@ -228,10 +230,16 @@ def tile_list_translator_brief_scores_kernel(
         load_briefs(3)
         load_page(3)
         load_weight(range(1))
-        load_weight(range(1, SLOTS))
+        load_weight(range(1, 2))
+        load_weight(range(2, SLOTS))
         tab2 = keep.tile([P, T3], U32, name="tab2", align_bytes=64)
         load_words(tab2[:], tab2_words[0])
         idx4 = load_list(offs4, "idx4")
+        for q in range(QUADRANTS):
+            nc.sync.dma_start(
+                v2_scales[32 * q : 32 * q + SCALE_ROWS].bitcast(I32),
+                picked2_scales[32 * q : 32 * (q + 1) : 8].bitcast(I32),
+            )
 
         w2_ops = [(w2_codes[:, a, :].bitcast(FP4X4), w2_scale_rows[:, a, :]) for a in range(PASSES)]
         w3_ops = [(w3_codes[:, a, :].bitcast(FP8X4), w3_scale_rows[:, a, :]) for a in range(PASSES)]
@@ -258,11 +266,14 @@ def tile_list_translator_brief_scores_kernel(
             f2 = table_sum(b, w2_ops, v_scales_raised, b)
             nc.vector.tensor_tensor(product[b // 2][:, b % 2], f2, f3[b][:], MULT)
 
-        def quantize_weight(raw, name, interleave):
+        def quantize_weight(raw, name, interleave, parts=1):
             words, scales = moving_operand(name)
             staged = staging()
-            interleave(raw[:], staged[:])
-            quantize(staged[:], words, scales)
+            pieces = [slice(lo, lo + BANK // parts) for lo in range(0, BANK, BANK // parts)]
+            for cols in pieces:
+                interleave(raw[:, :, cols], staged[:, cols, :])
+            for cols in pieces:
+                quantize(staged[:, cols, :], words[:, cols], scales[:, cols])
             return words[:].bitcast(FP8X4), scales[:]
 
         def times_f1(b, out_tile, bank_number):
@@ -318,16 +329,16 @@ def tile_list_translator_brief_scores_kernel(
             window = page[i][:].indirect(entries(idx3, lo, hi))
             nc.vector.tensor_tensor(window, h[half][:, i, cols], weight[i, half][:, cols], MULT)
 
-        w1_ops = [quantize_weight(w1_raw[0], "w1_0", interleave_on_vector)]
+        w1_ops = [quantize_weight(w1_raw[0], "w1_0", interleave_on_vector, 2)]
         for b in range(BLOCKS):
             fetch_f3(b)
-        w1_ops.append(quantize_weight(w1_raw[1], "w1_1", interleave_on_vector))
+        w1_ops.append(quantize_weight(w1_raw[1], "w1_1", interleave_on_vector, 2))
         for b in range(BLOCKS):
             times_f2(b)
         w4_ops = [quantize_weight(w4_raw[a], f"w4_{a}", interleave_on_scalar) for a in range(PASSES)]
         shape = [P, PASSES, QUARTER, SLOTS]
         quantize_briefs(0, reuse.tile(shape, BF16, name="staged", tag="late", align_bytes=64),
-                        (interleave_on_scalar, interleave_on_vector))
+                        (interleave_on_vector, interleave_on_scalar))
         late = reuse.tile([P, HALF_BLOCKS, SLOTS, P], F32, name="late", tag="late", align_bytes=64)
         for b in range(2):
             times_f1(b, product[0][:, b], 4 + b)
@@ -342,11 +353,6 @@ def tile_list_translator_brief_scores_kernel(
         for quarter in range(2):
             for i in range(2):
                 amend(i, quarter * QUARTER, (quarter + 1) * QUARTER)
-        for q in range(QUADRANTS):
-            nc.sync.dma_start(
-                v2_scales[32 * q : 32 * q + SCALE_ROWS].bitcast(I32),
-                picked2_scales[32 * q : 32 * (q + 1) : 8].bitcast(I32),
-            )
         amend(2, 0, HALF)
         for quarter in range(2, 4):
             staged = reuse.tile(shape, BF16, name="staged", tag="staged", bufs=3, align_bytes=64)
@@ -368,6 +374,9 @@ def tile_list_translator_brief_scores_kernel(
             for c in range(CHUNKS):
                 nc.scalar.copy(pairs[c // 2][:, c % 2, i // 2, :, i % 2], page[i][:, c * BANK : (c + 1) * BANK])
         nc.vector.tensor_copy(v2_words[:], tab2[:].indirect(idx2[:]))
+
+        warm = bank(CHUNKS - 1, [P, BANK])
+        mx_sum(warm, [(v2_words[:, :P].bitcast(FP8X4), v2_scales[:, :P])] * WARM_UPS, w4_ops[:1] * WARM_UPS)
 
         page_staged, page_ops = [], []
         for step in range(CHUNKS + 1):
@@ -414,19 +423,22 @@ def tile_list_translator_brief_scores_kernel(
 
         def inverse_root(g, lo, hi):
             part = inverse[g][:, lo:hi]
-            nc.scalar.activation(
-                part, part, ACT.Abs_reciprocal_sqrt, bias=unit_room[:, g : g + 1], scale=unit[:, g : g + 1]
-            )
+            if (g, lo, hi) in GPSIMD_TWICE + VECTOR_TWICE:
+                nc.scalar.activation(part, part, ACT.Abs_reciprocal_sqrt, bias=room_col[:, g : g + 1])
+            else:
+                nc.scalar.activation(
+                    part, part, ACT.Abs_reciprocal_sqrt, bias=unit_room[:, g : g + 1], scale=unit[:, g : g + 1]
+                )
 
         def finish(g, lo, hi):
             rows, part, piece = slice(g * P, (g + 1) * P), inverse[g][:, lo:hi], x[g][:, lo:hi]
-            if (g, lo, hi) in TWO_PRODUCTS:
-                nc.vector.scalar_tensor_tensor(piece, piece, unit[:, g : g + 1], part, MULT, MULT)
+            engine = nc.gpsimd if (g, lo, hi) in GPSIMD_TWICE + GPSIMD_ONCE else nc.vector
+            if (g, lo, hi) in GPSIMD_TWICE + VECTOR_TWICE:
+                engine.tensor_tensor(piece, piece, part, MULT)
             else:
                 nc.scalar.activation(part, part, ACT.Square, scale=root[:, g : g + 1])
-            engine = nc.gpsimd if g < GPSIMD_GROUPS else nc.vector
             engine.tensor_tensor(piece, piece, part, MULT)
-            if g == GROUPS - 1:
+            if g >= 2:
                 nc.sync.dma_start(out[rows, lo:hi], piece)
             elif hi == S:
                 nc.sync.dma_start(out[rows, :], x[g])

@@ -33,6 +33,7 @@ CHUNKS = T2 // BANK
 GROUPS = S2 // P
 HALVES_IN_TURN = (0, 2, 1, 3)
 WARM_UPS = 3
+KEEP = 2
 LINE = 4
 PIECES = [(g, lo, lo + HALF) for g in range(GROUPS) for lo in (0, HALF)][:-1] + [
     (GROUPS - 1, lo, lo + QUARTER) for lo in (HALF, HALF + QUARTER)
@@ -295,6 +296,7 @@ def tile_list_translator_brief_scores_kernel(
             )
             briefs_ops[quarter] = words, scales
 
+        d_blocks = []
         h = {}
 
         def features(quarter, fetch):
@@ -311,10 +313,13 @@ def tile_list_translator_brief_scores_kernel(
                 else:
                     d.append(reuse.tile([P, SLOTS, P], F32, name="d", tag=f"f3_{2 * quarter + n}")[:])
                 fetch[n](d[n], by_slot(acc))
+            if quarter == 2:
+                mx_sum(bank(4, [P, H]), [(words[:, 0, :P].bitcast(FP8X4), scales[:, 0, :P])] * KEEP, w4_ops[:1] * KEEP)
             half, lo = quarter // 2, quarter % 2 * QUARTER
             if lo == 0:
                 h[half] = buffer8(half, [P, SLOTS, HALF], f"h{half}")
-            for u in range(2):
+            d_blocks.extend(d)
+            for u in range(2 if half == 0 else 1):
                 acc = bank(first_bank + 2 + u, [P, 2, 2, P])
                 terms = [triple[2 * quarter + n] for n in range(2)] + d
                 for k, term in enumerate(terms):
@@ -322,6 +327,14 @@ def tile_list_translator_brief_scores_kernel(
                         nc.tensor.matmul(acc[:, m, k % 2, :], term[:, 2 * u + m, :], ident[:],
                                          start=(k + m == 0), stop=(k + m == 4), is_transpose=True)
                 nc.scalar.copy(h[half][:, 2 * u : 2 * u + 2, lo : lo + QUARTER], acc[:].rearrange("p m n j -> p m (n j)"))
+
+        def late_slot(i):
+            acc = bank(4 * i - 5, [P, HALF_BLOCKS, P])
+            terms = [triple[HALF_BLOCKS + n] for n in range(HALF_BLOCKS)] + d_blocks[HALF_BLOCKS:]
+            for k, term in enumerate(terms):
+                nc.tensor.matmul(acc[:, k % HALF_BLOCKS, :], term[:, i, :], ident[:],
+                                 start=(k == 0), stop=(k == len(terms) - 1), is_transpose=True)
+            nc.scalar.copy(h[1][:, i, :], acc[:].rearrange("p n j -> p (n j)"))
 
         def amend(i, lo, hi):
             half, first = lo // HALF, lo % HALF
@@ -362,6 +375,8 @@ def tile_list_translator_brief_scores_kernel(
             if quarter == 2:
                 amend(3, 0, HALF)
             amend(0, quarter * QUARTER, (quarter + 1) * QUARTER)
+        for i in range(2, SLOTS):
+            late_slot(i)
         for i in range(1, SLOTS):
             amend(i, HALF, S)
 

@@ -32,15 +32,13 @@ HALF_BLOCKS = HALF // P
 CHUNKS = T2 // BANK
 GROUPS = S2 // P
 HALVES_IN_TURN = (0, 2, 1, 3)
-WARM_UPS = 3
-KEEP = 2
 LINE = 4
 PIECES = [(g, lo, lo + HALF) for g in range(GROUPS) for lo in (0, HALF)][:-1] + [
     (GROUPS - 1, lo, lo + QUARTER) for lo in (HALF, HALF + QUARTER)
 ]
 VECTOR_LAST_BANKS = 3
 GPSIMD_TWICE = PIECES[:1]
-GPSIMD_ONCE = PIECES[1:4]
+GPSIMD_ONCE = PIECES[1:3]
 VECTOR_TWICE = PIECES[5:6]
 
 
@@ -60,8 +58,8 @@ def tile_list_translator_brief_scores_kernel(
         def bank(number, shape):
             return psum.tile(shape, F32, name=f"bank{number}", tag=f"bank{number}")
 
-        def staging():
-            return reuse.tile([P, BANK, SLOTS], BF16, name="staged", tag="staged", bufs=3, align_bytes=64)
+        def staging(shape=(P, BANK, SLOTS)):
+            return reuse.tile(list(shape), BF16, name="staged", tag="staged", bufs=3, align_bytes=64)
 
         def moving_operand(name):
             words = reuse.tile([P, BANK], U32, name=name + "_words", tag="moving_words", bufs=4, align_bytes=64)
@@ -105,16 +103,20 @@ def tile_list_translator_brief_scores_kernel(
         def interleave_on_vector(raw, staged):
             nc.vector.tensor_copy(staged, raw.rearrange("p i c -> p c i"))
 
+        def interleave_on_both(raw, staged):
+            interleave_on_scalar(raw[:, :, :P], staged[:, :P, :])
+            interleave_on_vector(raw[:, :, P:], staged[:, P:, :])
+
         def quantize(staged, words, scales):
             nc.vector.quantize_mx(
                 out=words[:].bitcast(FP8X4), scales=scales[:], in_=staged.rearrange("p c i -> p (c i)")
             )
 
         def mx_sum(acc, lhs, rhs):
-            for a in range(len(rhs)):
+            for a in range(PASSES):
                 nc.tensor.matmul_mx(
                     out=acc[:], lhsT=lhs[a][0], lhsT_scale=lhs[a][1], rhs=rhs[a][0], rhs_scale=rhs[a][1],
-                    start=(a == 0), stop=(a == len(rhs) - 1),
+                    start=(a == 0), stop=(a == PASSES - 1),
                 )
 
         def by_slot(acc):
@@ -230,9 +232,8 @@ def tile_list_translator_brief_scores_kernel(
         load_page(2)
         load_briefs(3)
         load_page(3)
-        load_weight(range(1))
-        load_weight(range(1, 2))
-        load_weight(range(2, SLOTS))
+        for slots in (range(0, 1), range(1, 2), range(2, SLOTS)):
+            load_weight(slots)
         tab2 = keep.tile([P, T3], U32, name="tab2", align_bytes=64)
         load_words(tab2[:], tab2_words[0])
         idx4 = load_list(offs4, "idx4")
@@ -277,8 +278,8 @@ def tile_list_translator_brief_scores_kernel(
                 quantize(staged[:, cols, :], words[:, cols], scales[:, cols])
             return words[:].bitcast(FP8X4), scales[:]
 
-        def times_f1(b, out_tile, bank_number):
-            f1 = table_sum(b, w1_ops, v_scales[SCALE_ROWS:P], bank_number)
+        def times_f1(b, out_tile):
+            f1 = table_sum(b, w1_ops, v_scales[SCALE_ROWS:P], 4 + b % HALF_BLOCKS)
             nc.vector.tensor_tensor(out_tile, f1, product[b // 2][:, b % 2], MULT)
             triple[b] = out_tile
 
@@ -296,41 +297,37 @@ def tile_list_translator_brief_scores_kernel(
             )
             briefs_ops[quarter] = words, scales
 
-        d_blocks = []
+        d = {}
         h = {}
 
-        def features(quarter, fetch):
+        def features(quarter):
             words, scales = briefs_ops[quarter]
-            first_bank = 4 * (quarter % 2)
-            d = []
-            for n in range(2):
-                cols = slice(n * P, (n + 1) * P)
-                acc = bank((0 if quarter >= 2 else first_bank) + n, [P, H])
-                mx_sum(acc, [(words[:, a, cols].bitcast(FP8X4), scales[:, a, cols]) for a in range(PASSES)], w4_ops)
-                if quarter == 2:
-                    both = buffer8(7, [P, 2, SLOTS, P], "d") if n == 0 else both
-                    d.append(both[:, n])
-                else:
-                    d.append(reuse.tile([P, SLOTS, P], F32, name="d", tag=f"f3_{2 * quarter + n}")[:])
-                fetch[n](d[n], by_slot(acc))
+            blocks = (2 * quarter, 2 * quarter + 1)
             if quarter == 2:
-                mx_sum(bank(4, [P, H]), [(words[:, 0, :P].bitcast(FP8X4), scales[:, 0, :P])] * KEEP, w4_ops[:1] * KEEP)
+                held = buffer8(7, [P, 2, SLOTS, P], "d")
+            for n, b in enumerate(blocks):
+                cols = slice(n * P, (n + 1) * P)
+                acc = bank(4 * (quarter == 1) + n, [P, H])
+                mx_sum(acc, [(words[:, a, cols].bitcast(FP8X4), scales[:, a, cols]) for a in range(PASSES)], w4_ops)
+                d[b] = held[:, n] if quarter == 2 else reuse.tile([P, SLOTS, P], F32, name="d", tag=f"f3_{b}")[:]
+                nc.scalar.copy(d[b], by_slot(acc))
             half, lo = quarter // 2, quarter % 2 * QUARTER
             if lo == 0:
                 h[half] = buffer8(half, [P, SLOTS, HALF], f"h{half}")
-            d_blocks.extend(d)
-            for u in range(2 if half == 0 else 1):
-                acc = bank(first_bank + 2 + u, [P, 2, 2, P])
-                terms = [triple[2 * quarter + n] for n in range(2)] + d
+            for u in range(2 - half):
+                acc = bank(4 * (quarter % 2) + 2 + u, [P, 2, 2, P])
+                terms = [triple[b] for b in blocks] + [d[b] for b in blocks]
                 for k, term in enumerate(terms):
                     for m in range(2):
                         nc.tensor.matmul(acc[:, m, k % 2, :], term[:, 2 * u + m, :], ident[:],
                                          start=(k + m == 0), stop=(k + m == 4), is_transpose=True)
-                nc.scalar.copy(h[half][:, 2 * u : 2 * u + 2, lo : lo + QUARTER], acc[:].rearrange("p m n j -> p m (n j)"))
+                rows = h[half][:, 2 * u : 2 * u + 2, lo : lo + QUARTER]
+                nc.scalar.copy(rows, acc[:].rearrange("p m n j -> p m (n j)"))
 
         def late_slot(i):
-            acc = bank(4 * i - 5, [P, HALF_BLOCKS, P])
-            terms = [triple[HALF_BLOCKS + n] for n in range(HALF_BLOCKS)] + d_blocks[HALF_BLOCKS:]
+            acc = bank(4 * (i - 2) + 3, [P, HALF_BLOCKS, P])
+            blocks = range(HALF_BLOCKS, BLOCKS)
+            terms = [triple[b] for b in blocks] + [d[b] for b in blocks]
             for k, term in enumerate(terms):
                 nc.tensor.matmul(acc[:, k % HALF_BLOCKS, :], term[:, i, :], ident[:],
                                  start=(k == 0), stop=(k == len(terms) - 1), is_transpose=True)
@@ -350,31 +347,27 @@ def tile_list_translator_brief_scores_kernel(
             times_f2(b)
         w4_ops = [quantize_weight(w4_raw[a], f"w4_{a}", interleave_on_scalar) for a in range(PASSES)]
         shape = [P, PASSES, QUARTER, SLOTS]
-        quantize_briefs(0, reuse.tile(shape, BF16, name="staged", tag="late", align_bytes=64),
-                        (interleave_on_vector, interleave_on_scalar))
+        first_staged = reuse.tile(shape, BF16, name="staged", tag="late", align_bytes=64)
+        quantize_briefs(0, first_staged, (interleave_on_vector, interleave_on_scalar))
         late = reuse.tile([P, HALF_BLOCKS, SLOTS, P], F32, name="late", tag="late", align_bytes=64)
         for b in range(2):
-            times_f1(b, product[0][:, b], 4 + b)
-        features(0, (nc.scalar.copy, nc.scalar.copy))
-        for b in range(2, 2 + HALF_BLOCKS):
-            times_f1(b, late[:, b - 2], 4 + b % HALF_BLOCKS)
-        staged = reuse.tile(shape, BF16, name="staged", tag="staged", bufs=3, align_bytes=64)
-        quantize_briefs(1, staged, (interleave_on_scalar, interleave_on_scalar))
-        for b in range(2 + HALF_BLOCKS, BLOCKS):
-            times_f1(b, product[b // 2][:, b % 2], b)
-        features(1, (nc.scalar.copy, nc.scalar.copy))
+            times_f1(b, product[0][:, b])
+        features(0)
+        quantize_briefs(1, staging(shape), (interleave_on_scalar, interleave_on_both))
+        for b in range(2, BLOCKS):
+            times_f1(b, late[:, b - 2] if b < 2 + HALF_BLOCKS else product[b // 2][:, b % 2])
+        features(1)
         for quarter in range(2):
             for i in range(2):
                 amend(i, quarter * QUARTER, (quarter + 1) * QUARTER)
         amend(2, 0, HALF)
         for quarter in range(2, 4):
-            staged = reuse.tile(shape, BF16, name="staged", tag="staged", bufs=3, align_bytes=64)
-            quantize_briefs(quarter, staged, (interleave_on_scalar, interleave_on_scalar))
-        for quarter in range(2, 4):
-            features(quarter, (nc.scalar.copy, nc.scalar.copy))
-            if quarter == 2:
-                amend(3, 0, HALF)
-            amend(0, quarter * QUARTER, (quarter + 1) * QUARTER)
+            quantize_briefs(quarter, staging(shape), (interleave_on_scalar, interleave_on_scalar))
+        features(2)
+        amend(3, 0, HALF)
+        amend(0, HALF, HALF + QUARTER)
+        features(3)
+        amend(0, HALF + QUARTER, S)
         for i in range(2, SLOTS):
             late_slot(i)
         for i in range(1, SLOTS):
@@ -389,9 +382,6 @@ def tile_list_translator_brief_scores_kernel(
             for c in range(CHUNKS):
                 nc.scalar.copy(pairs[c // 2][:, c % 2, i // 2, :, i % 2], page[i][:, c * BANK : (c + 1) * BANK])
         nc.vector.tensor_copy(v2_words[:], tab2[:].indirect(idx2[:]))
-
-        warm = bank(CHUNKS - 1, [P, BANK])
-        mx_sum(warm, [(v2_words[:, :P].bitcast(FP8X4), v2_scales[:, :P])] * WARM_UPS, w4_ops[:1] * WARM_UPS)
 
         page_staged, page_ops = [], []
         for step in range(CHUNKS + 1):
@@ -453,7 +443,7 @@ def tile_list_translator_brief_scores_kernel(
             else:
                 nc.scalar.activation(part, part, ACT.Square, scale=root[:, g : g + 1])
             engine.tensor_tensor(piece, piece, part, MULT)
-            if g >= 2:
+            if g >= GROUPS // 2:
                 nc.sync.dma_start(out[rows, lo:hi], piece)
             elif hi == S:
                 nc.sync.dma_start(out[rows, :], x[g])

@@ -32,6 +32,7 @@ HALF_BLOCKS = HALF // P
 CHUNKS = T2 // BANK
 GROUPS = S2 // P
 HALVES_IN_TURN = (0, 2, 1, 3)
+WARM_UPS = 3
 LINE = 4
 PIECES = [(g, lo, lo + HALF) for g in range(GROUPS) for lo in (0, HALF)][:-1] + [
     (GROUPS - 1, lo, lo + QUARTER) for lo in (HALF, HALF + QUARTER)
@@ -113,10 +114,10 @@ def tile_list_translator_brief_scores_kernel(
             )
 
         def mx_sum(acc, lhs, rhs):
-            for a in range(PASSES):
+            for a in range(len(rhs)):
                 nc.tensor.matmul_mx(
                     out=acc[:], lhsT=lhs[a][0], lhsT_scale=lhs[a][1], rhs=rhs[a][0], rhs_scale=rhs[a][1],
-                    start=(a == 0), stop=(a == PASSES - 1),
+                    start=(a == 0), stop=(a == len(rhs) - 1),
                 )
 
         def by_slot(acc):
@@ -382,6 +383,9 @@ def tile_list_translator_brief_scores_kernel(
             for c in range(CHUNKS):
                 nc.scalar.copy(pairs[c // 2][:, c % 2, i // 2, :, i % 2], page[i][:, c * BANK : (c + 1) * BANK])
         nc.vector.tensor_copy(v2_words[:], tab2[:].indirect(idx2[:]))
+
+        warm = bank(CHUNKS - 1, [P, BANK])
+        mx_sum(warm, [(v2_words[:, :P].bitcast(FP8X4), v2_scales[:, :P])] * WARM_UPS, w4_ops[:1] * WARM_UPS)
 
         page_staged, page_ops = [], []
         for step in range(CHUNKS + 1):

@@ -301,14 +301,14 @@ def tile_list_translator_brief_scores_kernel(
         d = {}
         h = {}
 
-        def features(quarter):
+        waiting = []
+
+        def features(quarter, held=None):
             words, scales = briefs_ops[quarter]
             blocks = (2 * quarter, 2 * quarter + 1)
-            if quarter == 2:
-                held = buffer8(7, [P, 2, SLOTS, P], "d")
             for n, b in enumerate(blocks):
                 cols = slice(n * P, (n + 1) * P)
-                acc = bank(4 * (quarter == 1) + n, [P, H])
+                acc = bank(4 * (quarter % 2) + n, [P, H])
                 mx_sum(acc, [(words[:, a, cols].bitcast(FP8X4), scales[:, a, cols]) for a in range(PASSES)], w4_ops)
                 d[b] = held[:, n] if quarter == 2 else reuse.tile([P, SLOTS, P], F32, name="d", tag=f"f3_{b}")[:]
                 nc.scalar.copy(d[b], by_slot(acc))
@@ -323,7 +323,12 @@ def tile_list_translator_brief_scores_kernel(
                         nc.tensor.matmul(acc[:, m, k % 2, :], term[:, 2 * u + m, :], ident[:],
                                          start=(k + m == 0), stop=(k + m == 4), is_transpose=True)
                 rows = h[half][:, 2 * u : 2 * u + 2, lo : lo + QUARTER]
-                nc.scalar.copy(rows, acc[:].rearrange("p m n j -> p m (n j)"))
+                turned = acc[:].rearrange("p m n j -> p m (n j)")
+                if (quarter, u) == (1, 1):
+                    nc.scalar.copy(rows[:, 1], turned[:, 1])
+                    waiting.append(turned[:, 0])
+                else:
+                    nc.scalar.copy(rows, turned)
 
         def late_slot(i):
             acc = bank(4 * (i - 2) + 3, [P, HALF_BLOCKS, P])
@@ -348,9 +353,8 @@ def tile_list_translator_brief_scores_kernel(
             times_f2(b)
         w4_ops = [quantize_weight(w4_raw[a], f"w4_{a}", interleave_on_scalar) for a in range(PASSES)]
         shape = [P, PASSES, QUARTER, SLOTS]
-        first_staged = reuse.tile(shape, BF16, name="staged", tag="late", align_bytes=64)
-        quantize_briefs(0, first_staged, (interleave_on_vector, interleave_on_scalar))
-        late = reuse.tile([P, HALF_BLOCKS, SLOTS, P], F32, name="late", tag="late", align_bytes=64)
+        quantize_briefs(0, staging(shape), (interleave_on_vector, interleave_on_scalar))
+        late = buffer8(4, [P, HALF_BLOCKS, SLOTS, P], "late")
         for b in range(2):
             times_f1(b, product[0][:, b])
         features(0)
@@ -361,14 +365,18 @@ def tile_list_translator_brief_scores_kernel(
         for quarter in range(2):
             for i in range(2):
                 amend(i, quarter * QUARTER, (quarter + 1) * QUARTER)
-        amend(2, 0, HALF)
+        amend(2, 0, QUARTER)
         for quarter in range(2, 4):
             quantize_briefs(quarter, staging(shape), (interleave_on_scalar, interleave_on_scalar))
-        features(2)
+        held = buffer8(7, [P, 3, SLOTS, P], "held")
+        second = held[:, 2].rearrange("p i j -> p (i j)")[:, :QUARTER]
+        nc.scalar.copy(second, waiting[0])
+        window = page[2][:].indirect(entries(idx3, QUARTER, HALF))
+        nc.vector.tensor_tensor(window, second, weight[2, 0][:, QUARTER:], MULT)
+        features(2, held)
         amend(3, 0, HALF)
-        amend(0, HALF, HALF + QUARTER)
         features(3)
-        amend(0, HALF + QUARTER, S)
+        amend(0, HALF, S)
         for i in range(2, SLOTS):
             late_slot(i)
         for i in range(1, SLOTS):
@@ -379,9 +387,12 @@ def tile_list_translator_brief_scores_kernel(
             reuse.tile([P, 2, 2, BANK, 2], BF16, name=f"pairs{u}", tag=f"tab{u}", align_bytes=64)
             for u in range(CHUNKS // 2)
         ]
-        for i in range(SLOTS):
-            for c in range(CHUNKS):
-                nc.scalar.copy(pairs[c // 2][:, c % 2, i // 2, :, i % 2], page[i][:, c * BANK : (c + 1) * BANK])
+        for i in range(SLOTS - 1):
+            for u in range(CHUNKS // 2):
+                two = page[i][:, 2 * u * BANK : 2 * (u + 1) * BANK].rearrange("p (c n) -> p c n", c=2)
+                nc.scalar.copy(pairs[u][:, :, i // 2, :, i % 2], two)
+        for c in range(CHUNKS):
+            nc.scalar.copy(pairs[c // 2][:, c % 2, 1, :, 1], page[SLOTS - 1][:, c * BANK : (c + 1) * BANK])
         nc.vector.tensor_copy(v2_words[:], tab2[:].indirect(idx2[:]))
 
         warm = bank(CHUNKS - 1, [P, BANK])
@@ -456,9 +467,9 @@ def tile_list_translator_brief_scores_kernel(
             scores(g)
             pick(g)
         for step in range(len(PIECES) + 2):
-            if step < len(PIECES):
-                magnitude(*PIECES[step])
-            if 1 <= step <= len(PIECES):
-                inverse_root(*PIECES[step - 1])
             if step >= 2:
                 finish(*PIECES[step - 2])
+            if 1 <= step <= len(PIECES):
+                inverse_root(*PIECES[step - 1])
+            if step < len(PIECES):
+                magnitude(*PIECES[step])

from contextlib import ExitStack

import concourse.mybir as mybir
from concourse.masks import make_identity

K, H, T, S, T2, T3, S2 = 1024, 512, 2048, 1024, 2048, 2048, 512
FLOPS = 4 * 2 * K * H * S + 2 * H * S2 * T2

F32 = mybir.dt.float32
BF16 = mybir.dt.bfloat16
I32 = mybir.dt.int32
U32 = mybir.dt.uint32
U16 = mybir.dt.uint16
U8 = mybir.dt.uint8
FP8X4 = mybir.dt.float8_e4m3fn_x4
FP4X4 = mybir.dt.float4_e2m1fn_x4
MULT = mybir.AluOpType.mult
ACT = mybir.ActivationFunctionType

P = 128
SLOTS = 4
K_PASS = P * SLOTS
PASSES = K // K_PASS
QUADRANTS = 4
SCALE_ROWS = 4
BANK = 512
PER_COLUMN = 16
HALF = S // 2
QUARTER = S // 4
BLOCKS = S // P
HALF_BLOCKS = HALF // P
CHUNKS = T2 // BANK
GROUPS = S2 // P
HALVES_IN_TURN = (0, 2, 1, 3)
WARM_UPS = 3
LINE = 4
PIECES = [(g, lo, lo + HALF) for g in range(GROUPS) for lo in (0, HALF)][:-1] + [
    (GROUPS - 1, lo, lo + QUARTER) for lo in (HALF, HALF + QUARTER)
]
VECTOR_LAST_BANKS = 3
GPSIMD_TWICE = PIECES[:1]
GPSIMD_ONCE = PIECES[1:3]
VECTOR_TWICE = PIECES[5:6]


def tile_list_translator_brief_scores_kernel(
    tc, tab_words, tab_scales, tab2_words, tab2_scales, w1, w2_words, w2_scales, w3_words, w3_scales,
    w4, briefs, page0, wgs, room, offs, offs2, offs3, offs4, out,
):
    nc = tc.nc
    with ExitStack() as ctx:
        keep = ctx.enter_context(tc.tile_pool(name="keep", bufs=1))
        reuse = ctx.enter_context(tc.tile_pool(name="reuse", bufs=1))
        psum = ctx.enter_context(tc.psum_pool(name="psum", bufs=1))

        def buffer8(number, shape, name):
            return reuse.tile(shape, F32, name=name, tag=f"buffer8_{number}", align_bytes=64)

        def bank(number, shape):
            return psum.tile(shape, F32, name=f"bank{number}", tag=f"bank{number}")

        def staging(shape=(P, BANK, SLOTS)):
            return reuse.tile(list(shape), BF16, name="staged", tag="staged", bufs=3, align_bytes=64)

        def moving_operand(name):
            words = reuse.tile([P, BANK], U32, name=name + "_words", tag="moving_words", bufs=4, align_bytes=64)
            scales = reuse.tile([P, BANK], U8, name=name + "_scales", tag="moving_scales", bufs=4, align_bytes=64)
            return words, scales

        def zeroed_scales(shape, name):
            scales = keep.tile(shape, U8, name=name, align_bytes=64)
            nc.vector.memset(scales[:].bitcast(I32), 0)
            return scales

        def load_list(src, name):
            lst = keep.tile(list(src.shape), U16, name=name)
            nc.sync.dma_start(lst[:], src)
            return lst

        def entries(lst, lo, hi):
            return lst[:, lo // PER_COLUMN : hi // PER_COLUMN]

        def load_words(words, src):
            nc.sync.dma_start(words.bitcast(I32), src.rearrange("p t i -> p (t i)").bitcast(I32))

        def load_scale_rows(queue, scales, src):
            for q in range(QUADRANTS):
                queue.dma_start(
                    scales[32 * q : 32 * q + SCALE_ROWS].bitcast(I32),
                    src[:, SCALE_ROWS * q : SCALE_ROWS * (q + 1), :].rearrange("a r c -> r a c").bitcast(I32),
                )

        def load_pass(number, src, name):
            raw = buffer8(number, [P, SLOTS, BANK], name)
            nc.sync.dma_start(raw[:], src.rearrange("(p i) c -> p i c", i=SLOTS))
            return raw

        def interleave_on_scalar(raw, staged):
            nc.scalar.copy(
                staged.rearrange("p (c n) i -> p c i n", n=LINE),
                raw.rearrange("p i (c n) -> p c i n", n=LINE),
            )

        def interleave_on_vector(raw, staged):
            nc.vector.tensor_copy(staged, raw.rearrange("p i c -> p c i"))

        def interleave_on_both(raw, staged):
            interleave_on_scalar(raw[:, :, :P], staged[:, :P, :])
            interleave_on_vector(raw[:, :, P:], staged[:, P:, :])

        def quantize(staged, words, scales):
            nc.vector.quantize_mx(
                out=words[:].bitcast(FP8X4), scales=scales[:], in_=staged.rearrange("p c i -> p (c i)")
            )

        def mx_sum(acc, lhs, rhs):
            for a in range(len(rhs)):
                nc.tensor.matmul_mx(
                    out=acc[:], lhsT=lhs[a][0], lhsT_scale=lhs[a][1], rhs=rhs[a][0], rhs_scale=rhs[a][1],
                    start=(a == 0), stop=(a == len(rhs) - 1),
                )

        def by_slot(acc):
            return acc[:].rearrange("j (p i) -> j i p", i=SLOTS)

        room_rows = keep.tile([P, P], F32, name="room_rows")
        nc.vector.memset(room_rows[:], 0.0)
        tab_scale_rows = zeroed_scales([P, T], "tab_scale_rows")
        w3_scale_rows = zeroed_scales([P, PASSES, H], "w3_scale_rows")
        w2_scale_rows = zeroed_scales([P, PASSES, H], "w2_scale_rows")
        tab2_scale_rows = zeroed_scales([P, T3], "tab2_scale_rows")
        v2_scales = zeroed_scales([P, S2], "v2_scales")
        v_scales_raised = zeroed_scales([P, S], "v_scales_raised")

        ident = keep.tile([P, P], F32, name="ident")
        make_identity(nc, ident[:])
        nc.sync.dma_start(room_rows[:GROUPS], room.rearrange("(g p) -> g p", p=P))
        room_turned = bank(0, [P, P])
        nc.tensor.matmul(room_turned[:], room_rows[:], ident[:], start=True, stop=True, is_transpose=True)
        room_col = keep.tile([P, GROUPS], F32, name="room_col")
        load_scale_rows(nc.gpsimd, w2_scale_rows, w2_scales)

        root = keep.tile([P, GROUPS], F32, name="root")
        unit = keep.tile([P, GROUPS], F32, name="unit")
        unit_room = keep.tile([P, GROUPS], F32, name="unit_room")
        nc.scalar.activation(root[:], room_turned[:, :GROUPS], ACT.Abs_reciprocal_sqrt)
        nc.scalar.copy(room_col[:], room_turned[:, :GROUPS])
        nc.gpsimd.tensor_tensor(unit[:], root[:], root[:], MULT)
        nc.gpsimd.tensor_tensor(unit_room[:], unit[:], room_col[:], MULT)

        wgs_rows = keep.tile([P, HALF], F32, name="wgs_rows0")
        nc.sync.dma_start(wgs_rows[:], wgs[:, :HALF])
        for q in HALVES_IN_TURN:
            nc.sync.dma_start(
                tab_scale_rows[32 * q : 32 * q + PASSES * SCALE_ROWS].bitcast(I32),
                tab_scales[:, SCALE_ROWS * q : SCALE_ROWS * (q + 1), :].bitcast(I32),
            )
        idx = load_list(offs, "idx")
        tab = [reuse.tile([P, T], U32, name=f"tab{a}", tag=f"tab{a}", align_bytes=64) for a in range(PASSES)]
        load_words(tab[0][:], tab_words[0])
        idx2 = load_list(offs2, "idx2")
        nc.sync.dma_start(tab2_scale_rows[0:P:8].bitcast(I32), tab2_scales[0].bitcast(I32))
        w3_codes = keep.tile([P, PASSES, H], U32, name="w3_codes", align_bytes=64)
        nc.sync.dma_start(w3_codes[:].bitcast(I32), w3_words.rearrange("a p c i -> p a (c i)").bitcast(I32))
        load_words(tab[1][:], tab_words[1])
        load_scale_rows(nc.sync, w3_scale_rows, w3_scales)
        w1_raw = [load_pass(a, w1[a * K_PASS : (a + 1) * K_PASS, :], f"w1_raw{a}") for a in range(PASSES)]

        v_words = [keep.tile([P, S], U32, name=f"v_words{a}", align_bytes=64) for a in range(PASSES)]
        v_scales = keep.tile([P, S], U8, name="v_scales", align_bytes=64)
        nc.vector.tensor_copy(v_scales[:], tab_scale_rows[:].indirect(idx[:]))
        nc.vector.tensor_copy(v_words[0][:], tab[0][:].indirect(idx[:]))
        picked2_scales = keep.tile([P, S2], U8, name="picked2_scales", align_bytes=64)
        nc.vector.tensor_copy(picked2_scales[:], tab2_scale_rows[:].indirect(idx2[:]))
        for lo in (0, HALF):
            nc.vector.tensor_copy(v_words[1][:, lo : lo + HALF], tab[1][:].indirect(entries(idx, lo, lo + HALF)))

        for q in range(QUADRANTS):
            nc.sync.dma_start(
                v_scales_raised[32 * q : 32 * q + SCALE_ROWS].bitcast(I32),
                v_scales[32 * q + SCALE_ROWS : 32 * q + 2 * SCALE_ROWS].bitcast(I32),
            )
        w2_codes = keep.tile([P, PASSES, 2 * H], U8, name="w2_codes", align_bytes=64)
        nc.sync.dma_start(w2_codes[:].bitcast(I32), w2_words.rearrange("a p c -> p a c").bitcast(I32))

        w4_raw = [load_pass(2 + a, w4[a * K_PASS : (a + 1) * K_PASS, :], f"w4_raw{a}") for a in range(PASSES)]
        briefs_raw, weight, page = {}, {}, {}

        def load_briefs(quarter):
            raw = buffer8(4 + quarter, [P, PASSES, SLOTS, QUARTER], f"briefs_raw{quarter}")
            for a in range(PASSES):
                src = briefs[a * K_PASS : (a + 1) * K_PASS, quarter * QUARTER : (quarter + 1) * QUARTER]
                nc.sync.dma_start(raw[:, a], src.rearrange("(p i) c -> p i c", i=SLOTS))
            briefs_raw[quarter] = raw

        def load_weight(slots):
            rows = keep.tile([P, len(slots), HALF], F32, name=f"weight1_{slots[0]}")
            src = wgs.rearrange("(p i) j -> p i j", i=SLOTS)[:, slots[0] : slots[-1] + 1, HALF:]
            for q in HALVES_IN_TURN:
                nc.sync.dma_start(rows[32 * q : 32 * (q + 1)], src)
            for n, i in enumerate(slots):
                weight[i, 1] = rows[:, n, :]

        def spread_weight():
            turned = bank(7, [P, HALF_BLOCKS, P])
            for n in range(HALF_BLOCKS):
                nc.tensor.matmul(turned[:, n, :], wgs_rows[:, n * P : (n + 1) * P], ident[:],
                                 start=(n == 0), stop=(n == HALF_BLOCKS - 1), is_transpose=True)
            repeated = buffer8(7, [P, SLOTS, HALF_BLOCKS, QUADRANTS, 32], "repeated")
            rows = keep.tile([P, SLOTS, HALF], F32, name="weight0")
            for i in range(SLOTS):
                src = turned[:].rearrange("j n (p i) -> j i n p", i=SLOTS)[:, i]
                nc.scalar.copy(repeated[:, i], src.unsqueeze(2).to_broadcast([P, HALF_BLOCKS, QUADRANTS, 32]))
            for i in range(SLOTS):
                back = bank(3 + i, [P, HALF_BLOCKS, P])
                for n in range(HALF_BLOCKS):
                    nc.tensor.matmul(back[:, n, :], repeated[:, i, n].rearrange("j q p -> j (q p)"), ident[:],
                                     start=(n == 0), stop=(n == HALF_BLOCKS - 1), is_transpose=True)
                nc.scalar.copy(rows[:, i, :], back[:].rearrange("p n j -> p (n j)"))
                weight[i, 0] = rows[:, i, :]

        def load_page(i):
            page[i] = keep.tile([P, T2], F32, name=f"page{i}")
            nc.sync.dma_start(page[i][:], page0.rearrange("(p i) t -> p i t", i=SLOTS)[:, i, :])

        spread_weight()
        load_briefs(0)
        load_briefs(1)
        idx3 = load_list(offs3, "idx3")
        load_page(0)
        load_page(1)
        load_briefs(2)
        load_page(2)
        load_briefs(3)
        load_page(3)
        for slots in (range(0, 1), range(1, 2), range(2, SLOTS)):
            load_weight(slots)
        tab2 = keep.tile([P, T3], U32, name="tab2", align_bytes=64)
        load_words(tab2[:], tab2_words[0])
        idx4 = load_list(offs4, "idx4")
        for q in range(QUADRANTS):
            nc.sync.dma_start(
                v2_scales[32 * q : 32 * q + SCALE_ROWS].bitcast(I32),
                picked2_scales[32 * q : 32 * (q + 1) : 8].bitcast(I32),
            )

        w2_ops = [(w2_codes[:, a, :].bitcast(FP4X4), w2_scale_rows[:, a, :]) for a in range(PASSES)]
        w3_ops = [(w3_codes[:, a, :].bitcast(FP8X4), w3_scale_rows[:, a, :]) for a in range(PASSES)]
        product = {}
        triple = {}

        def table_sum(b, w_ops, second_scales, bank_number):
            cols = slice(b * P, (b + 1) * P)
            scales = (v_scales[:, cols], second_scales[:, cols])
            v_ops = [(v_words[a][:, cols].bitcast(FP8X4), scales[a]) for a in range(PASSES)]
            acc = bank(bank_number, [P, H])
            mx_sum(acc, v_ops, w_ops)
            return by_slot(acc)

        f3 = {}

        def fetch_f3(b):
            f3[b] = reuse.tile([P, SLOTS, P], F32, name="f3", tag=f"f3_{b}")
            nc.scalar.copy(f3[b][:], table_sum(b, w3_ops, v_scales[SCALE_ROWS:P], b))

        def times_f2(b):
            if b % 2 == 0:
                product[b // 2] = reuse.tile([P, 2, SLOTS, P], F32, name="product", tag="product", bufs=BLOCKS // 2)
            f2 = table_sum(b, w2_ops, v_scales_raised, b)
            nc.vector.tensor_tensor(product[b // 2][:, b % 2], f2, f3[b][:], MULT)

        def quantize_weight(raw, name, interleave, parts=1):
            words, scales = moving_operand(name)
            staged = staging()
            pieces = [slice(lo, lo + BANK // parts) for lo in range(0, BANK, BANK // parts)]
            for cols in pieces:
                interleave(raw[:, :, cols], staged[:, cols, :])
            for cols in pieces:
                quantize(staged[:, cols, :], words[:, cols], scales[:, cols])
            return words[:].bitcast(FP8X4), scales[:]

        def times_f1(b, out_tile):
            f1 = table_sum(b, w1_ops, v_scales[SCALE_ROWS:P], 4 + b % HALF_BLOCKS)
            nc.vector.tensor_tensor(out_tile, f1, product[b // 2][:, b % 2], MULT)
            triple[b] = out_tile

        briefs_ops = {}

        def quantize_briefs(quarter, staged, interleave):
            words = keep.tile([P, PASSES, QUARTER], U32, name=f"briefs_words{quarter}", align_bytes=64)
            scales = keep.tile([P, PASSES, QUARTER], U8, name=f"briefs_scales{quarter}", align_bytes=64)
            for a in range(PASSES):
                interleave[a](briefs_raw[quarter][:, a], staged[:, a])
            quantize(
                staged[:].rearrange("p a c i -> p (a c) i"),
                words[:].rearrange("p a c -> p (a c)"),
                scales[:].rearrange("p a c -> p (a c)"),
            )
            briefs_ops[quarter] = words, scales

        d = {}
        h = {}

        waiting = []

        def features(quarter, held=None):
            words, scales = briefs_ops[quarter]
            blocks = (2 * quarter, 2 * quarter + 1)
            for n, b in enumerate(blocks):
                cols = slice(n * P, (n + 1) * P)
                acc = bank(4 * (quarter % 2) + n, [P, H])
                mx_sum(acc, [(words[:, a, cols].bitcast(FP8X4), scales[:, a, cols]) for a in range(PASSES)], w4_ops)
                d[b] = held[:, n] if quarter == 2 else reuse.tile([P, SLOTS, P], F32, name="d", tag=f"f3_{b}")[:]
                nc.scalar.copy(d[b], by_slot(acc))
            half, lo = quarter // 2, quarter % 2 * QUARTER
            if lo == 0:
                h[half] = buffer8(half, [P, SLOTS, HALF], f"h{half}")
            for u in range(2 - half):
                acc = bank(4 * (quarter % 2) + 2 + u, [P, 2, 2, P])
                terms = [triple[b] for b in blocks] + [d[b] for b in blocks]
                for k, term in enumerate(terms):
                    for m in range(2):
                        nc.tensor.matmul(acc[:, m, k % 2, :], term[:, 2 * u + m, :], ident[:],
                                         start=(k + m == 0), stop=(k + m == 4), is_transpose=True)
                rows = h[half][:, 2 * u : 2 * u + 2, lo : lo + QUARTER]
                turned = acc[:].rearrange("p m n j -> p m (n j)")
                if (quarter, u) == (1, 1):
                    nc.scalar.copy(rows[:, 1], turned[:, 1])
                    waiting.append(turned[:, 0])
                else:
                    nc.scalar.copy(rows, turned)

        def late_slot(i):
            acc = bank(4 * (i - 2) + 3, [P, HALF_BLOCKS, P])
            blocks = range(HALF_BLOCKS, BLOCKS)
            terms = [triple[b] for b in blocks] + [d[b] for b in blocks]
            for k, term in enumerate(terms):
                nc.tensor.matmul(acc[:, k % HALF_BLOCKS, :], term[:, i, :], ident[:],
                                 start=(k == 0), stop=(k == len(terms) - 1), is_transpose=True)
            nc.scalar.copy(h[1][:, i, :], acc[:].rearrange("p n j -> p (n j)"))

        def amend(i, lo, hi):
            half, first = lo // HALF, lo % HALF
            cols = slice(first, first + hi - lo)
            window = page[i][:].indirect(entries(idx3, lo, hi))
            nc.vector.tensor_tensor(window, h[half][:, i, cols], weight[i, half][:, cols], MULT)

        w1_ops = [quantize_weight(w1_raw[0], "w1_0", interleave_on_vector, 2)]
        for b in range(BLOCKS):
            fetch_f3(b)
        w1_ops.append(quantize_weight(w1_raw[1], "w1_1", interleave_on_vector, 2))
        for b in range(BLOCKS):
            times_f2(b)
        w4_ops = [quantize_weight(w4_raw[a], f"w4_{a}", interleave_on_scalar) for a in range(PASSES)]
        shape = [P, PASSES, QUARTER, SLOTS]
        quantize_briefs(0, staging(shape), (interleave_on_vector, interleave_on_scalar))
        late = buffer8(4, [P, HALF_BLOCKS, SLOTS, P], "late")
        for b in range(2):
            times_f1(b, product[0][:, b])
        features(0)
        quantize_briefs(1, staging(shape), (interleave_on_scalar, interleave_on_both))
        for b in range(2, BLOCKS):
            times_f1(b, late[:, b - 2] if b < 2 + HALF_BLOCKS else product[b // 2][:, b % 2])
        features(1)
        for quarter in range(2):
            for i in range(2):
                amend(i, quarter * QUARTER, (quarter + 1) * QUARTER)
        amend(2, 0, QUARTER)
        for quarter in range(2, 4):
            quantize_briefs(quarter, staging(shape), (interleave_on_scalar, interleave_on_scalar))
        held = buffer8(7, [P, 3, SLOTS, P], "held")
        second = held[:, 2].rearrange("p i j -> p (i j)")[:, :QUARTER]
        nc.scalar.copy(second, waiting[0])
        window = page[2][:].indirect(entries(idx3, QUARTER, HALF))
        nc.vector.tensor_tensor(window, second, weight[2, 0][:, QUARTER:], MULT)
        features(2, held)
        amend(3, 0, HALF)
        features(3)
        amend(0, HALF, S)
        for i in range(2, SLOTS):
            late_slot(i)
        for i in range(1, SLOTS):
            amend(i, HALF, S)

        v2_words = keep.tile([P, S2], U32, name="v2_words", align_bytes=64)
        pairs = [
            reuse.tile([P, 2, 2, BANK, 2], BF16, name=f"pairs{u}", tag=f"tab{u}", align_bytes=64)
            for u in range(CHUNKS // 2)
        ]
        for i in range(SLOTS - 1):
            for u in range(CHUNKS // 2):
                two = page[i][:, 2 * u * BANK : 2 * (u + 1) * BANK].rearrange("p (c n) -> p c n", c=2)
                nc.scalar.copy(pairs[u][:, :, i // 2, :, i % 2], two)
        for c in range(CHUNKS):
            nc.scalar.copy(pairs[c // 2][:, c % 2, 1, :, 1], page[SLOTS - 1][:, c * BANK : (c + 1) * BANK])
        nc.vector.tensor_copy(v2_words[:], tab2[:].indirect(idx2[:]))

        warm = bank(CHUNKS - 1, [P, BANK])
        mx_sum(warm, [(v2_words[:, :P].bitcast(FP8X4), v2_scales[:, :P])] * WARM_UPS, w4_ops[:1] * WARM_UPS)

        page_staged, page_ops = [], []
        for step in range(CHUNKS + 1):
            if step < CHUNKS:
                page_staged.append(staging())
                copy = nc.scalar.copy if step == CHUNKS - 1 else nc.vector.tensor_copy
                words = pairs[step // 2][:, step % 2].rearrange("p u c n -> p u (c n)").bitcast(F32)
                copy(
                    page_staged[step][:].rearrange("p c i -> p (c i)").bitcast(F32).rearrange("p (c u) -> p c u", u=2),
                    words.rearrange("p u c -> p c u"),
                )
            if step > 0:
                page_ops.append(moving_operand(f"page_{step - 1}"))
                quantize(page_staged[step - 1][:], *page_ops[step - 1])

        e, x, inverse = {}, {}, {}

        def vector_empties(g, c):
            return g == 1 or g * CHUNKS + c >= GROUPS * CHUNKS - VECTOR_LAST_BANKS

        def scores(g):
            rows = slice(g * P, (g + 1) * P)
            e[g] = buffer8(2 + g, [P, T2], f"e{g}")
            for c in range(CHUNKS):
                acc = bank(CHUNKS * (g % 2) + (c + 2 * (g // 2)) % CHUNKS, [P, BANK])
                nc.tensor.matmul_mx(
                    out=acc[:], lhsT=v2_words[:, rows].bitcast(FP8X4), lhsT_scale=v2_scales[:, rows],
                    rhs=page_ops[c][0][:].bitcast(FP8X4), rhs_scale=page_ops[c][1][:], start=True, stop=True,
                )
                copy = nc.vector.tensor_copy if vector_empties(g, c) else nc.scalar.copy
                copy(e[g][:, c * BANK : (c + 1) * BANK], acc[:])

        def pick(g):
            if g % 2 == 0:
                both = buffer8(6 + g // 2, [P, 2, S], "x")
                x[g], x[g + 1] = both[:, 0, :], both[:, 1, :]
            for lo in (0, HALF):
                nc.vector.tensor_copy(x[g][:, lo : lo + HALF], e[g][:].indirect(entries(idx4, lo, lo + HALF)))

        def magnitude(g, lo, hi):
            if lo == 0:
                inverse[g] = reuse.tile([P, S], F32, name="inverse", tag="product", bufs=BLOCKS // 2)
            nc.scalar.activation(inverse[g][:, lo:hi], x[g][:, lo:hi], ACT.Abs)

        def inverse_root(g, lo, hi):
            part = inverse[g][:, lo:hi]
            if (g, lo, hi) in GPSIMD_TWICE + VECTOR_TWICE:
                nc.scalar.activation(part, part, ACT.Abs_reciprocal_sqrt, bias=room_col[:, g : g + 1])
            else:
                nc.scalar.activation(
                    part, part, ACT.Abs_reciprocal_sqrt, bias=unit_room[:, g : g + 1], scale=unit[:, g : g + 1]
                )

        def finish(g, lo, hi):
            rows, part, piece = slice(g * P, (g + 1) * P), inverse[g][:, lo:hi], x[g][:, lo:hi]
            engine = nc.gpsimd if (g, lo, hi) in GPSIMD_TWICE + GPSIMD_ONCE else nc.vector
            if (g, lo, hi) in GPSIMD_TWICE + VECTOR_TWICE:
                engine.tensor_tensor(piece, piece, part, MULT)
            else:
                nc.scalar.activation(part, part, ACT.Square, scale=root[:, g : g + 1])
            engine.tensor_tensor(piece, piece, part, MULT)
            if g >= GROUPS // 2:
                nc.sync.dma_start(out[rows, lo:hi], piece)
            elif hi == S:
                nc.sync.dma_start(out[rows, :], x[g])

        for g in range(GROUPS):
            scores(g)
            pick(g)
        for step in range(len(PIECES) + 2):
            if step >= 2:
                finish(*PIECES[step - 2])
            if 1 <= step <= len(PIECES):
                inverse_root(*PIECES[step - 1])
            if step < len(PIECES):
                magnitude(*PIECES[step])
